import numpy as np, ml_dtypes
CORES = [48,51,52,55]
N = 4
import mx_ref
BF = ml_dtypes.bfloat16
def gcols(t, e):
    v = np.concatenate([t.reshape(8, 16, -1, 4), np.zeros((8, 16, 1, 4), BF)], axis=2)
    return np.ascontiguousarray(np.stack([v[g][:, e[g]] for g in range(8)])).reshape(128, -1)
def tile(rs):
    return np.stack(rs, axis=2).reshape(128, -1).astype(BF)
def pick(q, e):
    c = np.concatenate([q[0].reshape(128, -1, 4), np.zeros((128, 1, 4), np.uint8)], axis=1); s = np.concatenate([q[1], np.ones((16, 1), np.uint8)], axis=1)
    return (np.ascontiguousarray(c[:, e].reshape(128, -1)), np.ascontiguousarray(s[:, e]))
def join(*qs):
    return (np.concatenate([q[0] for q in qs], axis=1), np.concatenate([q[1] for q in qs], axis=1))
def put(q, e, v):
    c, s = q[0].reshape(128, -1, 4).copy(), q[1].copy(); c[:, e] = v[0].reshape(128, -1, 4); s[:, e] = v[1]
    return (c.reshape(128, -1), s)
def pk(c, s):
    return (np.ascontiguousarray(c), mx_ref.live(s))
def emit(q):
    return q[0], q[1]
def packed(v, rng):
    q = [mx_ref.quantize(np.ascontiguousarray(v[r])) for r in range(N)]
    return np.stack([a for a, b in q]), np.stack([mx_ref.plane(b, rng) for a, b in q])
def values_of_codes():
    e, c = np.zeros((128, 128, 4), np.float32), np.zeros((128, 2, 4), np.uint8)
    e[np.arange(128), np.arange(128), 0] = 1
    c[:127, :, 0] = np.arange(256).reshape(2, 128).T[:127]
    return mx_ref.matmul(mx_ref.quantize(e.reshape(128, 512).astype(BF)), (c.reshape(128, 8), np.full((16, 2), 127, np.uint8))).T.reshape(-1).astype(np.float64)
CODE_VALUE, SCALE_VALUE = values_of_codes(), 2.0 ** (np.arange(256) - 127.0)
def decode(q):
    return (CODE_VALUE[q[0]].reshape(16, 8, -1, 4) * SCALE_VALUE[q[1]][:, None, :, None] + 0.0).reshape(128, -1).astype(np.float32)
def f(rng, *shape):
    return mx_ref.flush((rng.standard_normal(shape, dtype=np.float32) * np.exp2(rng.integers(-2, 3, shape[:-1] + (1,)))).astype(BF))
def wide(rng, *shape, cols=0):
    v = rng.standard_normal(shape, dtype=np.float32) * np.exp2(rng.integers(-12, 13, shape)).astype(np.float32)
    if cols: v *= np.repeat(np.exp2(rng.integers(-cols, cols + 1, shape[:-2] + (1, shape[-1] // 4))) * (rng.random(shape[:-2] + (1, shape[-1] // 4)) > 0.0625), 4, axis=-1).astype(np.float32)
    return mx_ref.flush(v.astype(BF))
C, A, B, S = 384, 192, 96, 24
def top(s, k):
    return np.sort(np.argsort(-s, axis=-1, kind="stable")[..., :k], axis=-1)
def layer(w, q):
    return tile([np.maximum(mx_ref.matmul(pick(w, np.arange(128 * b, 128 * b + 128)), q), np.float32(0.0)) * np.float32(0.03125) for b in range(4)])
def gadd(t, e, v):
    a, c = t.astype(np.float32).reshape(8, 16, -1, 4), v.astype(np.float32).reshape(8, 16, -1, 4)
    for g in range(8): a[g][:, e[g]] = a[g][:, e[g]] + c[g]
    return a.reshape(128, -1).astype(BF)
def big(v, k):
    v = v.astype(np.float32) * np.float32(k)
    v[np.abs(v) < np.float32(2.0 ** -16)] = 0
    return v.astype(BF)
def numbers_of(rng):
    return {"x": big(f(rng, N, 128, 4 * C), 1), "u1": np.array(f(rng, N, 128, 512)), "u2": np.array(f(rng, N, 128, 512)), "v": np.array(f(rng, N, 128, 512))}
def weights(rng, w, z):
    a, b = packed(w, rng)
    c, e = packed(z, rng)
    return {"wc": a, "ws": b, "zc": c, "zs": e}
def unit(k):
    w = np.zeros((N, 128, 4, 128, 4), np.float32)
    i = np.arange(128)
    for b in range(4): w[:, i, b, i, b] = k
    return w.reshape(N, 128, 2048).astype(BF)
def signs(rng):
    return np.stack([rng.permutation(8) % 2 * 2.0 - 1.0 for r in range(N)])
def steps(n):
    return np.minimum((np.arange(n) + 1) // 2, n // 2 - 1)
def planted(rng, p1, p2, k):
    d = numbers_of(rng)
    s1, t, s2 = np.zeros((N, 8, C), int), np.zeros((N, 8, A), int), np.zeros((N, 8, C), int)
    np.put_along_axis(s1, p1, np.broadcast_to(steps(C), p1.shape), axis=2)
    np.put_along_axis(t, p2, np.broadcast_to(steps(A), p2.shape), axis=2)
    first = top(s1, A)
    np.put_along_axis(s2, first, t, axis=2)
    x = d["x"].astype(np.float32).reshape(N, 8, 16, C, 4)
    x[:, :, 0] = 0
    x[:, :, 0, :, 0] = 1
    np.put_along_axis(x[:, :, 0, :, 1], p1[..., -1:], np.float32(2.0 ** 13), axis=2)
    np.put_along_axis(x[:, :, 0, :, 1], p1[..., :1], np.float32(-2.0 ** 30), axis=2)
    np.put_along_axis(x[:, :, 0, :, 2], np.take_along_axis(first, p2[..., -1:], axis=2), np.float32(2.0 ** 13), axis=2)
    for s, at in ((s1, 8), (s2, 10)):
        g = ((s[..., None] >> np.arange(8)) & 1) * np.exp2(np.arange(8) - 23.0)
        x[:, :, at] = g[..., :4]
        x[:, :, at + 1] = g[..., 4:]
    x[:, :, 12] = 0
    x[:, :, 12, :, 0] = 2.0 ** -10
    x[:, :, 13:] = rng.integers(4, 8, (N, 8, 3, C, 4)) * rng.choice([-1.0, 1.0], (N, 8, 3, C, 4)) * 2.0 ** -20
    d["x"] = x.reshape(N, 128, 4 * C).astype(BF)
    for n, at, far in (("u1", 8, 1), ("u2", 10, 2)):
        u = d[n].reshape(N, 128, 128, 4)
        u[:, :, ::16] = 0
        g = (signs(rng) * k).astype(BF)
        for i in range(8):
            u[:, 16 * i, 16 * i, 0] = g[:, i]
            u[:, 16 * i, 16 * i, far] = 2.0 ** 13 * k
            u[:, 16 * i + at:16 * i + at + 2, 16 * i] = k
            u[:, 16 * i + 12, 16 * i, 0] = g[:, i]
        d[n] = u.reshape(N, 128, 512)
    return {**d, **weights(rng, unit(32), f(rng, N, 128, 2048))}
def setup_inputs(rng):
    return {**numbers_of(rng), **weights(rng, f(rng, N, 128, 2048), f(rng, N, 128, 2048))}
def setup_inputs_ties(rng):
    d = numbers_of(rng)
    e = rng.permutation(N)
    x = d["x"].reshape(N, 8, 16, C, 4)
    for r in range(N):
        k = np.zeros(C, int) if r == e[0] else rng.permutation(C) % 3
        a = x[r][:, :8, :3].copy()
        a[:, :, 2] = 0
        x[r][:, :8] = a[:, :, k]
    d["x"] = x.reshape(N, 128, 4 * C)
    w = np.array(f(rng, N, 128, 2048)).reshape(N, 8, 16, 4, 8, 16, 4)
    w[:, :, 8:, :, :, :8] = 0
    for g in range(8): w[:, np.arange(8) != g, :, :, g, :8] = 0
    for n in ("u1", "u2"):
        u = d[n].reshape(N, 8, 16, 128, 4)
        u[:, :, 8:, ::16] = 0
        for g in range(8): u[:, np.arange(8) != g, :, 16 * g] = 0
        d[n] = u.reshape(N, 128, 512)
    return {**d, **weights(rng, w.reshape(N, 128, 2048), f(rng, N, 128, 2048))}
def setup_inputs_near(rng):
    p = []
    for n, k in ((C, A), (A, B)):
        a = rng.permuted(np.tile(np.arange(n), (N, 8, 1)), axis=2)
        a[:, :, n - k - 3:n - k + 1] = np.sort(a[:, :, n - k - 3:n - k + 1], axis=2)
        p.append(a)
    return planted(rng, p[0], p[1], 1.0)
def setup_inputs_runs(rng):
    a, b = signs(rng)[:, :, None] > 0, signs(rng)[:, :, None] > 0
    return planted(rng, np.where(a, np.arange(C), np.arange(C)[::-1]), np.where(b, np.arange(A), np.arange(A)[::-1]), 2.0 ** -30)
def setup_inputs_huge(rng):
    d = numbers_of(rng)
    c = np.stack([rng.permutation(C) % 2 * 2.0 - 1.0 for r in range(N)])
    c[rng.permutation(N) < N // 2] = -1
    x = 2.0 ** 30 * (0.6 + 0.3 * rng.random((N, 128, C, 4))) * c[:, None, :, None]
    d["x"] = x.astype(np.float32).reshape(N, 128, 4 * C).astype(BF)
    for n in ("u1", "u2"):
        u = d[n].reshape(N, 128, 128, 4)
        a = 2.0 ** 30 * (1 - 0.25 * rng.random((N, 128, 8, 4))) * signs(rng)[:, None, :, None]
        u[:, :, ::16] = a.astype(np.float32).astype(BF)
        d[n] = u.reshape(N, 128, 512)
    return {**d, **weights(rng, unit(-32), big(f(rng, N, 128, 2048), 2.0 ** -6))}
def setup_inputs_spread(rng):
    d = setup_inputs(rng)
    d["x"] = big(wide(rng, N, 128, 4 * C, cols=6), 1)
    return d
def check_inputs(d):
    b = []
    for k in ("x", "u1", "u2", "v"):
        a = np.abs(d[k].astype(np.float32))
        if not (np.isfinite(a).all() and ((a == 0) | (a >= 2.0 ** -30) & (a <= 2.0 ** 30)).all()): b.append("a value of " + k)
    return b
def reference(x, u1, u2, v, wc, ws, zc, zs):
    one, two, h, down = [], [], [], []
    for r in range(N):
        p = mx_ref.matmul(mx_ref.quantize(u1[r]), mx_ref.quantize(x[r]))
        one.append(top(p[::16] + np.float32(0.0), A))
        h.append(layer(pk(wc[r], ws[r]), mx_ref.quantize(gcols(x[r], one[r]))))
        p = mx_ref.matmul(mx_ref.quantize(u2[r]), mx_ref.quantize(h[r]))
        two.append(top(p[::16] + np.float32(0.0), B))
        down.append(mx_ref.quantize(gcols(h[r], two[r])))
    done = []
    for d in range(N):
        q = join(*[pick(down[r], S * d + np.arange(S)) for r in range(N)])
        done.append(mx_ref.quantize(layer(pk(zc[d], zs[d]), q)))
    y, ol = np.zeros((N, 128, C), np.float32), np.zeros((N, 8, B), np.float32)
    oc, osc = np.zeros((N, 128, 4 * C), np.uint8), np.zeros((N, 16, C), np.uint8)
    for r in range(N):
        came = decode(join(*[pick(done[d], S * r + np.arange(S)) for d in range(N)]))
        q = mx_ref.quantize(gadd(x[r], one[r], gadd(h[r], two[r], came)))
        y[r] = mx_ref.matmul(mx_ref.quantize(v[r]), q)
        ol[r] = np.take_along_axis(one[r], two[r], axis=1)
        oc[r], osc[r] = emit(q)
    return {"y": y, "ol": ol, "oc": oc, "osc": osc}

@@ -1,0 +1,554 @@
+from concourse.bass import DstId, RemoteDMATransfer
+from concourse.mybir import dt, AluOpType as A, AxisListType, ActivationFunctionType as F
+
+C, KA, KB, PC = 384, 192, 96, 24
+BIG = 2.0 ** 90
+XO = 4 * (KB + KA)
+PITCH = C - KA + 16
+X4, U8, BF, F32, I32, U16 = "float8_e4m3fn_x4", "uint8", "bfloat16", "float32", "int32", "uint16"
+
+SCRATCH = {}
+for _n, _w in (("x", C + 3 * PC), ("h", KA + 3 * PC), ("f", KA), ("g", 128), ("t", 128), ("o", 128), ("u1", 128),
+               ("u2", 128), ("p1", 384), ("p2", 384), ("v", 128), ("e", 512), ("w", 512), ("z", 512), ("y", C)):
+    SCRATCH["q" + _n] = ("sbuf", [128, _w], X4)
+    SCRATCH["s" + _n] = ("sbuf", [128, _w], U8)
+for _n, _w, _d in (
+        ("win", XO + 4 * C, BF), ("xp", 4 * C, BF), ("hp", 4 * KA, BF), ("tu1", 512, BF), ("tu2", 512, BF),
+        ("tv", 512, BF), ("tf", 4 * KA, BF), ("th", 4 * KA, BF), ("tg", 512, BF), ("tt", 512, BF), ("to", 512, BF),
+        ("te", 2048, BF), ("one", 512, BF), ("zero", C, BF), ("fg", 4 * KB, BF), ("hs", 4 * KB, BF),
+        ("tx", 4 * C, BF), ("yb", C, F32),
+        ("oi", 36, I32), ("offc", 36, U16), ("pi", 4, I32), ("pf", 4, F32), ("m16", 12, F32), ("thr", 12, F32),
+        ("cs", 12, F32), ("ramp", C, F32), ("idx", C, F32), ("jm", KB, F32), ("gate", KB, F32), ("oh", 4, F32),
+        ("l1", KA, F32), ("olr", KB, F32), ("old", KB, F32), ("offo", 6, U16), ("pick", C, F32), ("sum2", KA, F32),
+        ("sum1", KB, F32), ("gate2", KB, F32), ("olm", KB, F32), ("thr2", 18, F32), ("offx", KB, U16),
+        ("srt", 40, F32)):
+    SCRATCH[_n] = ("sbuf", [128, _w], _d)
+for _i, _c, _k, _m in ((1, C, KA, 16), (2, KA, KB, 12)):
+    for _n, _w, _d in (("tr", _c, F32), ("ks", 16, F32), ("junk", 12 * _c, BF), ("cmp", 6 * _c, BF),
+                       ("so", 6 * _c, BF), ("d0", 4 * _m, F32), ("d1", 3 * _m, F32), ("both", 2 * _m, F32),
+                       ("sc", 3 * _m, F32), ("ex", 96, F32), ("tex", 96, F32), ("red", 4, F32), ("gt", _c, BF),
+                       ("ge", _c, BF), ("sg", _c, BF), ("cap", _c, BF), ("pos", _c, BF), ("cj", 6 * PITCH, BF),
+                       ("cc", 6 * PITCH, BF), ("co", 12 * PITCH, BF), ("ck", 6, F32), ("off", 12, U16)):
+        SCRATCH["%s%d" % (_n, _i)] = ("sbuf", [128, _w], _d)
+for _i in range(8):
+    SCRATCH["b%d" % _i] = ("psum", [128, 512], F32)
+
+SEMAPHORES = ["cV", "cS", "cP", "cG", "arr1", "arr2", "left1", "left2"] + ["d%02d" % _i for _i in range(40)]
+
+
+def rank_program(g, core, T, topo):
+    rank = T.rank_of(core)
+    if rank is None:
+        return
+    N = len(T.cores)
+    Q = {"V": g.vector, "S": g.scalar, "P": g.tensor, "G": g, "Y": g.sync}
+    clock = {e: {} for e in Q}
+    count = {}
+    seen = {}
+    log = {}
+    ndma = [0]
+
+    def ap(w):
+        n, a, b, s = w
+        return T[n][:, a:b] if s == 1 else T[n][:, a:b:s]
+
+    def v(n, a=0, b=None, s=1):
+        return (n, a, SCRATCH[n][1][1] if b is None and s > 0 else b, s)
+
+    def cols(w):
+        n, a, b, s = w
+        return set(range(a, -1 if b is None else b, s))
+
+    def wait(e, sem, c, ck):
+        if clock[e].get(sem, 0) < c:
+            Q[e].wait_ge(T.sem[sem], c)
+            clock[e][sem] = c
+            seen[sem] = max(seen.get(sem, 0), c)
+            for k, x in ck.items():
+                if clock[e].get(k, 0) < x:
+                    clock[e][k] = x
+
+    def order(e, reads, writes):
+        need = {}
+        for w, wr in [(w, False) for w in reads] + [(w, True) for w in writes]:
+            cs, bank = cols(w), SCRATCH[w[0]][0] == "psum"
+            for (e2, sem, c, ck, cs2, wr2) in log.get(w[0], []):
+                if (bank and e2 != e) or ((wr or wr2) and cs & cs2):
+                    if need.get(sem, (0, None))[0] < c:
+                        need[sem] = (c, ck)
+        for sem, (c, ck) in sorted(need.items(), key=lambda kv: -len(kv[1][1])):
+            wait(e, sem, c, ck)
+
+    def note(e, sem, c, reads, writes):
+        ck = dict(clock[e]) if e in clock else {}
+        for w, wr in [(w, False) for w in reads] + [(w, True) for w in writes]:
+            log.setdefault(w[0], []).append((e, sem, c, ck, cols(w), wr))
+
+    def op(e, call, reads, writes):
+        order(e, reads, writes)
+        sem = "c" + e
+        count[sem] = count.get(sem, 0) + 1
+        call().then_inc(T.sem[sem], 1)
+        note(e, sem, count[sem], reads, writes)
+
+    def dma(e, out, in_, reads, writes, **how):
+        order(e, reads, writes)
+        sem = "d%02d" % ndma[0]
+        ndma[0] += 1
+        count[sem] = 16
+        Q[e].dma_start(out, in_, **how).then_inc(T.sem[sem], 16)
+        note(e, sem, 16, reads, writes)
+
+    def views(*xs):
+        return [x for x in xs if isinstance(x, tuple)]
+
+    def val(x):
+        return ap(x) if isinstance(x, tuple) else x
+
+    V, S = g.vector, g.scalar
+
+    def fill(w, c):
+        op("V", lambda: V.memset(ap(w), c), [], [w])
+
+    def copy(o, i, e="V"):
+        if e == "V":
+            op("V", lambda: V.tensor_copy(ap(o), ap(i)), [i], [o])
+        else:
+            op("S", lambda: S.activation(ap(o), ap(i), F.Copy), [i], [o])
+
+    def tt(o, a, b, alu):
+        op("V", lambda: V.tensor_tensor(ap(o), ap(a), ap(b), alu), [a, b], [o])
+
+    def ts(o, a, s1, o1, s2=None, o2=None):
+        if o2 is None:
+            op("V", lambda: V.tensor_scalar(ap(o), ap(a), val(s1), None, o1), views(a, s1), [o])
+        else:
+            op("V", lambda: V.tensor_scalar(ap(o), ap(a), val(s1), val(s2), o1, o2), views(a, s1, s2), [o])
+
+    def scan(o, d0, d1, init, o0, o1):
+        op("V", lambda: V.tensor_tensor_scan(ap(o), ap(d0), ap(d1), init, o0, o1), [d0, d1], [o])
+
+    def reduce(o, i, alu, neg):
+        op("V", lambda: V.tensor_reduce(ap(o), ap(i), AxisListType.X, alu, negate=neg), [i], [o])
+
+    def turn(o, i):
+        op("V", lambda: V.transpose(ap(o), ap(i)), [i], [o])
+
+    def gather(e, o, w, off):
+        if e == "V":
+            op("V", lambda: V.tensor_copy(ap(o), ap(w).indirect(ap(off))), [w, off], [o])
+        else:
+            op("S", lambda: S.activation(ap(o), ap(w).indirect(ap(off)), F.Copy), [w, off], [o])
+
+    def scatter(w, off, i):
+        op("V", lambda: V.tensor_copy(ap(w).indirect(ap(off)), ap(i)), [i, off], [w])
+
+    def sign(o, row, thr, acc=None):
+        op("S", lambda: S.activation(ap(o), ap(row), F.Sign, bias=ap(thr), scale=-1.0, accum_out=val(acc)),
+           [row, thr], views(o, acc))
+
+    def relu(e, o, i):
+        if e == "V":
+            ts(o, i, 0.0, A.max, 0.03125, A.mult)
+        else:
+            op("S", lambda: S.activation(ap(o), ap(i), F.Relu, scale=0.03125), [i], [o])
+
+    def quant(n, a, b, tile):
+        q, s = v("q" + n, a, b), v("s" + n, a, b)
+        op("V", lambda: V.quantize_mx(ap(q), ap(s), ap(tile)), [tile], [q, s])
+
+    def mm(bank, l, la, r, ra, n):
+        o, lq, ls = v("b%d" % bank, 0, n), v("q" + l, la, la + 128), v("s" + l, la, la + 128)
+        rq, rs = v("q" + r, ra, ra + n), v("s" + r, ra, ra + n)
+        op("P", lambda: g.tensor.matmul_mx(ap(o), ap(lq), ap(ls), ap(rq), ap(rs), True, True), [lq, ls, rq, rs], [o])
+
+    def iota(o, pattern, base, cm=0):
+        if SCRATCH[o[0]][2] == I32:
+            op("G", lambda: g.iota(ap(o), pattern, base, cm), [], [o])
+        else:
+            op("G", lambda: g.iota(ap(o), pattern, base, cm, allow_small_or_imprecise_dtypes=True), [], [o])
+
+    def level(o, c):
+        iota(o, [[0, len(cols(o))]], c)
+
+    def planes(dst, src, a, n):
+        for t in range(4):
+            o, i = v(dst, n * t, n * t + n), v(src, a + t, a + 4 * n, 4)
+            op("G", lambda: g.affine_select(ap(o), ap(i), [[0, n]], A.is_ge, 0.0, 0, 0), [i], [o])
+
+    def picks(e, n, a, b):
+        off = v("offc", a // 16, b // 16)
+        if e == "V":
+            o, i = v("qp" + n, a, b), v("qu" + n)
+            op("V", lambda: V.tensor_copy(ap(o).bitcast(dt.uint32), ap(i).bitcast(dt.uint32).indirect(ap(off))),
+               [i, off], [o])
+        else:
+            o, i = v("sp" + n, a, b), v("su" + n)
+            op("S", lambda: S.activation(ap(o), ap(i).indirect(ap(off)), F.Copy), [i, off], [o])
+
+    def codes(n, a, b):
+        return ap(v("q" + n, a, b)).bitcast(dt.uint8)
+
+    def exchange(src, src_at, dst, dst_at, sem, left):
+        for kind in ("q", "s"):
+            order("G", [v(kind + src)], [])
+            trs = []
+            for j in range(1, N):
+                d = (rank + j) % N
+                en = topo.engines(core, T.cores[d])
+                k = len(en) // 4
+                lo, hi = en[:2 * k], en[2 * k:]
+                if kind == "s":
+                    lo, hi = hi, lo
+                use = (lo[:k], lo[k:], hi)[j - 1]
+                rid, pid = topo.addr(T.cores[d])[:2]
+                a, b = src_at(d), dst_at(d)
+                if kind == "q":
+                    i, o = codes(src, a, a + PC), codes(dst, b, b + PC)
+                else:
+                    i, o = ap(v("s" + src, a, a + PC)), ap(v("s" + dst, b, b + PC))
+                trs.append(RemoteDMATransfer(dst_ids=[DstId(rid=rid, pnc=pid)], dma_engine_mask=sum(1 << x for x in use),
+                                             remote_sem=T.sem[sem], src=i, dst=o))
+                count[left] = count.get(left, 0) + len(use)
+                count[sem] = count.get(sem, 0) + len(use)
+            g.remote_dma_fused(trs, local_sem=T.sem[left])
+
+    def landed(sem, n, a, b):
+        note("remote", sem, count[sem], [], [v("q" + n, a, b), v("s" + n, a, b)])
+
+    def consts(i, m):
+        fill(v("d0%d" % i, 2 * m, 2 * m + 2), -128 * BIG)
+        fill(v("d0%d" % i, 3 * m, 3 * m + 2), -128 * BIG)
+        fill(v("d1%d" % i, 0, m), -64 * BIG)
+
+    def zeros(i, m):
+        level(v("d0%d" % i, 2 * m + 2, 3 * m), 0)
+        level(v("d0%d" % i, 3 * m + 2, 4 * m), 0)
+
+    def vcmp(i, n, slot, bank, thr):
+        ts(v("cmp%d" % i, n * slot, n * slot + n), v("b%d" % bank, 0, n), thr, A.is_gt)
+
+    def vsum(i, n, k, slot):
+        scan(v("so%d" % i, n * slot, n * slot + n), v("zero", 0, n), v("cmp%d" % i, n * slot, n * slot + n),
+             float(k), A.add, A.subtract)
+
+    def threshold(i, n, m, k, eoff):
+        s = str(i)
+        tt(v("d1" + s, m, 3 * m), v("d0" + s, 0, 2 * m), v("both" + s), A.add)
+        for h in range(2):
+            scan(v("sc" + s, h * 3 * m // 2, (h + 1) * 3 * m // 2), v("d0" + s, m + h, 4 * m, 2),
+                 v("d1" + s, h, 3 * m, 2), (k - 0.5) / 32 * BIG, A.add, A.max)
+        gather("V", v("ex" + s), v("sc" + s), v("offc", eoff, eoff + 6))
+        turn(v("tex" + s), v("ex" + s))
+        o, i_, acc = v("junk" + s, 11 * n, 11 * n + 32), v("tex" + s, 0, 32), v("red" + s, 0, 1)
+        op("S", lambda: S.activation(ap(o), ap(i_), F.Identity, scale=-1.0, accum_out=ap(acc)), [i_], [o, acc])
+        reduce(v("red" + s, 1, 2), v("tex" + s, 32, 64), A.max, True)
+        reduce(v("red" + s, 2, 3), v("tex" + s, 64, 96), A.max, False)
+        ts(v("red" + s, 3, 4), v("red" + s, 0, 1), v("red" + s, 1, 2), A.min, v("red" + s, 2, 3), A.max)
+
+    def spans(n, k, turn_by):
+        w, half = n - k + 16, k // 32
+        first = [(16 * m + turn_by) % k for m in range(2 * half)]
+        span = [(a, a + w) if a + 16 <= k else (0, n) for a in first]
+        low = all(b - a == w for a, b in span[:half])
+        return span, list(range(half)) if low else list(range(half, 2 * half))
+
+    def make_list(i, n, k, bank, bank2, co, thr, turn_by):
+        s = str(i)
+        row, t = v("b%d" % bank, 0, n), v("red" + s, 3, 4)
+        ts(v("gt" + s), row, t, A.is_gt)
+        if bank2 is None:
+            ts(v("ge" + s), row, t, A.is_ge)
+        else:
+            sign(v("sg" + s), v("b%d" % bank2, 0, n), t)
+        scan(v("cap" + s, n - 2, None, -1), v("zero", 0, n - 1), v("gt" + s, n - 1, 0, -1), float(k), A.add, A.subtract)
+        if bank2 is not None:
+            ts(v("ge" + s), v("sg" + s), 0.0, A.is_le)
+        scan(v("pos" + s), v("ge" + s), v("cap" + s), 0.0, A.add, A.min)
+        w, half = n - k + 16, k // 32
+        span, on_s = spans(n, k, turn_by)
+        on_v = [m for m in range(2 * half) if m not in on_s]
+        for j, m in enumerate(on_s):
+            sign(v("cj" + s, w * j, w * j + w), v("pos" + s, *span[m]), v(thr, m, m + 1), v("ck" + s, j, j + 1))
+
+        def cmp(j):
+            a, b = span[on_v[j]]
+            ts(v("cc" + s, PITCH * j, PITCH * j + b - a), v("pos" + s, a, b), v(thr, on_v[j], on_v[j] + 1), A.is_le,
+               2.0, A.mult)
+
+        def tot(j):
+            a, b = span[on_v[j]]
+            end = PITCH * on_v[j] + PITCH
+            scan(v("co" + s, end - b + a, end), v("zero", 0, b - a), v("cc" + s, PITCH * j, PITCH * j + b - a),
+                 float(2 * a - 256), A.add, A.add)
+
+        cmp(0)
+        for j in range(1, half):
+            cmp(j)
+            tot(j - 1)
+        tot(half - 1)
+        tt(v("co" + s, PITCH * on_s[0] + PITCH - 1, PITCH * on_s[-1] + PITCH, PITCH), v("ck" + s, 0, half),
+           v("cs", co, co + half), A.add)
+        ts(v("off" + s, 0, 2 * half), v("co" + s, PITCH - 1, 2 * PITCH * half, PITCH), 0.5, A.mult, 128.0, A.add)
+
+    def xs(j):
+        return v("win", XO + 512 * j, XO + 512 * j + 512)
+
+    dma("Y", ap(v("tu1")), T.u1[:], [], [v("tu1")])
+    dma("S", ap(xs(0)), T.x[:, 0:512], [], [xs(0)])
+    dma("Y", ap(xs(1)), T.x[:, 512:1024], [], [xs(1)])
+    dma("S", ap(xs(2)), T.x[:, 1024:1536], [], [xs(2)])
+    dma("Y", ap(v("tu2")), T.u2[:], [], [v("tu2")])
+    dma("Y", codes("w", 0, 512), T.wc[:], [], [v("qw")])
+    dma("Y", ap(v("sw")), T.ws[:], [], [v("sw")])
+    dma("Y", codes("z", 0, 512), T.zc[:], [], [v("qz")])
+    dma("Y", ap(v("sz")), T.zs[:], [], [v("sz")])
+    dma("Y", ap(v("tv")), T.v[:], [], [v("tv")])
+
+    iota(v("oi", 0, 16), [[16, 2], [32, 4], [0, 2]], 0)
+    iota(v("oi", 16, 24), [[16, 8]], 0)
+    iota(v("oi", 24, 30), [[8, 3], [24, 2]], 7)
+    iota(v("oi", 30, 36), [[6, 3], [18, 2]], 5)
+    iota(v("pi", 0, 1), [[0, 1]], 0, 1)
+    iota(v("m16"), [[16, 12]], 0)
+    iota(v("jm"), [[0, 6], [1, 16]], 0)
+    fill(v("zero"), 0.0)
+    consts(1, 16)
+    consts(2, 12)
+    copy(v("offc"), v("oi"))
+    ts(v("pi", 1, 2), v("pi", 0, 1), 15, A.bitwise_and)
+    ts(v("pi", 3, 4), v("pi", 0, 1), 3, A.bitwise_and)
+    ts(v("pi", 2, 3), v("pi", 1, 2), 2, A.logical_shift_right)
+    copy(v("pf"), v("pi"))
+    ts(v("thr"), v("m16"), v("pf", 1, 2), A.add, 0.5, A.add)
+    ts(v("gate"), v("jm"), v("pf", 1, 2), A.is_le, BIG, A.mult)
+    ts(v("thr2", 6, 12), v("thr", 0, 6), float(PC * rank), A.add)
+    ts(v("thr2", 12, 18), v("thr", 0, 6), float(KB - PC * rank), A.is_ge, -float(KB), A.mult)
+    ts(v("gate2"), v("jm"), v("pf", 1, 2), A.is_gt, 1024.0, A.mult)
+    tt(v("thr2", 0, 6), v("thr2", 6, 12), v("thr2", 12, 18), A.add)
+    ts(v("oh"), v("jm", 0, 4), v("pf", 2, 3), A.is_equal, 4.0, A.mult)
+    zeros(1, 16)
+    zeros(2, 12)
+    for at, n, k, by in ((0, C, KA, 0), (6, KA, KB, PC * rank)):
+        span, on_s = spans(n, k, by)
+        iota(v("cs", at, at + 6), [[32, 6]], sum(span[on_s[0]]) - 256)
+    level(v("cap1", C - 1), KA)
+    level(v("cap2", KA - 1), KB)
+
+    ca, cb, cc = v("tr1", 0, 128, 16), v("tr1", 128, 256, 16), v("tr1", 256, 384, 16)
+    mn, mx, z, lo, hi = (v("srt", 8 * j, 8 * j + 8) for j in range(5))
+    quant("u1", 0, 128, v("tu1"))
+    picks("V", "1", 0, 256)
+    picks("S", "1", 0, 256)
+    picks("S", "1", 256, 384)
+    quant("x", 0, 128, xs(0))
+    mm(0, "u1", 0, "x", 0, 128)
+    quant("x", 128, 256, xs(1))
+    mm(1, "u1", 0, "x", 128, 128)
+    turn(v("tr1", 0, 128), v("b0", 0, 128))
+    quant("x", 256, 384, xs(2))
+    mm(2, "u1", 0, "x", 256, 128)
+    mm(3, "p1", 0, "x", 0, C)
+    mm(4, "p1", 128, "x", 0, C)
+    mm(5, "p1", 128, "x", 0, C)
+    turn(v("tr1", 128, 256), v("b1", 0, 128))
+    tt(mx, ca, cb, A.max)
+    tt(mn, ca, cb, A.min)
+    planes("xp", "win", XO, C)
+    level(v("one"), 1)
+    for b in range(4):
+        op("G", lambda: g.affine_select(ap(v("te", 512 * b, 512 * b + 512)), ap(v("one")), [[8, 128], [1, 4]],
+                                        A.is_equal, 0.0, -b, -8), [v("one")], [v("te", 512 * b, 512 * b + 512)])
+    level(v("tg", 4 * KB), 0)
+    iota(v("ramp"), [[1, C]], 0)
+    iota(v("idx"), [[1, C]], KB + KA)
+
+    turn(v("tr1", 256, 384), v("b2", 0, 128))
+    tt(z, mx, cc, A.min)
+    tt(lo, mn, cc, A.min)
+    tt(v("both1", 16, 24), mn, z, A.max)
+    tt(hi, mx, cc, A.max)
+
+    def cand(c):
+        return v("both1", 16 + c, 17 + c)
+
+    def scount(j, c):
+        sign(v("junk1", C * j, C * j + C), v("b%d" % (5 if c % 2 else 3), 0, C), cand(c), v("ks1", c, c + 1))
+
+    def gate1(o, i):
+        ts(o, i, 0.0, A.is_gt, -2 * BIG, A.mult)
+
+    def choose(a, b, step):
+        if step == 0:
+            tt(v("srt", a, b), v("srt", 32 + a, 32 + b), v("d01", 16 + a, 16 + b), A.add)
+        else:
+            tt(v("both1", 24 + a, 24 + b), v("srt", a, b), v("srt", 24 + a, 24 + b), A.max)
+
+    for j, c in enumerate((0, 2, 4, 6, 5, 7)):
+        scount(j, c)
+    picks("V", "1", 256, 384)
+    mm(6, "p1", 256, "x", 0, C)
+    mm(7, "p1", 256, "x", 0, C)
+    vcmp(1, C, 0, 4, cand(1))
+    vcmp(1, C, 1, 4, cand(3))
+    vsum(1, C, KA, 0)
+    vsum(1, C, KA, 1)
+    gate1(v("d01", 16, 21, 2), v("ks1", 0, 5, 2))
+    gate1(v("d01", 17, 20, 2), v("so1", C - 1, 2 * C, C))
+    choose(0, 5, 0)
+    choose(0, 5, 1)
+    for j, c in enumerate((8, 10, 12)):
+        scount(6 + j, c)
+    vcmp(1, C, 2, 4, cand(9))
+    gate1(v("d01", 21, 24), v("ks1", 5, 8))
+    vcmp(1, C, 3, 4, cand(11))
+    choose(5, 8, 0)
+    vsum(1, C, KA, 2)
+    choose(5, 8, 1)
+    scount(9, 14)
+    scount(10, 15)
+    vsum(1, C, KA, 3)
+    vcmp(1, C, 4, 4, cand(13))
+    ts(v("d01", 0, 8), v("d01", 16, 24), 0.0, A.is_equal, -BIG, A.mult)
+    vsum(1, C, KA, 4)
+    ts(v("both1", 0, 16), v("both1", 16, 32), -1.0, A.mult)
+    copy(v("ks1", 9, 14, 2), v("so1", 3 * C - 1, 5 * C, C))
+    quant("u2", 0, 128, v("tu2"))
+    picks("S", "2", 0, 384)
+    ts(v("d01", 24, 32), v("ks1", 8, 16), 0.0, A.is_gt, -BIG, A.mult)
+    ts(v("d01", 8, 16), v("ks1", 8, 16), 0.0, A.is_le, -BIG, A.mult)
+    threshold(1, C, 16, KA, 24)
+    make_list(1, C, KA, 6, 7, 0, "thr", 0)
+
+    for t, e in enumerate("SVSV"):
+        gather(e, v("tf", t, 4 * KA, 4), v("xp", C * t, C * t + C), v("off1"))
+    quant("f", 0, KA, v("tf"))
+    for b in range(4):
+        mm(b, "w", 128 * b, "f", 0, KA)
+    fh = v("win", 4 * KB, XO)
+    dma("Y", ap(fh), ap(v("tf")), [v("tf")], [fh])
+    picks("V", "2", 0, 384)
+    quant("e", 0, 256, v("te", 0, 1024))
+    for b, e in enumerate("SSSV"):
+        relu(e, v("th", b, 4 * KA, 4), v("b%d" % b, 0, KA))
+    quant("h", 0, KA, v("th"))
+    planes("hp", "th", 0, KA)
+    dma("G", ap(fh), ap(v("th")), [v("th"), fh], [fh], accum_op=A.add)
+    level(v("to", 4 * PC), 0)
+    level(v("tt", 12 * PC), 0)
+    mm(4, "u2", 0, "h", 0, KA)
+    mm(5, "p2", 0, "h", 0, KA)
+    mm(6, "p2", 128, "h", 0, KA)
+    mm(7, "p2", 128, "h", 0, KA)
+    mm(0, "p2", 256, "h", 0, KA)
+    quant("e", 256, 512, v("te", 1024))
+
+    turn(v("tr2"), v("b4", 0, KA))
+    for j, c in enumerate((0, 2, 4, 6, 8, 10, 9, 11)):
+        sign(v("junk2", KA * j, KA * j + KA), v("b%d" % (7 if c % 2 else 5), 0, KA), v("tr2", 16 * c, 16 * c + 1),
+             v("ks2", c, c + 1))
+    vcmp(2, KA, 0, 6, v("tr2", 16, 17))
+    for j in range(1, 4):
+        vcmp(2, KA, j, 6, v("tr2", 32 * j + 16, 32 * j + 17))
+        vsum(2, KA, KB, j - 1)
+    ts(v("both2", 0, 12), v("tr2", 0, KA, 16), -1.0, A.mult)
+    vsum(2, KA, KB, 3)
+    copy(v("both2", 12, 24), v("tr2", 0, KA, 16))
+    copy(v("ks2", 1, 8, 2), v("so2", KA - 1, 4 * KA, KA))
+    ts(v("d02", 12, 24), v("ks2", 0, 12), 0.0, A.is_gt, -BIG, A.mult)
+    ts(v("d02", 0, 12), v("ks2", 0, 12), 0.0, A.is_le, -BIG, A.mult)
+    gather("S", v("l1"), v("ramp"), v("off1"))
+    threshold(2, KA, 12, KB, 30)
+    make_list(2, KA, KB, 0, None, 6, "thr2", PC * rank)
+    off2 = v("off2", 0, 6)
+
+    for t, e in enumerate("SVSV"):
+        gather(e, v("tg", t, 4 * KB, 4), v("hp", KA * t, KA * t + KA), off2)
+    quant("g", 0, 128, v("tg"))
+    exchange("g", lambda d: PC * ((d - rank) % N), "x", lambda d: C + PC * ((rank - d) % N - 1), "arr1", "left1")
+    landed("arr1", "x", C, C + 3 * PC)
+
+    def up(b, at, a, e):
+        tt(v("hs", 4 * a + b, 4 * e, 4), v("b%d" % (1 + b), at, at + e - a), v("tg", 4 * a + b, 4 * e, 4), A.add)
+
+    def up2(b, a, e):
+        tt(v("win", 4 * a + b, 4 * e, 4), v("hs", 4 * a + b, 4 * e, 4), v("fg", 4 * a + b, 4 * e, 4), A.add)
+
+    for b in range(4):
+        mm(1 + b, "z", 128 * b, "g", 0, 128)
+    gather("S", v("olr"), v("l1"), off2)
+    for b in range(4):
+        relu("S", v("to", b, 4 * PC, 4), v("b%d" % (1 + b), 0, PC))
+    tt(v("olm"), v("olr"), v("gate2"), A.add)
+    scatter(v("idx"), v("off1"), v("ramp", KB, KB + KA))
+    scan(v("old"), v("gate"), v("olm"), 0.0, A.add, A.min)
+    quant("o", 0, 128, v("to"))
+    copy(v("offo"), v("old", 15, KB, 16))
+    for b in range(4):
+        mm(1 + b, "e", 128 * b, "o", 0, 128)
+    for t in range(4):
+        gather("S", v("fg", t, 4 * KB, 4), v("xp", C * t, C * t + C), v("offo"))
+    scatter(v("idx"), v("offo"), v("ramp", 0, KB))
+    for b in range(4):
+        up(b, 0, 0, PC)
+    for a in range(4):
+        o, i, sc = v("pick", KB * a, KB * a + KB), v("idx", a, C, 4), v("oh", a, a + 1)
+        op("S", lambda: S.activation(ap(o), ap(i), F.Copy, scale=ap(sc)), [i, sc], [o])
+    wait("Y", "left1", count["left1"], {})
+    dma("Y", T.ol[:, PC * rank:KB], T.olr[0:128:16, 0:KB - PC * rank], [v("olr")], [])
+    if rank:
+        dma("Y", T.ol[:, 0:PC * rank], T.olr[0:128:16, KB - PC * rank:KB], [v("olr")], [])
+
+    zb, at = (5, 6, 7, 0), 128 - 3 * PC
+    for b in range(4):
+        mm(zb[b], "z", 128 * b, "x", C - at, 128)
+    for b, e in enumerate("SVSV"):
+        relu(e, v("tt", b, 12 * PC, 4), v("b%d" % zb[b], at, 128))
+    quant("t", 0, 128, v("tt"))
+    exchange("t", lambda d: PC * ((d - rank) % N - 1), "h", lambda d: KA + PC * ((rank - d) % N - 1), "arr2", "left2")
+    landed("arr2", "h", KA, KA + 3 * PC)
+
+    tt(v("sum2"), v("pick", 0, KA), v("pick", KA, C), A.add)
+    quant("v", 0, 128, v("tv"))
+    tt(v("sum1"), v("sum2", 0, KB), v("sum2", KB, KA), A.add)
+    tt(v("win", 0, 4 * PC), v("hs", 0, 4 * PC), v("fg", 0, 4 * PC), A.add)
+    ts(v("offx"), v("sum1"), v("pf", 3, 4), A.add)
+
+    for b in range(4):
+        mm(1 + b, "e", 128 * b, "h", KA - at, 128)
+    up(0, at, PC, KB)
+    up(1, at, PC, KB)
+    up2(0, PC, KB)
+    up(2, at, PC, KB)
+    up2(1, PC, KB)
+    up(3, at, PC, KB)
+    up2(2, PC, KB)
+    up2(3, PC, KB)
+
+    def place(e, a, b):
+        gather(e, v("tx", 4 * a, 4 * b), v("win"), v("offx", a // 4, b // 4))
+
+    def yout(e, q, j):
+        w = v("yb", 128 * j, 128 * j + 128)
+        copy(w, v("b%d" % (5 + j), 0, 128), e)
+        dma(q, T.y[:, 128 * j:128 * j + 128], ap(w), [w], [])
+
+    cut = (64, 80, 80)
+    for j in range(3):
+        a = 128 * j
+        place("S", a, a + cut[j])
+        place("V", a + cut[j], a + 128)
+        if j == 1:
+            yout("V", "Y", 0)
+        quant("y", a, a + 128, v("tx", 4 * a, 4 * a + 512))
+        if j == 2:
+            yout("S", "S", 1)
+        mm(5 + j, "v", 0, "y", a, 128)
+        dma("Y", T.oc[:, 4 * a:4 * a + 512], codes("y", a, a + 128), [v("qy", a, a + 128)], [])
+    for k in range(4):
+        dma("YS"[k // 2], T.osc[4 * k:4 * k + 4, :], T.sy[32 * k:32 * k + 4, :], [v("sy")], [])
+    yout("V", "S", 2)
+
+    for sem in SEMAPHORES:
+        if seen.get(sem, 0) < count.get(sem, 0):
+            g.wait_ge(T.sem[sem], count[sem])

@@ -3,37 +3,39 @@ from concourse.mybir import dt, AluOpType as A, AxisListType, ActivationFunction
 
 C, KA, KB, PC = 384, 192, 96, 24
 BIG = 2.0 ** 90
-XO = 4 * (KB + KA)
-PITCH = C - KA + 16
+W1, W2 = C - KA + 16, KA - KB + 16
+FAR = 4096.0
 X4, U8, BF, F32, I32, U16 = "float8_e4m3fn_x4", "uint8", "bfloat16", "float32", "int32", "uint16"
 
 SCRATCH = {}
-for _n, _w in (("x", C + 3 * PC), ("h", KA + 3 * PC), ("f", KA), ("g", 128), ("t", 128), ("o", 128), ("u1", 128),
-               ("u2", 128), ("p1", 384), ("p2", 384), ("v", 128), ("e", 512), ("w", 512), ("z", 512), ("y", C)):
+for _n, _w in (("x", C + 4 * PC), ("h", KA + 4 * PC), ("f", KA + 5 * PC), ("a", 128 + 4 * PC), ("g", 128 + 4 * PC),
+               ("t1", 128), ("t2", 128), ("t3", 128), ("u1", 128), ("u2", 128), ("p1", 384), ("p2", 384), ("v", 128),
+               ("e", 512), ("w", 512), ("z", 512), ("y", C)):
     SCRATCH["q" + _n] = ("sbuf", [128, _w], X4)
     SCRATCH["s" + _n] = ("sbuf", [128, _w], U8)
 for _n, _w, _d in (
-        ("win", XO + 4 * C, BF), ("xp", 4 * C, BF), ("hp", 4 * KA, BF), ("tu1", 512, BF), ("tu2", 512, BF),
-        ("tv", 512, BF), ("tf", 4 * KA, BF), ("th", 4 * KA, BF), ("tg", 512, BF), ("tt", 512, BF), ("to", 512, BF),
-        ("te", 2048, BF), ("one", 512, BF), ("zero", C, BF), ("fg", 4 * KB, BF), ("hs", 4 * KB, BF),
-        ("tx", 4 * C, BF), ("yb", C, F32),
-        ("oi", 36, I32), ("offc", 36, U16), ("pi", 4, I32), ("pf", 4, F32), ("m16", 12, F32), ("thr", 12, F32),
-        ("cs", 12, F32), ("ramp", C, F32), ("idx", C, F32), ("jm", KB, F32), ("gate", KB, F32), ("oh", 4, F32),
-        ("l1", KA, F32), ("olr", KB, F32), ("old", KB, F32), ("offo", 6, U16), ("pick", C, F32), ("sum2", KA, F32),
-        ("sum1", KB, F32), ("gate2", KB, F32), ("olm", KB, F32), ("thr2", 18, F32), ("offx", KB, U16),
-        ("srt", 40, F32)):
+        ("win", 4 * (C + KA), BF), ("xp", 4 * C, BF), ("hp", 4 * KA, BF), ("tu1", 512, BF), ("tu2", 512, BF),
+        ("tv", 512, BF), ("tf", 4 * KA, BF), ("th", 4 * KA, BF), ("tg", 4 * 224, BF), ("tt", 4 * 176, BF),
+        ("dd", 256, BF), ("te", 516, BF), ("one", 516, BF), ("zero", C, BF), ("fg", 4 * KB, BF), ("hs", 4 * KB, BF),
+        ("nw", 4 * KB, BF), ("tx", 4 * C, BF), ("yb", C, F32),
+        ("oi", 24, I32), ("offc", 24, U16), ("pi", 4, I32), ("pf", 8, F32), ("m16", KB, F32), ("thr", 12, F32),
+        ("cs", 6, F32), ("ramp", C, F32), ("jm", C, BF), ("gate", C, BF), ("m2", 8, F32), ("thr2", 8, F32),
+        ("l1", KA, F32), ("olr", 128, F32), ("old", 128, F32), ("offs", 24, U16), ("pa", C, BF), ("pb", C, BF),
+        ("yy", 4 * KB, F32), ("offx", KB, U16), ("srt", 40, F32), ("cd", 16, F32),
+        ("cj1", 6 * W1, BF), ("cc1", 12 * W1, BF), ("co1", 6 * W1, BF), ("ck1", 6, F32), ("off1", 12, U16),
+        ("cc2", 8 * W2, BF), ("co2", 4 * W2, F32), ("ck2", 8, F32), ("off2", 8, U16)):
     SCRATCH[_n] = ("sbuf", [128, _w], _d)
 for _i, _c, _k, _m in ((1, C, KA, 16), (2, KA, KB, 12)):
-    for _n, _w, _d in (("tr", _c, F32), ("ks", 16, F32), ("junk", 12 * _c, BF), ("cmp", 6 * _c, BF),
-                       ("so", 6 * _c, BF), ("d0", 4 * _m, F32), ("d1", 3 * _m, F32), ("both", 2 * _m, F32),
-                       ("sc", 3 * _m, F32), ("ex", 96, F32), ("tex", 96, F32), ("red", 4, F32), ("gt", _c, BF),
-                       ("ge", _c, BF), ("sg", _c, BF), ("cap", _c, BF), ("pos", _c, BF), ("cj", 6 * PITCH, BF),
-                       ("cc", 6 * PITCH, BF), ("co", 12 * PITCH, BF), ("ck", 6, F32), ("off", 12, U16)):
+    for _n, _w, _d in (("tr", _c, F32), ("ks", 16, F32), ("junk", 12 * _c, BF), ("cmp", 7 * _c, BF),
+                       ("so", 7 * _k, BF), ("gd", _m + 32, F32), ("gk", _m, F32), ("lb", _m + 32, F32),
+                       ("la", _m + 32, F32), ("ex", 192, F32), ("tex", 96, F32), ("red", 33, F32), ("gt", _c, BF),
+                       ("ge", _c, BF), ("sg", _c, BF), ("cap", _c, BF), ("pos", _c + 2, BF)):
         SCRATCH["%s%d" % (_n, _i)] = ("sbuf", [128, _w], _d)
 for _i in range(8):
     SCRATCH["b%d" % _i] = ("psum", [128, 512], F32)
 
-SEMAPHORES = ["cV", "cS", "cP", "cG", "arr1", "arr2", "left1", "left2"] + ["d%02d" % _i for _i in range(40)]
+SEMAPHORES = (["cV", "cS", "cP", "cG", "left1", "left2"] + ["arr%d" % _i for _i in range(6)]
+              + ["d%02d" % _i for _i in range(40)])
 
 
 def rank_program(g, core, T, topo):
@@ -110,6 +112,10 @@ def rank_program(g, core, T, topo):
     def fill(w, c):
         op("V", lambda: V.memset(ap(w), c), [], [w])
 
+    def act(o, i, f, bias=0.0, scale=1.0, acc=None):
+        op("S", lambda: S.activation(ap(o), ap(i), f, bias=val(bias), scale=val(scale), accum_out=val(acc)),
+           views(i, bias, scale), views(o, acc))
+
     def copy(o, i, e="V"):
         if e == "V":
             op("V", lambda: V.tensor_copy(ap(o), ap(i)), [i], [o])
@@ -126,10 +132,7 @@ def rank_program(g, core, T, topo):
             op("V", lambda: V.tensor_scalar(ap(o), ap(a), val(s1), val(s2), o1, o2), views(a, s1, s2), [o])
 
     def scan(o, d0, d1, init, o0, o1):
-        op("V", lambda: V.tensor_tensor_scan(ap(o), ap(d0), ap(d1), init, o0, o1), [d0, d1], [o])
-
-    def reduce(o, i, alu, neg):
-        op("V", lambda: V.tensor_reduce(ap(o), ap(i), AxisListType.X, alu, negate=neg), [i], [o])
+        op("V", lambda: V.tensor_tensor_scan(ap(o), ap(d0), ap(d1), val(init), o0, o1), views(d0, d1, init), [o])
 
     def turn(o, i):
         op("V", lambda: V.transpose(ap(o), ap(i)), [i], [o])
@@ -144,14 +147,13 @@ def rank_program(g, core, T, topo):
         op("V", lambda: V.tensor_copy(ap(w).indirect(ap(off)), ap(i)), [i, off], [w])
 
     def sign(o, row, thr, acc=None):
-        op("S", lambda: S.activation(ap(o), ap(row), F.Sign, bias=ap(thr), scale=-1.0, accum_out=val(acc)),
-           [row, thr], views(o, acc))
+        act(o, row, F.Sign, thr, -1.0, acc)
 
     def relu(e, o, i):
         if e == "V":
             ts(o, i, 0.0, A.max, 0.03125, A.mult)
         else:
-            op("S", lambda: S.activation(ap(o), ap(i), F.Relu, scale=0.03125), [i], [o])
+            act(o, i, F.Relu, 0.0, 0.03125)
 
     def quant(n, a, b, tile):
         q, s = v("q" + n, a, b), v("s" + n, a, b)
@@ -189,115 +191,75 @@ def rank_program(g, core, T, topo):
     def codes(n, a, b):
         return ap(v("q" + n, a, b)).bitcast(dt.uint8)
 
-    def exchange(src, src_at, dst, dst_at, sem, left):
-        for kind in ("q", "s"):
-            order("G", [v(kind + src)], [])
-            trs = []
-            for j in range(1, N):
-                d = (rank + j) % N
-                en = topo.engines(core, T.cores[d])
-                k = len(en) // 4
-                lo, hi = en[:2 * k], en[2 * k:]
-                if kind == "s":
-                    lo, hi = hi, lo
-                use = (lo[:k], lo[k:], hi)[j - 1]
-                rid, pid = topo.addr(T.cores[d])[:2]
-                a, b = src_at(d), dst_at(d)
-                if kind == "q":
-                    i, o = codes(src, a, a + PC), codes(dst, b, b + PC)
-                else:
-                    i, o = ap(v("s" + src, a, a + PC)), ap(v("s" + dst, b, b + PC))
-                trs.append(RemoteDMATransfer(dst_ids=[DstId(rid=rid, pnc=pid)], dma_engine_mask=sum(1 << x for x in use),
-                                             remote_sem=T.sem[sem], src=i, dst=o))
-                count[left] = count.get(left, 0) + len(use)
-                count[sem] = count.get(sem, 0) + len(use)
-            g.remote_dma_fused(trs, local_sem=T.sem[left])
+    def send(d, src, a, dst, b, both, sem, left):
+        en = topo.engines(core, T.cores[d])
+        rid, pid = topo.addr(T.cores[d])[:2]
+        wide = 4 * PC if both else PC
+        order("G", [v("q" + src, a, a + PC), v("s" + src, a, a + wide)], [])
+        pair = [(codes(src, a, a + PC), codes(dst, b, b + PC)),
+                (ap(v("s" + src, a, a + wide)), ap(v("s" + dst, b, b + wide)))]
+        half = len(en) // 2
+        use = (en[:half], en[half:]) if both else (en, en)
+        trs = [RemoteDMATransfer(dst_ids=[DstId(rid=rid, pnc=pid)], dma_engine_mask=sum(1 << x for x in u),
+                                 remote_sem=T.sem[sem], src=i, dst=o) for (i, o), u in zip(pair, use)]
+        for call in ([trs] if both else [trs[:1], trs[1:]]):
+            g.remote_dma_fused(call, local_sem=T.sem[left])
+        for k in (sem, left):
+            count[k] = count.get(k, 0) + len(use[0]) + len(use[1])
+        note("remote", sem, count[sem], [], [v("q" + dst, b, b + PC), v("s" + dst, b, b + wide)])
 
-    def landed(sem, n, a, b):
-        note("remote", sem, count[sem], [], [v("q" + n, a, b), v("s" + n, a, b)])
+    steps = sorted(range(1, N), key=lambda j: all(topo.die(T.cores[r]) == topo.die(T.cores[r ^ j]) for r in range(N)))
+    dest = [rank ^ j for j in steps] + [rank]
 
     def consts(i, m):
-        fill(v("d0%d" % i, 2 * m, 2 * m + 2), -128 * BIG)
-        fill(v("d0%d" % i, 3 * m, 3 * m + 2), -128 * BIG)
-        fill(v("d1%d" % i, 0, m), -64 * BIG)
-
-    def zeros(i, m):
-        level(v("d0%d" % i, 2 * m + 2, 3 * m), 0)
-        level(v("d0%d" % i, 3 * m + 2, 4 * m), 0)
+        fill(v("lb%d" % i, m), -64 * BIG)
+        fill(v("la%d" % i, m), 64 * BIG)
 
     def vcmp(i, n, slot, bank, thr):
-        ts(v("cmp%d" % i, n * slot, n * slot + n), v("b%d" % bank, 0, n), thr, A.is_gt)
+        ts(v("cmp%d" % i, n * slot, n * slot + n), v("b%d" % bank, 0, n), thr, A.is_gt, -1.0, A.mult)
 
-    def vsum(i, n, k, slot):
-        scan(v("so%d" % i, n * slot, n * slot + n), v("zero", 0, n), v("cmp%d" % i, n * slot, n * slot + n),
-             float(k), A.add, A.subtract)
+    def vsum(i, n, slot):
+        k = n // 2
+        scan(v("so%d" % i, k * slot, k * slot + k), v("cmp%d" % i, n * slot, n * slot + k),
+             v("cmp%d" % i, n * slot + k, n * slot + n), float(k), A.add, A.add)
 
-    def threshold(i, n, m, k, eoff):
+    def threshold(i, n, m, k, cands):
+        s, w = str(i), m // 2 + 16
+
+        def spread(block, src, other, init, alu):
+            at = 64 * block + 16
+            for h, o in enumerate((v("ex" + s, at + 16 - w, at + 16), v("ex" + s, at + 15 + w, at + 15, -1))):
+                d = v(src + s, h, 2 * w, 2)
+                scan(o, d, other or d, init, alu, alu)
+
+        def across(block):
+            turn(v("tex" + s, 32 * block, 32 * block + 32), v("ex" + s, 64 * block + 16, 64 * block + 48))
+
+        tt(v("lb" + s, 0, m), cands, v("gd" + s, 0, m), A.add)
+        tt(v("la" + s, 0, m), cands, v("gk" + s), A.add)
+        spread(0, "gd", v("zero", 0, w), (k - 0.5) / 32 * BIG, A.add)
+        spread(1, "lb", None, -64 * BIG, A.max)
+        across(0)
+        act(v("junk" + s, 11 * n, 11 * n + 32), v("tex" + s, 0, 32), F.Identity, 0.0, -1.0, v("red" + s, 32, 33))
+        spread(2, "la", None, 64 * BIG, A.min)
+        across(1)
+        across(2)
+        scan(v("red" + s, 0, 32), v("tex" + s, 32, 64), v("tex" + s, 64, 96), v("red" + s, 32, 33), A.max, A.min)
+
+    def running(i, n, k, bank, bank2, cut):
         s = str(i)
-        tt(v("d1" + s, m, 3 * m), v("d0" + s, 0, 2 * m), v("both" + s), A.add)
-        for h in range(2):
-            scan(v("sc" + s, h * 3 * m // 2, (h + 1) * 3 * m // 2), v("d0" + s, m + h, 4 * m, 2),
-                 v("d1" + s, h, 3 * m, 2), (k - 0.5) / 32 * BIG, A.add, A.max)
-        gather("V", v("ex" + s), v("sc" + s), v("offc", eoff, eoff + 6))
-        turn(v("tex" + s), v("ex" + s))
-        o, i_, acc = v("junk" + s, 11 * n, 11 * n + 32), v("tex" + s, 0, 32), v("red" + s, 0, 1)
-        op("S", lambda: S.activation(ap(o), ap(i_), F.Identity, scale=-1.0, accum_out=ap(acc)), [i_], [o, acc])
-        reduce(v("red" + s, 1, 2), v("tex" + s, 32, 64), A.max, True)
-        reduce(v("red" + s, 2, 3), v("tex" + s, 64, 96), A.max, False)
-        ts(v("red" + s, 3, 4), v("red" + s, 0, 1), v("red" + s, 1, 2), A.min, v("red" + s, 2, 3), A.max)
-
-    def spans(n, k, turn_by):
-        w, half = n - k + 16, k // 32
-        first = [(16 * m + turn_by) % k for m in range(2 * half)]
-        span = [(a, a + w) if a + 16 <= k else (0, n) for a in first]
-        low = all(b - a == w for a, b in span[:half])
-        return span, list(range(half)) if low else list(range(half, 2 * half))
-
-    def make_list(i, n, k, bank, bank2, co, thr, turn_by):
-        s = str(i)
-        row, t = v("b%d" % bank, 0, n), v("red" + s, 3, 4)
-        ts(v("gt" + s), row, t, A.is_gt)
-        if bank2 is None:
-            ts(v("ge" + s), row, t, A.is_ge)
-        else:
-            sign(v("sg" + s), v("b%d" % bank2, 0, n), t)
+        t = v("red" + s, 31, 32)
+        ts(v("gt" + s), v("b%d" % bank, 0, n), t, A.is_gt)
+        sign(v("sg" + s), v("b%d" % bank2, 0, n), t)
+        if cut < n:
+            act(v("ge" + s, cut, n), v("sg" + s, cut, n), F.Sign, 1.0, -1.0)
         scan(v("cap" + s, n - 2, None, -1), v("zero", 0, n - 1), v("gt" + s, n - 1, 0, -1), float(k), A.add, A.subtract)
-        if bank2 is not None:
-            ts(v("ge" + s), v("sg" + s), 0.0, A.is_le)
-        scan(v("pos" + s), v("ge" + s), v("cap" + s), 0.0, A.add, A.min)
-        w, half = n - k + 16, k // 32
-        span, on_s = spans(n, k, turn_by)
-        on_v = [m for m in range(2 * half) if m not in on_s]
-        for j, m in enumerate(on_s):
-            sign(v("cj" + s, w * j, w * j + w), v("pos" + s, *span[m]), v(thr, m, m + 1), v("ck" + s, j, j + 1))
-
-        def cmp(j):
-            a, b = span[on_v[j]]
-            ts(v("cc" + s, PITCH * j, PITCH * j + b - a), v("pos" + s, a, b), v(thr, on_v[j], on_v[j] + 1), A.is_le,
-               2.0, A.mult)
-
-        def tot(j):
-            a, b = span[on_v[j]]
-            end = PITCH * on_v[j] + PITCH
-            scan(v("co" + s, end - b + a, end), v("zero", 0, b - a), v("cc" + s, PITCH * j, PITCH * j + b - a),
-                 float(2 * a - 256), A.add, A.add)
-
-        cmp(0)
-        for j in range(1, half):
-            cmp(j)
-            tot(j - 1)
-        tot(half - 1)
-        tt(v("co" + s, PITCH * on_s[0] + PITCH - 1, PITCH * on_s[-1] + PITCH, PITCH), v("ck" + s, 0, half),
-           v("cs", co, co + half), A.add)
-        ts(v("off" + s, 0, 2 * half), v("co" + s, PITCH - 1, 2 * PITCH * half, PITCH), 0.5, A.mult, 128.0, A.add)
-
-    def xs(j):
-        return v("win", XO + 512 * j, XO + 512 * j + 512)
+        ts(v("ge" + s, 0, cut), v("sg" + s, 0, cut), 0.0, A.is_le)
+        scan(v("pos" + s, 1, n + 1), v("ge" + s), v("cap" + s), 0.0, A.add, A.min)
 
     dma("Y", ap(v("tu1")), T.u1[:], [], [v("tu1")])
-    dma("S", ap(xs(0)), T.x[:, 0:512], [], [xs(0)])
-    dma("Y", ap(xs(1)), T.x[:, 512:1024], [], [xs(1)])
-    dma("S", ap(xs(2)), T.x[:, 1024:1536], [], [xs(2)])
+    dma("Y", ap(v("win", 0, 1024)), T.x[:, 0:1024], [], [v("win", 0, 1024)])
+    dma("Y", ap(v("win", 1024, 1536)), T.x[:, 1024:1536], [], [v("win", 1024, 1536)])
     dma("Y", ap(v("tu2")), T.u2[:], [], [v("tu2")])
     dma("Y", codes("w", 0, 512), T.wc[:], [], [v("qw")])
     dma("Y", ap(v("sw")), T.ws[:], [], [v("sw")])
@@ -307,11 +269,7 @@ def rank_program(g, core, T, topo):
 
     iota(v("oi", 0, 16), [[16, 2], [32, 4], [0, 2]], 0)
     iota(v("oi", 16, 24), [[16, 8]], 0)
-    iota(v("oi", 24, 30), [[8, 3], [24, 2]], 7)
-    iota(v("oi", 30, 36), [[6, 3], [18, 2]], 5)
     iota(v("pi", 0, 1), [[0, 1]], 0, 1)
-    iota(v("m16"), [[16, 12]], 0)
-    iota(v("jm"), [[0, 6], [1, 16]], 0)
     fill(v("zero"), 0.0)
     consts(1, 16)
     consts(2, 12)
@@ -319,235 +277,343 @@ def rank_program(g, core, T, topo):
     ts(v("pi", 1, 2), v("pi", 0, 1), 15, A.bitwise_and)
     ts(v("pi", 3, 4), v("pi", 0, 1), 3, A.bitwise_and)
     ts(v("pi", 2, 3), v("pi", 1, 2), 2, A.logical_shift_right)
-    copy(v("pf"), v("pi"))
-    ts(v("thr"), v("m16"), v("pf", 1, 2), A.add, 0.5, A.add)
-    ts(v("gate"), v("jm"), v("pf", 1, 2), A.is_le, BIG, A.mult)
-    ts(v("thr2", 6, 12), v("thr", 0, 6), float(PC * rank), A.add)
-    ts(v("thr2", 12, 18), v("thr", 0, 6), float(KB - PC * rank), A.is_ge, -float(KB), A.mult)
-    ts(v("gate2"), v("jm"), v("pf", 1, 2), A.is_gt, 1024.0, A.mult)
-    tt(v("thr2", 0, 6), v("thr2", 6, 12), v("thr2", 12, 18), A.add)
-    ts(v("oh"), v("jm", 0, 4), v("pf", 2, 3), A.is_equal, 4.0, A.mult)
-    zeros(1, 16)
-    zeros(2, 12)
-    for at, n, k, by in ((0, C, KA, 0), (6, KA, KB, PC * rank)):
-        span, on_s = spans(n, k, by)
-        iota(v("cs", at, at + 6), [[32, 6]], sum(span[on_s[0]]) - 256)
+    copy(v("pf", 0, 4), v("pi"))
+    iota(v("m16"), [[16, KB]], 0)
+    for i in range(N):
+        iota(v("m2", 2 * i, 2 * i + 2), [[16, 2]], PC * dest[i])
+    level(v("gd1", 16), 0)
+    NS1 = 5
+    iota(v("cs", 0, NS1), [[32, NS1]], W1 - 256)
     level(v("cap1", C - 1), KA)
-    level(v("cap2", KA - 1), KB)
-
-    ca, cb, cc = v("tr1", 0, 128, 16), v("tr1", 128, 256, 16), v("tr1", 256, 384, 16)
-    mn, mx, z, lo, hi = (v("srt", 8 * j, 8 * j + 8) for j in range(5))
-    quant("u1", 0, 128, v("tu1"))
-    picks("V", "1", 0, 256)
-    picks("S", "1", 0, 256)
-    picks("S", "1", 256, 384)
-    quant("x", 0, 128, xs(0))
-    mm(0, "u1", 0, "x", 0, 128)
-    quant("x", 128, 256, xs(1))
-    mm(1, "u1", 0, "x", 128, 128)
-    turn(v("tr1", 0, 128), v("b0", 0, 128))
-    quant("x", 256, 384, xs(2))
-    mm(2, "u1", 0, "x", 256, 128)
-    mm(3, "p1", 0, "x", 0, C)
-    mm(4, "p1", 128, "x", 0, C)
-    mm(5, "p1", 128, "x", 0, C)
-    turn(v("tr1", 128, 256), v("b1", 0, 128))
-    tt(mx, ca, cb, A.max)
-    tt(mn, ca, cb, A.min)
-    planes("xp", "win", XO, C)
-    level(v("one"), 1)
-    for b in range(4):
-        op("G", lambda: g.affine_select(ap(v("te", 512 * b, 512 * b + 512)), ap(v("one")), [[8, 128], [1, 4]],
-                                        A.is_equal, 0.0, -b, -8), [v("one")], [v("te", 512 * b, 512 * b + 512)])
-    level(v("tg", 4 * KB), 0)
-    iota(v("ramp"), [[1, C]], 0)
-    iota(v("idx"), [[1, C]], KB + KA)
-
-    turn(v("tr1", 256, 384), v("b2", 0, 128))
-    tt(z, mx, cc, A.min)
-    tt(lo, mn, cc, A.min)
-    tt(v("both1", 16, 24), mn, z, A.max)
-    tt(hi, mx, cc, A.max)
+    level(v("pos1", 0, 1), 0)
+    act(v("pf", 4, 5), v("pf", 1, 2), F.Identity, 0.5)
+    act(v("thr"), v("m16", 0, 12), F.Identity, v("pf", 4, 5))
+    act(v("pf", 6, 7), v("pf", 1, 2), F.Identity, 4.0 * C - 4 - FAR, -1.0)
+    act(v("pf", 7, 8), v("pf", 2, 3), F.Identity, FAR, FAR)
+    act(v("pf", 5, 6), v("pf", 3, 4), F.Identity, v("pf", 6, 7))
+    act(v("m2"), v("m2"), F.Identity, v("pf", 4, 5))
 
     def cand(c):
-        return v("both1", 16 + c, 17 + c)
+        return v("cd", c, c + 1)
+
+    def sort3(h, step):
+        ca, cb, cc = (v("tr1", 192 * h + 64 * j, 192 * h + 64 * j + 64, 16) for j in range(3))
+        mn, mx, z, lo, hi = (v("srt", 8 * j + 4 * h, 8 * j + 4 * h + 4) for j in range(5))
+        if step == 0:
+            tt(mx, ca, cb, A.max)
+            tt(mn, ca, cb, A.min)
+        elif step == 1:
+            tt(z, mx, cc, A.min)
+            tt(lo, mn, cc, A.min)
+        elif step == 2:
+            tt(v("cd", 4 * h, 4 + 4 * h), mn, z, A.max)
+        else:
+            tt(hi, mx, cc, A.max)
 
     def scount(j, c):
-        sign(v("junk1", C * j, C * j + C), v("b%d" % (5 if c % 2 else 3), 0, C), cand(c), v("ks1", c, c + 1))
+        sign(v("junk1", C * j, C * j + C), v("b%d" % (4 if c % 2 else 2), 0, C), cand(c), v("ks1", c, c + 1))
 
     def gate1(o, i):
         ts(o, i, 0.0, A.is_gt, -2 * BIG, A.mult)
 
-    def choose(a, b, step):
+    def choose(a, b, step, s=1):
         if step == 0:
-            tt(v("srt", a, b), v("srt", 32 + a, 32 + b), v("d01", 16 + a, 16 + b), A.add)
+            tt(v("srt", a, b, s), v("srt", 32 + a, 32 + b, s), v("gd1", a, b, s), A.add)
         else:
-            tt(v("both1", 24 + a, 24 + b), v("srt", a, b), v("srt", 24 + a, 24 + b), A.max)
+            tt(v("cd", 8 + a, 8 + b, s), v("srt", a, b, s), v("srt", 24 + a, 24 + b, s), A.max)
 
-    for j, c in enumerate((0, 2, 4, 6, 5, 7)):
-        scount(j, c)
-    picks("V", "1", 256, 384)
+    quant("u1", 0, 128, v("tu1"))
+    picks("V", "1", 0, 384)
+    picks("S", "1", 0, 384)
+    quant("x", 0, 128, v("win", 0, 512))
+    mm(0, "u1", 0, "x", 0, 128)
+    quant("x", 128, 256, v("win", 512, 1024))
+    mm(1, "u1", 0, "x", 128, 128)
+    turn(v("tr1", 0, 128), v("b0", 0, 128))
+    turn(v("tr1", 128, 192), v("b1", 0, 64))
+    quant("x", 256, 384, v("win", 1024, 1536))
+    mm(2, "p1", 0, "x", 0, C)
+    mm(5, "u1", 0, "x", 256, 128)
+    mm(3, "p1", 128, "x", 0, C)
+    mm(4, "p1", 128, "x", 0, C)
     mm(6, "p1", 256, "x", 0, C)
     mm(7, "p1", 256, "x", 0, C)
-    vcmp(1, C, 0, 4, cand(1))
-    vcmp(1, C, 1, 4, cand(3))
-    vsum(1, C, KA, 0)
-    vsum(1, C, KA, 1)
-    gate1(v("d01", 16, 21, 2), v("ks1", 0, 5, 2))
-    gate1(v("d01", 17, 20, 2), v("so1", C - 1, 2 * C, C))
-    choose(0, 5, 0)
-    choose(0, 5, 1)
-    for j, c in enumerate((8, 10, 12)):
-        scount(6 + j, c)
-    vcmp(1, C, 2, 4, cand(9))
-    gate1(v("d01", 21, 24), v("ks1", 5, 8))
-    vcmp(1, C, 3, 4, cand(11))
-    choose(5, 8, 0)
-    vsum(1, C, KA, 2)
-    choose(5, 8, 1)
-    scount(9, 14)
-    scount(10, 15)
-    vsum(1, C, KA, 3)
-    vcmp(1, C, 4, 4, cand(13))
-    ts(v("d01", 0, 8), v("d01", 16, 24), 0.0, A.is_equal, -BIG, A.mult)
-    vsum(1, C, KA, 4)
-    ts(v("both1", 0, 16), v("both1", 16, 32), -1.0, A.mult)
-    copy(v("ks1", 9, 14, 2), v("so1", 3 * C - 1, 5 * C, C))
+    level(v("one"), 1)
+    op("G", lambda: g.affine_select(ap(v("te")), ap(v("one")), [[1, 516]], A.is_equal, 0.0, -3, -4), [v("one")],
+       [v("te")])
+    planes("xp", "win", 0, C)
+    level(v("gd2", 12), 0)
+    level(v("cap2", KA - 1), KB)
+    level(v("tg", 128, 512), 0)
+    iota(v("ramp"), [[1, C]], 0)
+    iota(v("jm"), [[0, KB], [1, 4]], 0)
+    level(v("tt", 4 * 104), 0)
+
+    sort3(0, 0)
+    sort3(0, 1)
+    sort3(0, 2)
+    turn(v("tr1", 192, 256), v("b1", 64, 128))
+    turn(v("tr1", 256, 384), v("b5", 0, 128))
+    sort3(0, 3)
+    for j, c in enumerate((0, 2, 1)):
+        scount(j, c)
+    sort3(1, 0)
+    vcmp(1, C, 0, 3, cand(3))
+    sort3(1, 1)
+    vsum(1, C, 0)
+    sort3(1, 2)
+    gate1(v("gd1", 0, 4, 2), v("ks1", 0, 4, 2))
+    sort3(1, 3)
+    scount(3, 4)
+    scount(4, 6)
+    choose(0, 4, 0, 2)
+    vcmp(1, C, 1, 3, cand(5))
+    choose(0, 4, 1, 2)
+    scount(5, 8)
+    scount(6, 10)
+    gate1(v("gd1", 1, 2), v("ks1", 1, 2))
+    vsum(1, C, 1)
+    vcmp(1, C, 2, 3, cand(7))
+    gate1(v("gd1", 4, 8, 2), v("ks1", 4, 8, 2))
+    vsum(1, C, 2)
+    choose(4, 8, 0, 2)
+    gate1(v("gd1", 3, 8, 2), v("so1", KA - 1, 3 * KA, KA))
+    choose(4, 8, 1, 2)
+    choose(1, 8, 0, 2)
     quant("u2", 0, 128, v("tu2"))
-    picks("S", "2", 0, 384)
-    ts(v("d01", 24, 32), v("ks1", 8, 16), 0.0, A.is_gt, -BIG, A.mult)
-    ts(v("d01", 8, 16), v("ks1", 8, 16), 0.0, A.is_le, -BIG, A.mult)
-    threshold(1, C, 16, KA, 24)
-    make_list(1, C, KA, 6, 7, 0, "thr", 0)
+    choose(1, 8, 1, 2)
+    for j, c in enumerate((12, 14, 13, 15)):
+        scount(7 + j, c)
+    ts(v("gk1", 0, 8), v("gd1", 0, 8), 0.0, A.is_equal, BIG, A.mult)
+    vcmp(1, C, 3, 3, cand(9))
+    vcmp(1, C, 4, 3, cand(11))
+    vsum(1, C, 3)
+    vsum(1, C, 4)
+    ts(v("thr2"), v("m2"), KB - 0.5, A.min)
+    copy(v("ks1", 9, 12, 2), v("so1", 4 * KA - 1, 5 * KA, KA))
+    picks("S", "2", 0, 256)
+    picks("S", "2", 256, 384)
+    ts(v("gd1", 8, 16), v("ks1", 8, 16), 0.0, A.is_gt, -BIG, A.mult)
+    ts(v("gk1", 8, 16), v("ks1", 8, 16), 0.0, A.is_le, BIG, A.mult)
+    threshold(1, C, 16, KA, v("cd"))
+    running(1, C, KA, 6, 7, KA)
+
+    for m in range(NS1):
+        sign(v("cj1", W1 * m, W1 * m + W1), v("pos1", 1 + 16 * m, 1 + 16 * m + W1), v("thr", m, m + 1),
+             v("ck1", m, m + 1))
+    H1 = W1 // 2
+
+    def cmp1(m):
+        ts(v("cc1", W1 * m, W1 * m + W1), v("pos1", 1 + 16 * m, 1 + 16 * m + W1), v("thr", m, m + 1), A.is_le,
+           2.0, A.mult)
+
+    def tot1(m):
+        scan(v("co1", H1 * m, H1 * m + H1), v("cc1", W1 * m, W1 * m + H1), v("cc1", W1 * m + H1, W1 * m + W1),
+             float(32 * m - 256), A.add, A.add)
+
+    cmp1(NS1)
+    for m in range(NS1 + 1, 12):
+        cmp1(m)
+        tot1(m - 1)
+    tot1(11)
+    tt(v("co1", H1 - 1, H1 * NS1, H1), v("ck1", 0, NS1), v("cs", 0, NS1), A.add)
+    ts(v("off1"), v("co1", H1 - 1, 12 * H1, H1), 0.5, A.mult, 128.0, A.add)
 
     for t, e in enumerate("SVSV"):
         gather(e, v("tf", t, 4 * KA, 4), v("xp", C * t, C * t + C), v("off1"))
     quant("f", 0, KA, v("tf"))
     for b in range(4):
         mm(b, "w", 128 * b, "f", 0, KA)
-    fh = v("win", 4 * KB, XO)
+    fh = v("win", 4 * C)
     dma("Y", ap(fh), ap(v("tf")), [v("tf")], [fh])
-    picks("V", "2", 0, 384)
-    quant("e", 0, 256, v("te", 0, 1024))
-    for b, e in enumerate("SSSV"):
-        relu(e, v("th", b, 4 * KA, 4), v("b%d" % b, 0, KA))
+    act(v("gate"), v("jm"), F.Relu, v("pf", 7, 8), -FAR)
+    picks("V", "2", 0, 256)
+    relu("S", v("th", 0, 4 * KA, 4), v("b0", 0, KA))
+    relu("S", v("th", 1, 4 * KA, 4), v("b1", 0, KA))
+    relu("V", v("th", 2, 4 * KA, 4), v("b2", 0, KA))
+    relu("S", v("th", 3, 4 * KA, 4), v("b3", 0, KA))
     quant("h", 0, KA, v("th"))
     planes("hp", "th", 0, KA)
     dma("G", ap(fh), ap(v("th")), [v("th"), fh], [fh], accum_op=A.add)
-    level(v("to", 4 * PC), 0)
-    level(v("tt", 12 * PC), 0)
     mm(4, "u2", 0, "h", 0, KA)
     mm(5, "p2", 0, "h", 0, KA)
     mm(6, "p2", 128, "h", 0, KA)
     mm(7, "p2", 128, "h", 0, KA)
-    mm(0, "p2", 256, "h", 0, KA)
-    quant("e", 256, 512, v("te", 1024))
+    picks("V", "2", 256, 384)
 
-    turn(v("tr2"), v("b4", 0, KA))
+    turn(v("tr2", 0, 64), v("b4", 0, 64))
+    turn(v("tr2", 64, KA), v("b4", 64, KA))
     for j, c in enumerate((0, 2, 4, 6, 8, 10, 9, 11)):
         sign(v("junk2", KA * j, KA * j + KA), v("b%d" % (7 if c % 2 else 5), 0, KA), v("tr2", 16 * c, 16 * c + 1),
              v("ks2", c, c + 1))
+    mm(0, "p2", 256, "h", 0, KA)
+    mm(1, "p2", 256, "h", 0, KA)
     vcmp(2, KA, 0, 6, v("tr2", 16, 17))
     for j in range(1, 4):
         vcmp(2, KA, j, 6, v("tr2", 32 * j + 16, 32 * j + 17))
-        vsum(2, KA, KB, j - 1)
-    ts(v("both2", 0, 12), v("tr2", 0, KA, 16), -1.0, A.mult)
-    vsum(2, KA, KB, 3)
-    copy(v("both2", 12, 24), v("tr2", 0, KA, 16))
-    copy(v("ks2", 1, 8, 2), v("so2", KA - 1, 4 * KA, KA))
-    ts(v("d02", 12, 24), v("ks2", 0, 12), 0.0, A.is_gt, -BIG, A.mult)
-    ts(v("d02", 0, 12), v("ks2", 0, 12), 0.0, A.is_le, -BIG, A.mult)
+        vsum(2, KA, j - 1)
+    scan(v("pa"), v("gate"), v("pos1", 1, C + 1), 0.0, A.add, A.min)
+    vsum(2, KA, 3)
+    scan(v("pb"), v("gate"), v("pos1", 0, C), 0.0, A.add, A.min)
+    copy(v("ks2", 1, 8, 2), v("so2", KB - 1, 4 * KB, KB))
+    ya, yc, yd, ye = (v("yy", KB * j, KB * j + KB) for j in range(4))
+    act(ya, v("pa", 3, C, 4), F.Identity, v("pf", 5, 6), FAR + 4)
+    act(yc, v("pb", 3, C, 4), F.Identity, 0.0, FAR)
     gather("S", v("l1"), v("ramp"), v("off1"))
-    threshold(2, KA, 12, KB, 30)
-    make_list(2, KA, KB, 0, None, 6, "thr2", PC * rank)
-    off2 = v("off2", 0, 6)
+    ts(v("gd2", 0, 12), v("ks2", 0, 12), 0.0, A.is_gt, -BIG, A.mult)
+    ts(v("gk2", 0, 12), v("ks2", 0, 12), 0.0, A.is_le, BIG, A.mult)
+    threshold(2, KA, 12, KB, v("tr2", 0, KA, 16))
+    running(2, KA, KB, 0, 1, KA)
 
+    H2 = W2 // 2
+
+    def span2(m):
+        a = PC * dest[m // 2] + 16 * (m % 2)
+        return a, min(a + W2, KA)
+
+    def cmp2(m):
+        a, b = span2(m)
+        ts(v("cc2", W2 * m, W2 * m + b - a), v("pos2", 1 + a, 1 + b), v("thr2", m, m + 1), A.is_le)
+
+    def tot2(m):
+        a, b = span2(m)
+        h = (b - a) // 2
+        scan(v("co2", H2 * m + H2 - h, H2 * m + H2), v("cc2", W2 * m, W2 * m + h), v("cc2", W2 * m + h, W2 * m + 2 * h),
+             float(a), A.add, A.add)
+
+    def scnt2(m):
+        a, b = span2(m)
+        sign(v("cj1", W2 * m, W2 * m + b - a), v("pos2", 1 + a, 1 + b), v("thr2", m, m + 1), v("ck2", m, m + 1))
+
+    def sout2(m):
+        a, b = span2(m)
+        ts(v("off2", m, m + 1), v("ck2", m, m + 1), 0.5, A.mult, (a + b) / 2, A.add)
+
+    def tcol(i):
+        return 96 + 32 * i if i else 0
+
+    cmp2(0)
+    cmp2(1)
+    for m in (2, 3, 4):
+        scnt2(m)
+    tot2(0)
+    tot2(1)
+    copy(v("off2", 0, 2), v("co2", H2 - 1, 2 * H2, H2))
     for t, e in enumerate("SVSV"):
-        gather(e, v("tg", t, 4 * KB, 4), v("hp", KA * t, KA * t + KA), off2)
-    quant("g", 0, 128, v("tg"))
-    exchange("g", lambda d: PC * ((d - rank) % N), "x", lambda d: C + PC * ((rank - d) % N - 1), "arr1", "left1")
-    landed("arr1", "x", C, C + 3 * PC)
+        gather(e, v("tg", t, 128, 4), v("hp", KA * t, KA * t + KA), v("off2", 0, 2))
+    quant("a", 0, 128, v("tg", 0, 512))
+    send(dest[0], "a", 0, "g", 128, True, "arr0", "left1")
+    scnt2(5)
+    cmp2(6)
+    cmp2(7)
+    sout2(2)
+    tot2(6)
+    tot2(7)
+    for m in (3, 4, 5):
+        sout2(m)
+    copy(v("off2", 6, 8), v("co2", 7 * H2 - 1, 8 * H2, H2))
+    for t, e in enumerate("SVSV"):
+        gather(e, v("tg", 512 + t, 896, 4), v("hp", KA * t, KA * t + KA), v("off2", 2, 8))
+    quant("g", 0, 128, v("tg", 384, 896))
+    send(dest[1], "g", 32, "x", C, True, "arr1", "left1")
+    send(dest[2], "g", 64, "f", KA, False, "arr2", "left1")
 
-    def up(b, at, a, e):
-        tt(v("hs", 4 * a + b, 4 * e, 4), v("b%d" % (1 + b), at, at + e - a), v("tg", 4 * a + b, 4 * e, 4), A.add)
-
-    def up2(b, a, e):
-        tt(v("win", 4 * a + b, 4 * e, 4), v("hs", 4 * a + b, 4 * e, 4), v("fg", 4 * a + b, 4 * e, 4), A.add)
-
-    for b in range(4):
-        mm(1 + b, "z", 128 * b, "g", 0, 128)
-    gather("S", v("olr"), v("l1"), off2)
-    for b in range(4):
-        relu("S", v("to", b, 4 * PC, 4), v("b%d" % (1 + b), 0, PC))
-    tt(v("olm"), v("olr"), v("gate2"), A.add)
-    scatter(v("idx"), v("off1"), v("ramp", KB, KB + KA))
-    scan(v("old"), v("gate"), v("olm"), 0.0, A.add, A.min)
-    quant("o", 0, 128, v("to"))
-    copy(v("offo"), v("old", 15, KB, 16))
-    for b in range(4):
-        mm(1 + b, "e", 128 * b, "o", 0, 128)
-    for t in range(4):
-        gather("S", v("fg", t, 4 * KB, 4), v("xp", C * t, C * t + C), v("offo"))
-    scatter(v("idx"), v("offo"), v("ramp", 0, KB))
-    for b in range(4):
-        up(b, 0, 0, PC)
-    for a in range(4):
-        o, i, sc = v("pick", KB * a, KB * a + KB), v("idx", a, C, 4), v("oh", a, a + 1)
-        op("S", lambda: S.activation(ap(o), ap(i), F.Copy, scale=ap(sc)), [i, sc], [o])
+    gather("S", v("olr"), v("l1"), v("off2"))
+    tt(yd, ya, yc, A.subtract)
+    scan(v("old"), v("gate", 0, 128), v("olr"), 0.0, A.add, A.min)
+    tt(ye, yd, v("m16"), A.max)
+    ts(v("offs", 18, 24), v("old", 99, 120, 4), 4.0, A.mult, v("pf", 3, 4), A.add)
+    ts(v("offx"), ye, v("pf", 1, 2), A.add)
+    for i in range(N - 1):
+        ts(v("offs", 6 * i, 6 * i + 6), v("old", 32 * i + 3, 32 * i + PC, 4), 4.0, A.mult, v("pf", 3, 4), A.add)
     wait("Y", "left1", count["left1"], {})
-    dma("Y", T.ol[:, PC * rank:KB], T.olr[0:128:16, 0:KB - PC * rank], [v("olr")], [])
-    if rank:
-        dma("Y", T.ol[:, 0:PC * rank], T.olr[0:128:16, KB - PC * rank:KB], [v("olr")], [])
+    for i in range(N):
+        dma("Y", T.ol[:, PC * dest[i]:PC * dest[i] + PC], T.olr[0:128:16, 32 * i:32 * i + PC], [v("olr")], [])
 
-    zb, at = (5, 6, 7, 0), 128 - 3 * PC
-    for b in range(4):
-        mm(zb[b], "z", 128 * b, "x", C - at, 128)
-    for b, e in enumerate("SVSV"):
-        relu(e, v("tt", b, 12 * PC, 4), v("b%d" % zb[b], at, 128))
-    quant("t", 0, 128, v("tt"))
-    exchange("t", lambda d: PC * ((d - rank) % N - 1), "h", lambda d: KA + PC * ((rank - d) % N - 1), "arr2", "left2")
-    landed("arr2", "h", KA, KA + 3 * PC)
-
-    tt(v("sum2"), v("pick", 0, KA), v("pick", KA, C), A.add)
-    quant("v", 0, 128, v("tv"))
-    tt(v("sum1"), v("sum2", 0, KB), v("sum2", KB, KA), A.add)
-    tt(v("win", 0, 4 * PC), v("hs", 0, 4 * PC), v("fg", 0, 4 * PC), A.add)
-    ts(v("offx"), v("sum1"), v("pf", 3, 4), A.add)
-
-    for b in range(4):
-        mm(1 + b, "e", 128 * b, "h", KA - at, 128)
-    up(0, at, PC, KB)
-    up(1, at, PC, KB)
-    up2(0, PC, KB)
-    up(2, at, PC, KB)
-    up2(1, PC, KB)
-    up(3, at, PC, KB)
-    up2(2, PC, KB)
-    up2(3, PC, KB)
+    def parts(i, j):
+        gather("S", v("fg", KB * i, KB * j), v("win", 0, 4 * C), v("offs", 6 * i, 6 * j))
 
     def place(e, a, b):
         gather(e, v("tx", 4 * a, 4 * b), v("win"), v("offx", a // 4, b // 4))
 
-    def yout(e, q, j):
-        w = v("yb", 128 * j, 128 * j + 128)
-        copy(w, v("b%d" % (5 + j), 0, 128), e)
-        dma(q, T.y[:, 128 * j:128 * j + 128], ap(w), [w], [])
+    def emake(b):
+        quant("e", 128 * b, 128 * b + 128, v("te", 3 - b, 515 - b))
 
-    cut = (64, 80, 80)
-    for j in range(3):
-        a = 128 * j
-        place("S", a, a + cut[j])
-        place("V", a + cut[j], a + 128)
-        if j == 1:
-            yout("V", "Y", 0)
-        quant("y", a, a + 128, v("tx", 4 * a, 4 * a + 512))
-        if j == 2:
-            yout("S", "S", 1)
-        mm(5 + j, "v", 0, "y", a, 128)
-        dma("Y", T.oc[:, 4 * a:4 * a + 512], codes("y", a, a + 128), [v("qy", a, a + 128)], [])
+    def through(banks, src, a, at, to, n):
+        for b in range(4):
+            mm(banks[b], "z", 128 * b, src, a, 128)
+        for b in range(4):
+            relu("S", v("tt", 4 * to + b, 4 * (to + 128 - at), 4), v("b%d" % banks[b], at, 128))
+        quant(n, 0, 128, v("tt", 4 * to, 4 * to + 512))
+
+    def unpack(banks, src, a):
+        for b in range(4):
+            mm(banks[b], "e", 128 * b, src, a, 128)
+
+    def up(banks, at, i, via=None):
+        run = (KB * i, KB * i + KB)
+        if via is None:
+            for b in range(4):
+                tt(v("hs", KB * i + b, KB * i + KB, 4), v("b%d" % banks[b], at, at + PC),
+                   v("tg", 4 * tcol(i) + b, 4 * (tcol(i) + PC), 4), A.add)
+        else:
+            for b in range(4):
+                copy(v("dd", via + b, via + 4 * PC, 4), v("b%d" % banks[b], at, at + PC), "S")
+            tt(v("hs", *run), v("dd", via, via + 4 * PC), v("tg", 4 * tcol(i), 4 * (tcol(i) + PC)), A.add)
+
+    def up2(i):
+        run = (KB * i, KB * i + KB)
+        tt(v("nw", *run), v("hs", *run), v("fg", *run), A.add)
+
+    def put(i, j):
+        scatter(v("tx"), v("offs", 6 * i, 6 * j), v("nw", KB * i, KB * j))
+
+    lo4, hi4 = (0, 1, 2, 3), (4, 5, 6, 7)
+    place("S", 0, 96)
+    place("V", 288, C)
+    place("S", 96, 192)
+    parts(3, 4)
+    emake(0)
+    emake(1)
+    through(hi4, "g", PC, 72, 2 * PC, "t1")
+    send(dest[0], "t1", 32, "h", KA, True, "arr3", "left2")
+    emake(2)
+    through(lo4, "x", C + PC - 128, 104, PC, "t2")
+    send(dest[1], "t2", 0, "a", 128, True, "arr4", "left2")
+    emake(3)
+    through(hi4, "f", KA + PC - 128, 104, 0, "t3")
+    send(dest[2], "t3", 0, "f", KA + PC, True, "arr5", "left2")
+
+    unpack(lo4, "t1", 0)
+    place("S", 192, 288)
+    parts(0, 1)
+    parts(1, 3)
+    up(lo4, 0, 3)
+    quant("v", 0, 128, v("tv"))
+    up2(3)
+    put(3, 4)
+    unpack(hi4, "h", KA + PC - 128)
+    up(hi4, 104, 0, 0)
+    up2(0)
+    put(0, 1)
+    unpack(lo4, "a", PC)
+    up(lo4, 104, 1, 128)
+    unpack(hi4, "f", KA + 2 * PC - 128)
+    up(hi4, 104, 2)
+    up2(1)
+    up2(2)
+    put(1, 3)
+
+    quant("y", 0, 256, v("tx", 0, 1024))
+    mm(0, "v", 0, "y", 0, 256)
+    quant("y", 256, C, v("tx", 1024))
+    mm(1, "v", 0, "y", 256, 128)
+    dma("Y", T.oc[:], codes("y", 0, C), [v("qy")], [])
     for k in range(4):
-        dma("YS"[k // 2], T.osc[4 * k:4 * k + 4, :], T.sy[32 * k:32 * k + 4, :], [v("sy")], [])
-    yout("V", "S", 2)
+        dma("Y", T.osc[4 * k:4 * k + 4, :], T.sy[32 * k:32 * k + 4, :], [v("sy")], [])
+    copy(v("yb", 0, 256), v("b0", 0, 256), "S")
+    copy(v("yb", 256, C), v("b1", 0, 128), "V")
+    dma("Y", T.y[:], ap(v("yb")), [v("yb")], [])
 
     for sem in SEMAPHORES:
         if seen.get(sem, 0) < count.get(sem, 0):

@@ -16,18 +16,18 @@ for _n, _w in (("x", C + 4 * PC), ("h", KA + 4 * PC), ("f", KA + 5 * PC), ("a", 
 for _n, _w, _d in (
         ("win", 4 * (C + KA), BF), ("xp", 4 * C, BF), ("hp", 4 * KA, BF), ("tu1", 512, BF), ("tu2", 512, BF),
         ("tv", 512, BF), ("tf", 4 * KA, BF), ("th", 4 * KA, BF), ("tg", 4 * 224, BF), ("tt", 4 * 176, BF),
-        ("dd", 256, BF), ("te", 516, BF), ("one", 516, BF), ("zero", C, BF), ("fg", 4 * KB, BF), ("hs", 4 * KB, BF),
-        ("nw", 4 * KB, BF), ("tx", 4 * C, BF), ("yb", C, F32),
-        ("oi", 24, I32), ("offc", 24, U16), ("pi", 4, I32), ("pf", 8, F32), ("m16", KB, F32), ("thr", 12, F32),
+        ("te", 516, BF), ("one", 516, BF), ("zero", C, BF), ("hs", 1024, BF), ("alt", 2 * KB, BF),
+        ("nw", 1024, BF), ("tx", 4 * C, BF), ("yb", C, F32),
+        ("oi", 24, I32), ("offc", 24, U16), ("pi", 4, I32), ("pf", 8, F32), ("m16", 12, F32), ("thr", 12, F32),
         ("cs", 6, F32), ("ramp", C, F32), ("jm", C, BF), ("gate", C, BF), ("m2", 8, F32), ("thr2", 8, F32),
-        ("l1", KA, F32), ("olr", 128, F32), ("old", 128, F32), ("offs", 24, U16), ("pa", C, BF), ("pb", C, BF),
-        ("yy", 4 * KB, F32), ("offx", KB, U16), ("srt", 40, F32), ("cd", 16, F32),
+        ("l1", KA, F32), ("olr", 128, F32), ("old", 128, F32), ("offs", 32, U16), ("pa", C, BF), ("pb", C, BF),
+        ("yy", 6 * KB, F32), ("offx", KB, U16), ("srt", 40, F32), ("two", 16, F32), ("cd", 16, F32),
         ("cj1", 6 * W1, BF), ("cc1", 12 * W1, BF), ("co1", 6 * W1, BF), ("ck1", 6, F32), ("off1", 12, U16),
         ("cc2", 8 * W2, BF), ("co2", 4 * W2, F32), ("ck2", 8, F32), ("off2", 8, U16)):
     SCRATCH[_n] = ("sbuf", [128, _w], _d)
 for _i, _c, _k, _m in ((1, C, KA, 16), (2, KA, KB, 12)):
     for _n, _w, _d in (("tr", _c, F32), ("ks", 16, F32), ("junk", 12 * _c, BF), ("cmp", 7 * _c, BF),
-                       ("so", 7 * _k, BF), ("gd", _m + 32, F32), ("gk", _m, F32), ("lb", _m + 32, F32),
+                       ("so", 7 * _k, BF), ("gd", _m, F32), ("gk", 4, F32), ("lb", _m + 32, F32),
                        ("la", _m + 32, F32), ("ex", 192, F32), ("tex", 96, F32), ("red", 33, F32), ("gt", _c, BF),
                        ("ge", _c, BF), ("sg", _c, BF), ("cap", _c, BF), ("pos", _c + 2, BF)):
         SCRATCH["%s%d" % (_n, _i)] = ("sbuf", [128, _w], _d)
@@ -36,6 +36,24 @@ for _i in range(8):
 
 SEMAPHORES = (["cV", "cS", "cP", "cG", "left1", "left2"] + ["arr%d" % _i for _i in range(6)]
               + ["d%02d" % _i for _i in range(40)])
+
+ORDER = [
+    0, 1, 16, 2, 3, 4, 5, 6, 7, 8, 9, 12, 10, 11, 23, 18, 24, 25, 26, 27, 19, 20, 21, 17, 38, 22, 39, 41, 28, 32, 29, 40,
+    30, 43, 31, 42, 35, 44, 54, 34, 55, 56, 45, 47, 57, 49, 48, 58, 46, 67, 59, 68, 60, 61, 62, 50, 13, 69, 74, 72, 36,
+    71, 73, 63, 70, 78, 37, 79, 64, 65, 81, 80, 84, 85, 76, 75, 83, 51, 77, 89, 91, 90, 88, 82, 87, 92, 93, 14, 86, 95,
+    94, 66, 97, 113, 96, 98, 99, 100, 101, 102, 103, 107, 106, 108, 109, 104, 105, 117, 112, 116, 110, 119, 53, 118,
+    120, 122, 124, 121, 111, 123, 127, 128, 125, 33, 129, 126, 132, 130, 131, 133, 136, 52, 134, 135, 137, 138, 139,
+    146, 156, 148, 115, 143, 140, 152, 154, 145, 158, 142, 141, 144, 150, 149, 155, 151, 173, 147, 157, 153, 159, 160,
+    161, 164, 165, 162, 163, 167, 168, 114, 174, 169, 175, 172, 184, 170, 171, 177, 15, 176, 178, 179, 183, 193, 166,
+    185, 189, 217, 186, 194, 195, 191, 190, 205, 204, 207, 196, 201, 209, 187, 192, 188, 199, 200, 210, 211, 206, 197,
+    198, 208, 202, 212, 214, 180, 216, 220, 203, 221, 218, 222, 226, 219, 225, 223, 224, 229, 227, 181, 228, 231, 232,
+    230, 233, 234, 235, 236, 237, 239, 238, 252, 254, 240, 243, 244, 241, 245, 246, 253, 249, 247, 248, 256, 257, 250,
+    242, 259, 260, 255, 258, 261, 182, 251, 213, 264, 263, 262, 215, 265, 269, 266, 271, 267, 283, 272, 284, 270, 285,
+    288, 289, 282, 296, 287, 268, 324, 286, 273, 294, 295, 293, 280, 305, 300, 292, 290, 299, 306, 275, 303, 298, 297,
+    304, 310, 276, 314, 274, 277, 313, 316, 309, 315, 318, 278, 308, 307, 301, 279, 311, 291, 327, 302, 321, 323, 320,
+    317, 322, 330, 329, 325, 281, 331, 312, 328, 326, 336, 337, 333, 339, 332, 334, 338, 347, 340, 319, 342, 335, 344,
+    346, 345, 343, 341, 350, 349, 348, 352, 351, 353, 354, 355, 356, 357, 359, 358, 360, 361, 365, 364, 362, 363, 366,
+    367, 368]
 
 
 def rank_program(g, core, T, topo):
@@ -86,20 +104,28 @@ def rank_program(g, core, T, topo):
         for w, wr in [(w, False) for w in reads] + [(w, True) for w in writes]:
             log.setdefault(w[0], []).append((e, sem, c, ck, cols(w), wr))
 
-    def op(e, call, reads, writes):
-        order(e, reads, writes)
-        sem = "c" + e
-        count[sem] = count.get(sem, 0) + 1
-        call().then_inc(T.sem[sem], 1)
-        note(e, sem, count[sem], reads, writes)
+    todo = []
 
-    def dma(e, out, in_, reads, writes, **how):
-        order(e, reads, writes)
-        sem = "d%02d" % ndma[0]
-        ndma[0] += 1
-        count[sem] = 16
-        Q[e].dma_start(out, in_, **how).then_inc(T.sem[sem], 16)
-        note(e, sem, 16, reads, writes)
+    def op(e, call, reads, writes):
+        def issue():
+            order(e, reads, writes)
+            sem = "c" + e
+            count[sem] = count.get(sem, 0) + 1
+            call().then_inc(T.sem[sem], 1)
+            note(e, sem, count[sem], reads, writes)
+        todo.append((e, issue, reads, writes))
+
+    def dma(e, out, in_, reads, writes, after=None, **how):
+        def issue():
+            if after:
+                wait(e, after, count[after], {})
+            order(e, reads, writes)
+            sem = "d%02d" % ndma[0]
+            ndma[0] += 1
+            count[sem] = 16
+            Q[e].dma_start(out, in_, **how).then_inc(T.sem[sem], 16)
+            note(e, sem, 16, reads, writes)
+        todo.append((e, issue, reads, writes))
 
     def views(*xs):
         return [x for x in xs if isinstance(x, tuple)]
@@ -176,7 +202,7 @@ def rank_program(g, core, T, topo):
     def planes(dst, src, a, n):
         for t in range(4):
             o, i = v(dst, n * t, n * t + n), v(src, a + t, a + 4 * n, 4)
-            op("G", lambda: g.affine_select(ap(o), ap(i), [[0, n]], A.is_ge, 0.0, 0, 0), [i], [o])
+            op("G", lambda o=o, i=i: g.affine_select(ap(o), ap(i), [[0, n]], A.is_ge, 0.0, 0, 0), [i], [o])
 
     def picks(e, n, a, b):
         off = v("offc", a // 16, b // 16)
@@ -195,18 +221,23 @@ def rank_program(g, core, T, topo):
         en = topo.engines(core, T.cores[d])
         rid, pid = topo.addr(T.cores[d])[:2]
         wide = 4 * PC if both else PC
-        order("G", [v("q" + src, a, a + PC), v("s" + src, a, a + wide)], [])
+        reads = [v("q" + src, a, a + PC), v("s" + src, a, a + wide)]
+        lands = [v("q" + dst, b, b + PC), v("s" + dst, b, b + wide)]
         pair = [(codes(src, a, a + PC), codes(dst, b, b + PC)),
                 (ap(v("s" + src, a, a + wide)), ap(v("s" + dst, b, b + wide)))]
         half = len(en) // 2
         use = (en[:half], en[half:]) if both else (en, en)
         trs = [RemoteDMATransfer(dst_ids=[DstId(rid=rid, pnc=pid)], dma_engine_mask=sum(1 << x for x in u),
                                  remote_sem=T.sem[sem], src=i, dst=o) for (i, o), u in zip(pair, use)]
-        for call in ([trs] if both else [trs[:1], trs[1:]]):
-            g.remote_dma_fused(call, local_sem=T.sem[left])
-        for k in (sem, left):
-            count[k] = count.get(k, 0) + len(use[0]) + len(use[1])
-        note("remote", sem, count[sem], [], [v("q" + dst, b, b + PC), v("s" + dst, b, b + wide)])
+
+        def issue():
+            order("G", reads, [])
+            for call in ([trs] if both else [trs[:1], trs[1:]]):
+                g.remote_dma_fused(call, local_sem=T.sem[left])
+            for k in (sem, left):
+                count[k] = count.get(k, 0) + len(use[0]) + len(use[1])
+            note("remote", sem, count[sem], [], lands)
+        todo.append(("G", issue, reads, lands))
 
     steps = sorted(range(1, N), key=lambda j: all(topo.die(T.cores[r]) == topo.die(T.cores[r ^ j]) for r in range(N)))
     dest = [rank ^ j for j in steps] + [rank]
@@ -223,25 +254,38 @@ def rank_program(g, core, T, topo):
         scan(v("so%d" % i, k * slot, k * slot + k), v("cmp%d" % i, n * slot, n * slot + k),
              v("cmp%d" % i, n * slot + k, n * slot + n), float(k), A.add, A.add)
 
-    def threshold(i, n, m, k, cands):
+    def gate(o, i):
+        ts(o, i, 0.5, A.subtract, -BIG, A.mult)
+
+    def threshold(i, n, m, first, cands):
         s, w = str(i), m // 2 + 16
 
-        def spread(block, src, other, init, alu):
+        def spread(block, src, init, alu):
             at = 64 * block + 16
             for h, o in enumerate((v("ex" + s, at + 16 - w, at + 16), v("ex" + s, at + 15 + w, at + 15, -1))):
                 d = v(src + s, h, 2 * w, 2)
-                scan(o, d, other or d, init, alu, alu)
+                scan(o, d, d, init, alu, alu)
 
         def across(block):
             turn(v("tex" + s, 32 * block, 32 * block + 32), v("ex" + s, 64 * block + 16, 64 * block + 48))
 
-        tt(v("lb" + s, 0, m), cands, v("gd" + s, 0, m), A.add)
-        tt(v("la" + s, 0, m), cands, v("gk" + s), A.add)
-        spread(0, "gd", v("zero", 0, w), (k - 0.5) / 32 * BIG, A.add)
-        spread(1, "lb", None, -64 * BIG, A.max)
+        for h in range(2):
+            if first:
+                act(v("junk" + s, 11 * n + 8 * h, 11 * n + 8 * h + 4), v("gd" + s, h, first, 2), F.Sign, 0.0, -1.0,
+                    v("gk" + s, h, h + 1))
+        for h in range(2):
+            act(v("junk" + s, 11 * n + 16 + 8 * h, 11 * n + 16 + 8 * h + (m - first) // 2), v("ks" + s, first + h, m, 2),
+                F.Sign, -0.5, 1.0, v("gk" + s, 2 + h, 3 + h))
+        gate(v("gd" + s, first, m), v("ks" + s, first, m))
+        tt(v("lb" + s, 0, m), cands, v("gd" + s), A.min)
+        tt(v("la" + s, 0, m), cands, v("gd" + s), A.max)
+        for h in range(2):
+            act(v("ex" + s, 16 + 16 * h, 32 + 16 * h), v("two"), F.Identity, v("gk" + s, 2 + h, 3 + h),
+                v("gk" + s, h, h + 1) if first else 0.0)
+        spread(1, "lb", -64 * BIG, A.max)
+        spread(2, "la", 64 * BIG, A.min)
         across(0)
-        act(v("junk" + s, 11 * n, 11 * n + 32), v("tex" + s, 0, 32), F.Identity, 0.0, -1.0, v("red" + s, 32, 33))
-        spread(2, "la", None, 64 * BIG, A.min)
+        act(v("junk" + s, 11 * n + 32, 11 * n + 64), v("tex" + s, 0, 32), F.Identity, BIG / 64, BIG, v("red" + s, 32, 33))
         across(1)
         across(2)
         scan(v("red" + s, 0, 32), v("tex" + s, 32, 64), v("tex" + s, 64, 96), v("red" + s, 32, 33), A.max, A.min)
@@ -250,12 +294,15 @@ def rank_program(g, core, T, topo):
         s = str(i)
         t = v("red" + s, 31, 32)
         ts(v("gt" + s), v("b%d" % bank, 0, n), t, A.is_gt)
-        sign(v("sg" + s), v("b%d" % bank2, 0, n), t)
+        ts(v("ge" + s, 0, cut), v("b%d" % bank, 0, cut), t, A.is_ge)
         if cut < n:
+            sign(v("sg" + s, cut, n), v("b%d" % bank2, cut, n), t)
             act(v("ge" + s, cut, n), v("sg" + s, cut, n), F.Sign, 1.0, -1.0)
         scan(v("cap" + s, n - 2, None, -1), v("zero", 0, n - 1), v("gt" + s, n - 1, 0, -1), float(k), A.add, A.subtract)
-        ts(v("ge" + s, 0, cut), v("sg" + s, 0, cut), 0.0, A.is_le)
         scan(v("pos" + s, 1, n + 1), v("ge" + s), v("cap" + s), 0.0, A.add, A.min)
+
+    def emake(b):
+        quant("e", 128 * b, 128 * b + 128, v("te", 3 - b, 515 - b))
 
     dma("Y", ap(v("tu1")), T.u1[:], [], [v("tu1")])
     dma("Y", ap(v("win", 0, 1024)), T.x[:, 0:1024], [], [v("win", 0, 1024)])
@@ -273,17 +320,18 @@ def rank_program(g, core, T, topo):
     fill(v("zero"), 0.0)
     consts(1, 16)
     consts(2, 12)
+    fill(v("yy", 0, 2 * KB, 2), -2.0 ** 30)
     copy(v("offc"), v("oi"))
     ts(v("pi", 1, 2), v("pi", 0, 1), 15, A.bitwise_and)
     ts(v("pi", 3, 4), v("pi", 0, 1), 3, A.bitwise_and)
     ts(v("pi", 2, 3), v("pi", 1, 2), 2, A.logical_shift_right)
     copy(v("pf", 0, 4), v("pi"))
-    iota(v("m16"), [[16, KB]], 0)
+    iota(v("m16"), [[16, 12]], 0)
     for i in range(N):
         iota(v("m2", 2 * i, 2 * i + 2), [[16, 2]], PC * dest[i])
-    level(v("gd1", 16), 0)
+    level(v("two"), 2)
     NS1 = 5
-    iota(v("cs", 0, NS1), [[32, NS1]], W1 - 256)
+    iota(v("cs", 1, NS1), [[32, NS1 - 1]], W1 - 224)
     level(v("cap1", C - 1), KA)
     level(v("pos1", 0, 1), 0)
     act(v("pf", 4, 5), v("pf", 1, 2), F.Identity, 0.5)
@@ -313,12 +361,9 @@ def rank_program(g, core, T, topo):
     def scount(j, c):
         sign(v("junk1", C * j, C * j + C), v("b%d" % (4 if c % 2 else 2), 0, C), cand(c), v("ks1", c, c + 1))
 
-    def gate1(o, i):
-        ts(o, i, 0.0, A.is_gt, -2 * BIG, A.mult)
-
     def choose(a, b, step, s=1):
         if step == 0:
-            tt(v("srt", a, b, s), v("srt", 32 + a, 32 + b, s), v("gd1", a, b, s), A.add)
+            tt(v("srt", a, b, s), v("srt", 32 + a, 32 + b, s), v("gd1", a, b, s), A.min)
         else:
             tt(v("cd", 8 + a, 8 + b, s), v("srt", a, b, s), v("srt", 24 + a, 24 + b, s), A.max)
 
@@ -342,12 +387,13 @@ def rank_program(g, core, T, topo):
     op("G", lambda: g.affine_select(ap(v("te")), ap(v("one")), [[1, 516]], A.is_equal, 0.0, -3, -4), [v("one")],
        [v("te")])
     planes("xp", "win", 0, C)
-    level(v("gd2", 12), 0)
     level(v("cap2", KA - 1), KB)
+    iota(v("jm"), [[0, KB], [1, 4]], 0)
+    iota(v("yy", 2 * KB + 1, 4 * KB, 2), [[16, KB]], 0)
     level(v("tg", 128, 512), 0)
     iota(v("ramp"), [[1, C]], 0)
-    iota(v("jm"), [[0, KB], [1, 4]], 0)
     level(v("tt", 4 * 104), 0)
+    iota(v("alt"), [[0, KB], [1, 2]], 0)
 
     sort3(0, 0)
     sort3(0, 1)
@@ -362,43 +408,40 @@ def rank_program(g, core, T, topo):
     sort3(1, 1)
     vsum(1, C, 0)
     sort3(1, 2)
-    gate1(v("gd1", 0, 4, 2), v("ks1", 0, 4, 2))
     sort3(1, 3)
     scount(3, 4)
     scount(4, 6)
-    choose(0, 4, 0, 2)
-    vcmp(1, C, 1, 3, cand(5))
-    choose(0, 4, 1, 2)
-    scount(5, 8)
-    scount(6, 10)
-    gate1(v("gd1", 1, 2), v("ks1", 1, 2))
+    scount(5, 5)
+    vcmp(1, C, 1, 3, cand(7))
+    gate(v("gd1", 0, 3), v("ks1", 0, 3))
+    gate(v("gd1", 3, 4), v("so1", KA - 1, KA))
     vsum(1, C, 1)
-    vcmp(1, C, 2, 3, cand(7))
-    gate1(v("gd1", 4, 8, 2), v("ks1", 4, 8, 2))
+    choose(0, 4, 0)
+    choose(0, 4, 1)
+    gate(v("gd1", 7, 8), v("so1", 2 * KA - 1, 2 * KA))
+    vcmp(1, C, 2, 3, cand(9))
+    scount(6, 8)
+    scount(7, 10)
+    gate(v("gd1", 4, 7), v("ks1", 4, 7))
+    choose(4, 8, 0)
     vsum(1, C, 2)
-    choose(4, 8, 0, 2)
-    gate1(v("gd1", 3, 8, 2), v("so1", KA - 1, 3 * KA, KA))
-    choose(4, 8, 1, 2)
-    choose(1, 8, 0, 2)
-    quant("u2", 0, 128, v("tu2"))
-    choose(1, 8, 1, 2)
-    for j, c in enumerate((12, 14, 13, 15)):
-        scount(7 + j, c)
-    ts(v("gk1", 0, 8), v("gd1", 0, 8), 0.0, A.is_equal, BIG, A.mult)
-    vcmp(1, C, 3, 3, cand(9))
-    vcmp(1, C, 4, 3, cand(11))
+    choose(4, 8, 1)
+    vcmp(1, C, 3, 3, cand(11))
+    for j, c in enumerate((12, 14, 15)):
+        scount(8 + j, c)
+    vcmp(1, C, 4, 3, cand(13))
     vsum(1, C, 3)
     vsum(1, C, 4)
+    quant("u2", 0, 128, v("tu2"))
     ts(v("thr2"), v("m2"), KB - 0.5, A.min)
-    copy(v("ks1", 9, 12, 2), v("so1", 4 * KA - 1, 5 * KA, KA))
+    copy(v("ks1", 9, 14, 2), v("so1", 3 * KA - 1, 5 * KA, KA))
+    emake(0)
     picks("S", "2", 0, 256)
     picks("S", "2", 256, 384)
-    ts(v("gd1", 8, 16), v("ks1", 8, 16), 0.0, A.is_gt, -BIG, A.mult)
-    ts(v("gk1", 8, 16), v("ks1", 8, 16), 0.0, A.is_le, BIG, A.mult)
-    threshold(1, C, 16, KA, v("cd"))
-    running(1, C, KA, 6, 7, KA)
+    threshold(1, C, 16, 8, v("cd"))
+    running(1, C, KA, 6, 7, 160)
 
-    for m in range(NS1):
+    for m in list(range(1, NS1)) + [0]:
         sign(v("cj1", W1 * m, W1 * m + W1), v("pos1", 1 + 16 * m, 1 + 16 * m + W1), v("thr", m, m + 1),
              v("ck1", m, m + 1))
     H1 = W1 // 2
@@ -416,11 +459,13 @@ def rank_program(g, core, T, topo):
         cmp1(m)
         tot1(m - 1)
     tot1(11)
-    tt(v("co1", H1 - 1, H1 * NS1, H1), v("ck1", 0, NS1), v("cs", 0, NS1), A.add)
-    ts(v("off1"), v("co1", H1 - 1, 12 * H1, H1), 0.5, A.mult, 128.0, A.add)
+    tt(v("co1", 2 * H1 - 1, H1 * NS1, H1), v("ck1", 1, NS1), v("cs", 1, NS1), A.add)
+    ts(v("off1", 0, 1), v("ck1", 0, 1), 0.5, A.mult, W1 / 2, A.add)
+    ts(v("off1", 1, 12), v("co1", 2 * H1 - 1, 12 * H1, H1), 0.5, A.mult, 128.0, A.add)
 
     for t, e in enumerate("SVSV"):
         gather(e, v("tf", t, 4 * KA, 4), v("xp", C * t, C * t + C), v("off1"))
+    emake(1)
     quant("f", 0, KA, v("tf"))
     for b in range(4):
         mm(b, "w", 128 * b, "f", 0, KA)
@@ -430,8 +475,12 @@ def rank_program(g, core, T, topo):
     picks("V", "2", 0, 256)
     relu("S", v("th", 0, 4 * KA, 4), v("b0", 0, KA))
     relu("S", v("th", 1, 4 * KA, 4), v("b1", 0, KA))
+    scan(v("pa"), v("gate"), v("pos1", 1, C + 1), 0.0, A.add, A.min)
     relu("V", v("th", 2, 4 * KA, 4), v("b2", 0, KA))
     relu("S", v("th", 3, 4 * KA, 4), v("b3", 0, KA))
+    scan(v("pb"), v("gate"), v("pos1", 0, C), 0.0, A.add, A.min)
+    act(v("yy", 1, 2 * KB, 2), v("pa", 3, C, 4), F.Identity, v("pf", 5, 6), FAR + 4)
+    act(v("yy", 2 * KB, 4 * KB, 2), v("pb", 3, C, 4), F.Identity, 0.0, -FAR)
     quant("h", 0, KA, v("th"))
     planes("hp", "th", 0, KA)
     dma("G", ap(fh), ap(v("th")), [v("th"), fh], [fh], accum_op=A.add)
@@ -443,26 +492,20 @@ def rank_program(g, core, T, topo):
 
     turn(v("tr2", 0, 64), v("b4", 0, 64))
     turn(v("tr2", 64, KA), v("b4", 64, KA))
-    for j, c in enumerate((0, 2, 4, 6, 8, 10, 9, 11)):
+    for j, c in enumerate((0, 2, 4, 6, 8, 10, 11)):
         sign(v("junk2", KA * j, KA * j + KA), v("b%d" % (7 if c % 2 else 5), 0, KA), v("tr2", 16 * c, 16 * c + 1),
              v("ks2", c, c + 1))
     mm(0, "p2", 256, "h", 0, KA)
-    mm(1, "p2", 256, "h", 0, KA)
     vcmp(2, KA, 0, 6, v("tr2", 16, 17))
-    for j in range(1, 4):
+    for j in range(1, 5):
         vcmp(2, KA, j, 6, v("tr2", 32 * j + 16, 32 * j + 17))
         vsum(2, KA, j - 1)
-    scan(v("pa"), v("gate"), v("pos1", 1, C + 1), 0.0, A.add, A.min)
-    vsum(2, KA, 3)
-    scan(v("pb"), v("gate"), v("pos1", 0, C), 0.0, A.add, A.min)
-    copy(v("ks2", 1, 8, 2), v("so2", KB - 1, 4 * KB, KB))
-    ya, yc, yd, ye = (v("yy", KB * j, KB * j + KB) for j in range(4))
-    act(ya, v("pa", 3, C, 4), F.Identity, v("pf", 5, 6), FAR + 4)
-    act(yc, v("pb", 3, C, 4), F.Identity, 0.0, FAR)
+    scan(v("yy", 4 * KB), v("yy", 0, 2 * KB), v("yy", 2 * KB, 4 * KB), 0.0, A.add, A.max)
+    vsum(2, KA, 4)
+    ts(v("offx"), v("yy", 4 * KB + 1, 6 * KB, 2), v("pf", 1, 2), A.add)
+    copy(v("ks2", 1, 10, 2), v("so2", KB - 1, 5 * KB, KB))
     gather("S", v("l1"), v("ramp"), v("off1"))
-    ts(v("gd2", 0, 12), v("ks2", 0, 12), 0.0, A.is_gt, -BIG, A.mult)
-    ts(v("gk2", 0, 12), v("ks2", 0, 12), 0.0, A.is_le, BIG, A.mult)
-    threshold(2, KA, 12, KB, v("tr2", 0, KA, 16))
+    threshold(2, KA, 12, 0, v("tr2", 0, KA, 16))
     running(2, KA, KB, 0, 1, KA)
 
     H2 = W2 // 2
@@ -492,13 +535,13 @@ def rank_program(g, core, T, topo):
     def tcol(i):
         return 96 + 32 * i if i else 0
 
-    cmp2(0)
+    scnt2(0)
     cmp2(1)
     for m in (2, 3, 4):
         scnt2(m)
-    tot2(0)
     tot2(1)
-    copy(v("off2", 0, 2), v("co2", H2 - 1, 2 * H2, H2))
+    sout2(0)
+    copy(v("off2", 1, 2), v("co2", 2 * H2 - 1, 2 * H2))
     for t, e in enumerate("SVSV"):
         gather(e, v("tg", t, 128, 4), v("hp", KA * t, KA * t + KA), v("off2", 0, 2))
     quant("a", 0, 128, v("tg", 0, 512))
@@ -518,26 +561,20 @@ def rank_program(g, core, T, topo):
     send(dest[1], "g", 32, "x", C, True, "arr1", "left1")
     send(dest[2], "g", 64, "f", KA, False, "arr2", "left1")
 
-    gather("S", v("olr"), v("l1"), v("off2"))
-    tt(yd, ya, yc, A.subtract)
-    scan(v("old"), v("gate", 0, 128), v("olr"), 0.0, A.add, A.min)
-    tt(ye, yd, v("m16"), A.max)
-    ts(v("offs", 18, 24), v("old", 99, 120, 4), 4.0, A.mult, v("pf", 3, 4), A.add)
-    ts(v("offx"), ye, v("pf", 1, 2), A.add)
-    for i in range(N - 1):
-        ts(v("offs", 6 * i, 6 * i + 6), v("old", 32 * i + 3, 32 * i + PC, 4), 4.0, A.mult, v("pf", 3, 4), A.add)
-    wait("Y", "left1", count["left1"], {})
-    for i in range(N):
-        dma("Y", T.ol[:, PC * dest[i]:PC * dest[i] + PC], T.olr[0:128:16, 32 * i:32 * i + PC], [v("olr")], [])
-
-    def parts(i, j):
-        gather("S", v("fg", KB * i, KB * j), v("win", 0, 4 * C), v("offs", 6 * i, 6 * j))
+    A1, A2 = 128, 208
+    at4 = (0, 10, 16, 24)
 
     def place(e, a, b):
         gather(e, v("tx", 4 * a, 4 * b), v("win"), v("offx", a // 4, b // 4))
 
-    def emake(b):
-        quant("e", 128 * b, 128 * b + 128, v("te", 3 - b, 515 - b))
+    gather("S", v("olr"), v("l1"), v("off2"))
+    place("S", 0, A1)
+    place("V", A2, A2 + 64)
+    scan(v("old"), v("gate", 0, 128), v("olr"), 0.0, A.add, A.min)
+    place("V", A2 + 64, C)
+    ts(v("offs"), v("old", 3, 128, 4), 4.0, A.mult, v("pf", 3, 4), A.add)
+    for i in range(N):
+        dma("Y", T.ol[:, PC * dest[i]:PC * dest[i] + PC], T.olr[0:128:16, 32 * i:32 * i + PC], [v("olr")], [], "left1")
 
     def through(banks, src, a, at, to, n):
         for b in range(4):
@@ -550,71 +587,76 @@ def rank_program(g, core, T, topo):
         for b in range(4):
             mm(banks[b], "e", 128 * b, src, a, 128)
 
-    def up(banks, at, i, via=None):
-        run = (KB * i, KB * i + KB)
-        if via is None:
-            for b in range(4):
-                tt(v("hs", KB * i + b, KB * i + KB, 4), v("b%d" % banks[b], at, at + PC),
-                   v("tg", 4 * tcol(i) + b, 4 * (tcol(i) + PC), 4), A.add)
-        else:
-            for b in range(4):
-                copy(v("dd", via + b, via + 4 * PC, 4), v("b%d" % banks[b], at, at + PC), "S")
-            tt(v("hs", *run), v("dd", via, via + 4 * PC), v("tg", 4 * tcol(i), 4 * (tcol(i) + PC)), A.add)
+    def parts(i, n):
+        gather("S", v("hs", 32 * at4[i] + 1, 32 * at4[i] + 2 * KB * n, 2), v("win", 0, 4 * C),
+               v("offs", at4[i], at4[i] + 6 * n))
+
+    def up(banks, at, i, bs=range(4)):
+        for b in bs:
+            tt(v("hs", 32 * at4[i] + 2 * b, 32 * at4[i] + 2 * KB, 8), v("b%d" % banks[b], at, at + PC),
+               v("tg", 4 * tcol(i) + b, 4 * (tcol(i) + PC), 4), A.add)
 
     def up2(i):
-        run = (KB * i, KB * i + KB)
-        tt(v("nw", *run), v("hs", *run), v("fg", *run), A.add)
+        run = (32 * at4[i], 32 * at4[i] + 2 * KB)
+        scan(v("nw", *run), v("alt"), v("hs", *run), 0.0, A.mult, A.add)
 
-    def put(i, j):
-        scatter(v("tx"), v("offs", 6 * i, 6 * j), v("nw", KB * i, KB * j))
+    def put(i):
+        scatter(v("tx"), v("offs", at4[i], at4[i] + 6), v("nw", 32 * at4[i] + 1, 32 * at4[i] + 2 * KB, 2))
 
     lo4, hi4 = (0, 1, 2, 3), (4, 5, 6, 7)
-    place("S", 0, 96)
-    place("V", 288, C)
-    place("S", 96, 192)
-    parts(3, 4)
-    emake(0)
-    emake(1)
+    parts(3, 1)
+    emake(2)
+    ts(v("offs", 10, 16), v("old", 35, 56, 4), 4.0, A.mult, v("pf", 3, 4), A.add)
     through(hi4, "g", PC, 72, 2 * PC, "t1")
     send(dest[0], "t1", 32, "h", KA, True, "arr3", "left2")
-    emake(2)
+    emake(3)
     through(lo4, "x", C + PC - 128, 104, PC, "t2")
     send(dest[1], "t2", 0, "a", 128, True, "arr4", "left2")
-    emake(3)
     through(hi4, "f", KA + PC - 128, 104, 0, "t3")
     send(dest[2], "t3", 0, "f", KA + PC, True, "arr5", "left2")
 
     unpack(lo4, "t1", 0)
-    place("S", 192, 288)
+    place("S", A1, A2)
     parts(0, 1)
-    parts(1, 3)
+    parts(1, 2)
     up(lo4, 0, 3)
     quant("v", 0, 128, v("tv"))
     up2(3)
-    put(3, 4)
+    put(3)
     unpack(hi4, "h", KA + PC - 128)
-    up(hi4, 104, 0, 0)
+    up(hi4, 104, 0)
     up2(0)
-    put(0, 1)
     unpack(lo4, "a", PC)
-    up(lo4, 104, 1, 128)
+    up(lo4, 104, 1, (0,))
+    put(0)
+    up(lo4, 104, 1, (1, 2, 3))
     unpack(hi4, "f", KA + 2 * PC - 128)
-    up(hi4, 104, 2)
+    up(hi4, 104, 2, (0,))
     up2(1)
+    up(hi4, 104, 2, (1, 2, 3))
+    put(1)
     up2(2)
-    put(1, 3)
+    put(2)
 
     quant("y", 0, 256, v("tx", 0, 1024))
     mm(0, "v", 0, "y", 0, 256)
     quant("y", 256, C, v("tx", 1024))
     mm(1, "v", 0, "y", 256, 128)
     dma("Y", T.oc[:], codes("y", 0, C), [v("qy")], [])
-    for k in range(4):
-        dma("Y", T.osc[4 * k:4 * k + 4, :], T.sy[32 * k:32 * k + 4, :], [v("sy")], [])
+
+    def scales(e, k):
+        dma(e, T.osc[4 * k:4 * k + 4, :], T.sy[32 * k:32 * k + 4, :], [v("sy")], [])
+
+    scales("Y", 0)
+    scales("Y", 1)
     copy(v("yb", 0, 256), v("b0", 0, 256), "S")
     copy(v("yb", 256, C), v("b1", 0, 128), "V")
     dma("Y", T.y[:], ap(v("yb")), [v("yb")], [])
+    scales("S", 2)
+    scales("S", 3)
 
+    for i in ORDER or range(len(todo)):
+        todo[i][1]()
     for sem in SEMAPHORES:
         if seen.get(sem, 0) < count.get(sem, 0):
             g.wait_ge(T.sem[sem], count[sem])

@@ -9,8 +9,8 @@ X4, U8, BF, F32, I32, U16 = "float8_e4m3fn_x4", "uint8", "bfloat16", "float32", 
 
 SCRATCH = {}
 for _n, _w in (("x", C + 4 * PC), ("h", KA + 4 * PC), ("f", KA + 5 * PC), ("a", 128 + 4 * PC), ("g", 128 + 4 * PC),
-               ("t1", 128), ("t2", 128), ("t3", 128), ("u1", 128), ("u2", 128), ("p1", 384), ("p2", 384), ("v", 128),
-               ("e", 512), ("w", 512), ("z", 512), ("y", C)):
+               ("h0", 128), ("t1", 128), ("t2", 128), ("t3", 128), ("u1", 128), ("u2", 128), ("p1", 384), ("p2", 384),
+               ("v", 128), ("e", 512), ("w", 512), ("z", 512), ("y", C)):
     SCRATCH["q" + _n] = ("sbuf", [128, _w], X4)
     SCRATCH["s" + _n] = ("sbuf", [128, _w], U8)
 for _n, _w, _d in (
@@ -18,10 +18,10 @@ for _n, _w, _d in (
         ("tv", 512, BF), ("tf", 4 * KA, BF), ("th", 4 * KA, BF), ("tg", 4 * 224, BF), ("tt", 4 * 176, BF),
         ("te", 516, BF), ("one", 516, BF), ("zero", C, BF), ("hs", 1024, BF), ("alt", 2 * KB, BF),
         ("nw", 1024, BF), ("tx", 4 * C, BF), ("yb", C, F32),
-        ("oi", 24, I32), ("offc", 24, U16), ("pi", 4, I32), ("pf", 8, F32), ("m16", 12, F32), ("thr", 12, F32),
-        ("cs", 6, F32), ("ramp", C, F32), ("jm", C, BF), ("gate", C, BF), ("m2", 8, F32), ("thr2", 8, F32),
-        ("l1", KA, F32), ("olr", 128, F32), ("old", 128, F32), ("offs", 32, U16), ("pa", C, BF), ("pb", C, BF),
-        ("yy", 6 * KB, F32), ("offx", KB, U16), ("srt", 40, F32), ("two", 16, F32), ("cd", 16, F32),
+        ("oi", 24, I32), ("offc", 24, U16), ("pi", 4, I32), ("pf", 8, F32), ("m16", 12, F32), ("thr", 18, F32),
+        ("ramp", C, F32), ("jm", C, BF), ("gate", C, BF), ("m2", 8, F32), ("thr2", 8, F32),
+        ("l1", KA, F32), ("olr", 128, F32), ("old", 128, F32), ("offs", 32, U16), ("pa", 2 * C, BF),
+        ("yy", 6 * KB, F32), ("offx", KB, U16), ("srt", 48, F32), ("two", 16, F32), ("cd", 32, F32),
         ("cj1", 6 * W1, BF), ("cc1", 12 * W1, BF), ("co1", 6 * W1, BF), ("ck1", 6, F32), ("off1", 12, U16),
         ("cc2", 8 * W2, BF), ("co2", 4 * W2, F32), ("ck2", 8, F32), ("off2", 8, U16)):
     SCRATCH[_n] = ("sbuf", [128, _w], _d)
@@ -38,22 +38,22 @@ SEMAPHORES = (["cV", "cS", "cP", "cG", "left1", "left2"] + ["arr%d" % _i for _i 
               + ["d%02d" % _i for _i in range(40)])
 
 ORDER = [
-    0, 1, 16, 2, 3, 4, 5, 6, 7, 8, 9, 12, 10, 11, 23, 18, 24, 25, 26, 27, 19, 20, 21, 17, 38, 22, 39, 41, 28, 32, 29, 40,
-    30, 43, 31, 42, 35, 44, 54, 34, 55, 56, 45, 47, 57, 49, 48, 58, 46, 67, 59, 68, 60, 61, 62, 50, 13, 69, 74, 72, 36,
-    71, 73, 63, 70, 78, 37, 79, 64, 65, 81, 80, 84, 85, 76, 75, 83, 51, 77, 89, 91, 90, 88, 82, 87, 92, 93, 14, 86, 95,
-    94, 66, 97, 113, 96, 98, 99, 100, 101, 102, 103, 107, 106, 108, 109, 104, 105, 117, 112, 116, 110, 119, 53, 118,
-    120, 122, 124, 121, 111, 123, 127, 128, 125, 33, 129, 126, 132, 130, 131, 133, 136, 52, 134, 135, 137, 138, 139,
-    146, 156, 148, 115, 143, 140, 152, 154, 145, 158, 142, 141, 144, 150, 149, 155, 151, 173, 147, 157, 153, 159, 160,
-    161, 164, 165, 162, 163, 167, 168, 114, 174, 169, 175, 172, 184, 170, 171, 177, 15, 176, 178, 179, 183, 193, 166,
-    185, 189, 217, 186, 194, 195, 191, 190, 205, 204, 207, 196, 201, 209, 187, 192, 188, 199, 200, 210, 211, 206, 197,
-    198, 208, 202, 212, 214, 180, 216, 220, 203, 221, 218, 222, 226, 219, 225, 223, 224, 229, 227, 181, 228, 231, 232,
-    230, 233, 234, 235, 236, 237, 239, 238, 252, 254, 240, 243, 244, 241, 245, 246, 253, 249, 247, 248, 256, 257, 250,
-    242, 259, 260, 255, 258, 261, 182, 251, 213, 264, 263, 262, 215, 265, 269, 266, 271, 267, 283, 272, 284, 270, 285,
-    288, 289, 282, 296, 287, 268, 324, 286, 273, 294, 295, 293, 280, 305, 300, 292, 290, 299, 306, 275, 303, 298, 297,
-    304, 310, 276, 314, 274, 277, 313, 316, 309, 315, 318, 278, 308, 307, 301, 279, 311, 291, 327, 302, 321, 323, 320,
-    317, 322, 330, 329, 325, 281, 331, 312, 328, 326, 336, 337, 333, 339, 332, 334, 338, 347, 340, 319, 342, 335, 344,
-    346, 345, 343, 341, 350, 349, 348, 352, 351, 353, 354, 355, 356, 357, 359, 358, 360, 361, 365, 364, 362, 363, 366,
-    367, 368]
+    0, 1, 2, 3, 13, 4, 15, 5, 6, 7, 8, 9, 10, 11, 19, 16, 20, 21, 12, 18, 17, 38, 23, 22, 14, 40, 24, 44, 25, 26, 27, 28,
+    43, 39, 45, 41, 29, 42, 30, 31, 56, 46, 57, 47, 49, 58, 48, 69, 52, 50, 59, 70, 51, 121, 76, 53, 71, 34, 72, 77, 75,
+    60, 79, 73, 80, 81, 78, 83, 61, 93, 92, 62, 74, 55, 82, 63, 89, 64, 65, 84, 85, 90, 88, 100, 86, 101, 66, 91, 87, 67,
+    94, 102, 96, 68, 99, 103, 120, 105, 95, 106, 108, 54, 104, 113, 97, 117, 112, 109, 116, 110, 98, 115, 111, 107, 119,
+    114, 118, 131, 126, 132, 133, 134, 127, 128, 129, 136, 135, 130, 140, 32, 137, 142, 141, 138, 139, 33, 143, 144,
+    145, 146, 123, 147, 148, 150, 35, 149, 152, 151, 187, 153, 168, 162, 155, 156, 157, 159, 154, 160, 170, 158, 165,
+    164, 166, 171, 163, 161, 167, 172, 125, 169, 173, 174, 175, 177, 176, 179, 178, 194, 181, 186, 208, 188, 182, 183,
+    185, 37, 124, 189, 190, 193, 200, 196, 184, 192, 180, 197, 201, 199, 198, 202, 232, 205, 206, 191, 210, 209, 211,
+    215, 220, 203, 213, 204, 212, 214, 223, 221, 225, 207, 218, 227, 224, 217, 222, 216, 219, 228, 226, 230, 233, 122,
+    234, 239, 243, 242, 238, 236, 240, 241, 237, 235, 248, 36, 244, 246, 247, 245, 250, 251, 249, 252, 253, 254, 255,
+    195, 256, 257, 258, 229, 259, 260, 275, 263, 274, 262, 278, 265, 261, 266, 277, 264, 279, 270, 273, 269, 268, 267,
+    280, 281, 276, 284, 282, 271, 283, 272, 285, 231, 286, 293, 289, 299, 298, 301, 337, 292, 287, 300, 291, 294, 296,
+    290, 311, 310, 344, 309, 302, 303, 288, 305, 304, 308, 314, 306, 312, 319, 315, 313, 307, 316, 320, 317, 324, 321,
+    323, 297, 322, 335, 325, 334, 333, 342, 326, 336, 295, 318, 341, 347, 350, 327, 340, 343, 345, 349, 346, 348, 354,
+    351, 328, 339, 357, 353, 352, 358, 329, 356, 362, 338, 330, 359, 355, 365, 366, 367, 363, 360, 368, 364, 361, 370,
+    371, 369, 331, 332, 372, 373, 374, 375, 376, 377, 379, 378, 381, 382, 383, 384, 380, 385, 386, 387, 388]
 
 
 def rank_program(g, core, T, topo):
@@ -66,7 +66,7 @@ def rank_program(g, core, T, topo):
     count = {}
     seen = {}
     log = {}
-    ndma = [0]
+    ndma, last = [0], [None]
 
     def ap(w):
         n, a, b, s = w
@@ -123,6 +123,8 @@ def rank_program(g, core, T, topo):
             sem = "d%02d" % ndma[0]
             ndma[0] += 1
             count[sem] = 16
+            if writes == [] and reads == [v("yb")]:
+                last[0] = sem
             Q[e].dma_start(out, in_, **how).then_inc(T.sem[sem], 16)
             note(e, sem, 16, reads, writes)
         todo.append((e, issue, reads, writes))
@@ -247,17 +249,21 @@ def rank_program(g, core, T, topo):
         fill(v("la%d" % i, m), 64 * BIG)
 
     def vcmp(i, n, slot, bank, thr):
-        ts(v("cmp%d" % i, n * slot, n * slot + n), v("b%d" % bank, 0, n), thr, A.is_gt, -1.0, A.mult)
+        ts(v("cmp%d" % i, n * slot, n * slot + n), v("b%d" % bank, 0, n), thr, A.is_gt, BIG, A.mult)
+
+    def vcmp1(slot, c):
+        for h, bank in enumerate((1, 3)):
+            ts(v("cmp1", C * slot + KA * h, C * slot + KA * h + KA), v("b%d" % bank, 0, KA), cand(c), A.is_gt, BIG, A.mult)
 
     def vsum(i, n, slot):
         k = n // 2
         scan(v("so%d" % i, k * slot, k * slot + k), v("cmp%d" % i, n * slot, n * slot + k),
-             v("cmp%d" % i, n * slot + k, n * slot + n), float(k), A.add, A.add)
+             v("cmp%d" % i, n * slot + k, n * slot + n), (0.5 - k) * BIG, A.add, A.add)
 
     def gate(o, i):
         ts(o, i, 0.5, A.subtract, -BIG, A.mult)
 
-    def threshold(i, n, m, first, cands):
+    def threshold(i, n, m, cands, terms, weight):
         s, w = str(i), m // 2 + 16
 
         def spread(block, src, init, alu):
@@ -269,19 +275,16 @@ def rank_program(g, core, T, topo):
         def across(block):
             turn(v("tex" + s, 32 * block, 32 * block + 32), v("ex" + s, 64 * block + 16, 64 * block + 48))
 
+        for j, (w_, signed) in enumerate(terms):
+            if w_:
+                act(v("junk" + s, 11 * n + 8 * j, 11 * n + 8 * j + len(cols(w_))), w_, F.Sign, 0.0 if signed else -0.5,
+                    -1.0 if signed else 1.0, v("gk" + s, j, j + 1))
+        for a, b, step, c_, d_ in cands:
+            tt(v("lb" + s, a, b, step), c_, d_, A.min)
+            tt(v("la" + s, a, b, step), c_, d_, A.max)
         for h in range(2):
-            if first:
-                act(v("junk" + s, 11 * n + 8 * h, 11 * n + 8 * h + 4), v("gd" + s, h, first, 2), F.Sign, 0.0, -1.0,
-                    v("gk" + s, h, h + 1))
-        for h in range(2):
-            act(v("junk" + s, 11 * n + 16 + 8 * h, 11 * n + 16 + 8 * h + (m - first) // 2), v("ks" + s, first + h, m, 2),
-                F.Sign, -0.5, 1.0, v("gk" + s, 2 + h, 3 + h))
-        gate(v("gd" + s, first, m), v("ks" + s, first, m))
-        tt(v("lb" + s, 0, m), cands, v("gd" + s), A.min)
-        tt(v("la" + s, 0, m), cands, v("gd" + s), A.max)
-        for h in range(2):
-            act(v("ex" + s, 16 + 16 * h, 32 + 16 * h), v("two"), F.Identity, v("gk" + s, 2 + h, 3 + h),
-                v("gk" + s, h, h + 1) if first else 0.0)
+            act(v("ex" + s, 16 + 16 * h, 32 + 16 * h), weight, F.Identity, v("gk" + s, 2 + h, 3 + h),
+                v("gk" + s, h, h + 1) if terms[h][0] else 0.0)
         spread(1, "lb", -64 * BIG, A.max)
         spread(2, "la", 64 * BIG, A.min)
         across(0)
@@ -305,8 +308,8 @@ def rank_program(g, core, T, topo):
         quant("e", 128 * b, 128 * b + 128, v("te", 3 - b, 515 - b))
 
     dma("Y", ap(v("tu1")), T.u1[:], [], [v("tu1")])
-    dma("Y", ap(v("win", 0, 1024)), T.x[:, 0:1024], [], [v("win", 0, 1024)])
-    dma("Y", ap(v("win", 1024, 1536)), T.x[:, 1024:1536], [], [v("win", 1024, 1536)])
+    dma("Y", ap(v("win", 0, 768)), T.x[:, 0:768], [], [v("win", 0, 768)])
+    dma("Y", ap(v("win", 768, 1536)), T.x[:, 768:1536], [], [v("win", 768, 1536)])
     dma("Y", ap(v("tu2")), T.u2[:], [], [v("tu2")])
     dma("Y", codes("w", 0, 512), T.wc[:], [], [v("qw")])
     dma("Y", ap(v("sw")), T.ws[:], [], [v("sw")])
@@ -331,55 +334,51 @@ def rank_program(g, core, T, topo):
         iota(v("m2", 2 * i, 2 * i + 2), [[16, 2]], PC * dest[i])
     level(v("two"), 2)
     NS1 = 5
-    iota(v("cs", 1, NS1), [[32, NS1 - 1]], W1 - 224)
+    iota(v("thr", 13, 12 + NS1), [[32, NS1 - 1]], W1 - 224)
     level(v("cap1", C - 1), KA)
     level(v("pos1", 0, 1), 0)
     act(v("pf", 4, 5), v("pf", 1, 2), F.Identity, 0.5)
-    act(v("thr"), v("m16", 0, 12), F.Identity, v("pf", 4, 5))
+    act(v("thr", 0, 12), v("m16", 0, 12), F.Identity, v("pf", 4, 5))
     act(v("pf", 6, 7), v("pf", 1, 2), F.Identity, 4.0 * C - 4 - FAR, -1.0)
     act(v("pf", 7, 8), v("pf", 2, 3), F.Identity, FAR, FAR)
     act(v("pf", 5, 6), v("pf", 3, 4), F.Identity, v("pf", 6, 7))
     act(v("m2"), v("m2"), F.Identity, v("pf", 4, 5))
 
     def cand(c):
-        return v("cd", c, c + 1)
+        return v("cd", 2 * c + 1, 2 * c + 2)
 
     def sort3(h, step):
         ca, cb, cc = (v("tr1", 192 * h + 64 * j, 192 * h + 64 * j + 64, 16) for j in range(3))
-        mn, mx, z, lo, hi = (v("srt", 8 * j + 4 * h, 8 * j + 4 * h + 4) for j in range(5))
+        at = 192 * h + 128
+        d0, d1 = (v("tr1", at + j, at + 64, 8) for j in range(2))
+        mn, mx = (v("tr1", at + 8 + j, at + 64, 16) for j in range(2))
         if step == 0:
             tt(mx, ca, cb, A.max)
             tt(mn, ca, cb, A.min)
         elif step == 1:
-            tt(z, mx, cc, A.min)
-            tt(lo, mn, cc, A.min)
-        elif step == 2:
-            tt(v("cd", 4 * h, 4 + 4 * h), mn, z, A.max)
+            scan(v("cd", 8 * h, 8 * h + 8), d0, d1, 0.0, A.max, A.min)
         else:
-            tt(hi, mx, cc, A.max)
+            tt(v("srt", 32 + 4 * h, 36 + 4 * h), mn, cc, A.min)
+            tt(v("srt", 40 + 4 * h, 44 + 4 * h), mx, cc, A.max)
 
     def scount(j, c):
         sign(v("junk1", C * j, C * j + C), v("b%d" % (4 if c % 2 else 2), 0, C), cand(c), v("ks1", c, c + 1))
 
-    def choose(a, b, step, s=1):
-        if step == 0:
-            tt(v("srt", a, b, s), v("srt", 32 + a, 32 + b, s), v("gd1", a, b, s), A.min)
-        else:
-            tt(v("cd", 8 + a, 8 + b, s), v("srt", a, b, s), v("srt", 24 + a, 24 + b, s), A.max)
+    def choose(c, d=None):
+        ts(cand(8 + c), d or v("gd1", c, c + 1), v("srt", 40 + c, 41 + c), A.min, v("srt", 32 + c, 33 + c), A.max)
 
     quant("u1", 0, 128, v("tu1"))
-    picks("V", "1", 0, 384)
-    picks("S", "1", 0, 384)
-    quant("x", 0, 128, v("win", 0, 512))
-    mm(0, "u1", 0, "x", 0, 128)
-    quant("x", 128, 256, v("win", 512, 1024))
-    mm(1, "u1", 0, "x", 128, 128)
-    turn(v("tr1", 0, 128), v("b0", 0, 128))
-    turn(v("tr1", 128, 192), v("b1", 0, 64))
-    quant("x", 256, 384, v("win", 1024, 1536))
+    for a, b in ((256, 384), (128, 256), (0, 128)):
+        picks("V", "1", a, b)
+        picks("S", "1", a, b)
+    quant("x", 0, KA, v("win", 0, 768))
+    mm(0, "p1", 256, "x", 0, KA)
+    mm(1, "p1", 128, "x", 0, KA)
+    turn(v("tr1", 0, KA), v("b0", 0, KA))
+    quant("x", KA, C, v("win", 768, 1536))
     mm(2, "p1", 0, "x", 0, C)
-    mm(5, "u1", 0, "x", 256, 128)
-    mm(3, "p1", 128, "x", 0, C)
+    mm(3, "p1", 128, "x", KA, KA)
+    mm(5, "p1", 256, "x", KA, KA)
     mm(4, "p1", 128, "x", 0, C)
     mm(6, "p1", 256, "x", 0, C)
     mm(7, "p1", 256, "x", 0, C)
@@ -397,48 +396,53 @@ def rank_program(g, core, T, topo):
 
     sort3(0, 0)
     sort3(0, 1)
+    scount(0, 0)
+    scount(1, 2)
+    scount(2, 1)
     sort3(0, 2)
-    turn(v("tr1", 192, 256), v("b1", 64, 128))
-    turn(v("tr1", 256, 384), v("b5", 0, 128))
-    sort3(0, 3)
-    for j, c in enumerate((0, 2, 1)):
-        scount(j, c)
+    turn(v("tr1", KA, C), v("b5", 0, KA))
+    vcmp1(0, 3)
     sort3(1, 0)
-    vcmp(1, C, 0, 3, cand(3))
-    sort3(1, 1)
     vsum(1, C, 0)
+    sort3(1, 1)
+    gate(v("gd1", 0, 4, 2), v("ks1", 0, 4, 2))
+    choose(3, v("so1", KA - 1, KA))
+    choose(0)
+    choose(2)
+    gate(v("gd1", 1, 2), v("ks1", 1, 2))
+    vcmp1(1, 5)
+    choose(1)
     sort3(1, 2)
-    sort3(1, 3)
-    scount(3, 4)
-    scount(4, 6)
-    scount(5, 5)
-    vcmp(1, C, 1, 3, cand(7))
-    gate(v("gd1", 0, 3), v("ks1", 0, 3))
-    gate(v("gd1", 3, 4), v("so1", KA - 1, KA))
+    for j, c in enumerate((7, 4, 6, 8, 10)):
+        scount(3 + j, c)
+    vcmp1(3, 11)
     vsum(1, C, 1)
-    choose(0, 4, 0)
-    choose(0, 4, 1)
-    gate(v("gd1", 7, 8), v("so1", 2 * KA - 1, 2 * KA))
-    vcmp(1, C, 2, 3, cand(9))
-    scount(6, 8)
-    scount(7, 10)
-    gate(v("gd1", 4, 7), v("ks1", 4, 7))
-    choose(4, 8, 0)
-    vsum(1, C, 2)
-    choose(4, 8, 1)
-    vcmp(1, C, 3, 3, cand(11))
-    for j, c in enumerate((12, 14, 15)):
-        scount(8 + j, c)
-    vcmp(1, C, 4, 3, cand(13))
+    gate(v("gd1", 7, 8), v("ks1", 7, 8))
+    vcmp1(2, 9)
+    choose(5, v("so1", 2 * KA - 1, 2 * KA))
+    choose(7)
     vsum(1, C, 3)
+    gate(v("gd1", 4, 8, 2), v("ks1", 4, 8, 2))
+    vcmp1(4, 13)
+    vsum(1, C, 2)
+    choose(4)
+    choose(6)
+    scount(9, 12)
+    scount(10, 14)
+    vcmp1(5, 15)
     vsum(1, C, 4)
+    vsum(1, C, 5)
+    copy(v("gd1", 3, 6, 2), v("so1", KA - 1, 2 * KA, KA))
     quant("u2", 0, 128, v("tu2"))
     ts(v("thr2"), v("m2"), KB - 0.5, A.min)
-    copy(v("ks1", 9, 14, 2), v("so1", 3 * KA - 1, 5 * KA, KA))
     emake(0)
     picks("S", "2", 0, 256)
     picks("S", "2", 256, 384)
-    threshold(1, C, 16, 8, v("cd"))
+    gate(v("gd1", 8, 16, 2), v("ks1", 8, 16, 2))
+    late = v("so1", 3 * KA - 1, 6 * KA, KA)
+    threshold(1, C, 16, [(0, 8, 1, v("cd", 1, 16, 2), v("gd1", 0, 8)), (9, 16, 2, v("cd", 19, 32, 4), late),
+                         (8, 16, 2, v("cd", 17, 32, 4), v("gd1", 8, 16, 2))],
+              [(v("gd1", 0, 8, 2), True), (v("gd1", 1, 8, 2), True), (v("ks1", 8, 16, 2), False), (late, True)], v("two"))
     running(1, C, KA, 6, 7, 160)
 
     for m in list(range(1, NS1)) + [0]:
@@ -459,7 +463,7 @@ def rank_program(g, core, T, topo):
         cmp1(m)
         tot1(m - 1)
     tot1(11)
-    tt(v("co1", 2 * H1 - 1, H1 * NS1, H1), v("ck1", 1, NS1), v("cs", 1, NS1), A.add)
+    tt(v("co1", 2 * H1 - 1, H1 * NS1, H1), v("ck1", 1, NS1), v("thr", 13, 12 + NS1), A.add)
     ts(v("off1", 0, 1), v("ck1", 0, 1), 0.5, A.mult, W1 / 2, A.add)
     ts(v("off1", 1, 12), v("co1", 2 * H1 - 1, 12 * H1, H1), 0.5, A.mult, 128.0, A.add)
 
@@ -475,27 +479,29 @@ def rank_program(g, core, T, topo):
     picks("V", "2", 0, 256)
     relu("S", v("th", 0, 4 * KA, 4), v("b0", 0, KA))
     relu("S", v("th", 1, 4 * KA, 4), v("b1", 0, KA))
-    scan(v("pa"), v("gate"), v("pos1", 1, C + 1), 0.0, A.add, A.min)
+    scan(v("pa", 0, C), v("gate"), v("pos1", 1, C + 1), 0.0, A.add, A.min)
     relu("V", v("th", 2, 4 * KA, 4), v("b2", 0, KA))
     relu("S", v("th", 3, 4 * KA, 4), v("b3", 0, KA))
-    scan(v("pb"), v("gate"), v("pos1", 0, C), 0.0, A.add, A.min)
+    scan(v("pa", C, 2 * C), v("gate"), v("pos1", 0, C), 0.0, A.add, A.min)
     act(v("yy", 1, 2 * KB, 2), v("pa", 3, C, 4), F.Identity, v("pf", 5, 6), FAR + 4)
-    act(v("yy", 2 * KB, 4 * KB, 2), v("pb", 3, C, 4), F.Identity, 0.0, -FAR)
+    act(v("yy", 2 * KB, 4 * KB, 2), v("pa", C + 3, 2 * C, 4), F.Identity, 0.0, -FAR)
+    quant("h0", 0, 128, v("th", 0, 512))
+    mm(4, "u2", 0, "h0", 0, 128)
     quant("h", 0, KA, v("th"))
     planes("hp", "th", 0, KA)
     dma("G", ap(fh), ap(v("th")), [v("th"), fh], [fh], accum_op=A.add)
-    mm(4, "u2", 0, "h", 0, KA)
     mm(5, "p2", 0, "h", 0, KA)
     mm(6, "p2", 128, "h", 0, KA)
     mm(7, "p2", 128, "h", 0, KA)
     picks("V", "2", 256, 384)
 
     turn(v("tr2", 0, 64), v("b4", 0, 64))
-    turn(v("tr2", 64, KA), v("b4", 64, KA))
+    turn(v("tr2", 64, 128), v("b4", 64, 128))
+    mm(0, "p2", 256, "h", 0, KA)
+    turn(v("tr2", 128, KA), v("b0", 128, KA))
     for j, c in enumerate((0, 2, 4, 6, 8, 10, 11)):
         sign(v("junk2", KA * j, KA * j + KA), v("b%d" % (7 if c % 2 else 5), 0, KA), v("tr2", 16 * c, 16 * c + 1),
              v("ks2", c, c + 1))
-    mm(0, "p2", 256, "h", 0, KA)
     vcmp(2, KA, 0, 6, v("tr2", 16, 17))
     for j in range(1, 5):
         vcmp(2, KA, j, 6, v("tr2", 32 * j + 16, 32 * j + 17))
@@ -503,9 +509,13 @@ def rank_program(g, core, T, topo):
     scan(v("yy", 4 * KB), v("yy", 0, 2 * KB), v("yy", 2 * KB, 4 * KB), 0.0, A.add, A.max)
     vsum(2, KA, 4)
     ts(v("offx"), v("yy", 4 * KB + 1, 6 * KB, 2), v("pf", 1, 2), A.add)
-    copy(v("ks2", 1, 10, 2), v("so2", KB - 1, 5 * KB, KB))
     gather("S", v("l1"), v("ramp"), v("off1"))
-    threshold(2, KA, 12, 0, v("tr2", 0, KA, 16))
+    gate(v("gd2", 0, 12, 2), v("ks2", 0, 12, 2))
+    gate(v("gd2", 11, 12), v("ks2", 11, 12))
+    late = v("so2", KB - 1, 5 * KB, KB)
+    threshold(2, KA, 12, [(1, 10, 2, v("tr2", 16, 160, 32), late), (11, 12, 1, v("tr2", 176, 177), v("gd2", 11, 12)),
+                          (0, 12, 2, v("tr2", 0, KA, 32), v("gd2", 0, 12, 2))],
+              [(None, True), (v("ks2", 11, 12), False), (v("ks2", 0, 12, 2), False), (late, True)], v("one", 0, 16))
     running(2, KA, KB, 0, 1, KA)
 
     H2 = W2 // 2
@@ -535,26 +545,25 @@ def rank_program(g, core, T, topo):
     def tcol(i):
         return 96 + 32 * i if i else 0
 
-    scnt2(0)
-    cmp2(1)
-    for m in (2, 3, 4):
+    for m in (0, 1, 2, 3):
         scnt2(m)
-    tot2(1)
+    cmp2(5)
+    tot2(5)
     sout2(0)
-    copy(v("off2", 1, 2), v("co2", 2 * H2 - 1, 2 * H2))
+    sout2(1)
     for t, e in enumerate("SVSV"):
         gather(e, v("tg", t, 128, 4), v("hp", KA * t, KA * t + KA), v("off2", 0, 2))
     quant("a", 0, 128, v("tg", 0, 512))
     send(dest[0], "a", 0, "g", 128, True, "arr0", "left1")
-    scnt2(5)
+    scnt2(4)
     cmp2(6)
     cmp2(7)
     sout2(2)
     tot2(6)
     tot2(7)
-    for m in (3, 4, 5):
+    for m in (3, 4):
         sout2(m)
-    copy(v("off2", 6, 8), v("co2", 7 * H2 - 1, 8 * H2, H2))
+    copy(v("off2", 5, 8), v("co2", 6 * H2 - 1, 8 * H2, H2))
     for t, e in enumerate("SVSV"):
         gather(e, v("tg", 512 + t, 896, 4), v("hp", KA * t, KA * t + KA), v("off2", 2, 8))
     quant("g", 0, 128, v("tg", 384, 896))
@@ -573,8 +582,6 @@ def rank_program(g, core, T, topo):
     scan(v("old"), v("gate", 0, 128), v("olr"), 0.0, A.add, A.min)
     place("V", A2 + 64, C)
     ts(v("offs"), v("old", 3, 128, 4), 4.0, A.mult, v("pf", 3, 4), A.add)
-    for i in range(N):
-        dma("Y", T.ol[:, PC * dest[i]:PC * dest[i] + PC], T.olr[0:128:16, 32 * i:32 * i + PC], [v("olr")], [], "left1")
 
     def through(banks, src, a, at, to, n):
         for b in range(4):
@@ -614,6 +621,8 @@ def rank_program(g, core, T, topo):
     send(dest[1], "t2", 0, "a", 128, True, "arr4", "left2")
     through(hi4, "f", KA + PC - 128, 104, 0, "t3")
     send(dest[2], "t3", 0, "f", KA + PC, True, "arr5", "left2")
+    for i in range(N):
+        dma("Y", T.ol[:, PC * dest[i]:PC * dest[i] + PC], T.olr[0:128:16, 32 * i:32 * i + PC], [v("olr")], [], "left2")
 
     unpack(lo4, "t1", 0)
     place("S", A1, A2)
@@ -657,6 +666,6 @@ def rank_program(g, core, T, topo):
 
     for i in ORDER or range(len(todo)):
         todo[i][1]()
-    for sem in SEMAPHORES:
+    for sem in sorted(SEMAPHORES, key=lambda x: x == last[0]):
         if seen.get(sem, 0) < count.get(sem, 0):
             g.wait_ge(T.sem[sem], count[sem])

@@ -1,5 +1,5 @@
 from concourse.bass import DstId, RemoteDMATransfer
-from concourse.mybir import dt, AluOpType as A, AxisListType, ActivationFunctionType as F
+from concourse.mybir import dt, AluOpType as A, ActivationFunctionType as F
 
 C, KA, KB, PC = 384, 192, 96, 24
 BIG = 2.0 ** 90
@@ -8,52 +8,41 @@ FAR = 4096.0
 X4, U8, BF, F32, I32, U16 = "float8_e4m3fn_x4", "uint8", "bfloat16", "float32", "int32", "uint16"
 
 SCRATCH = {}
-for _n, _w in (("x", C + 4 * PC), ("h", KA + 4 * PC), ("f", KA + 5 * PC), ("a", 128 + 4 * PC), ("g", 128 + 4 * PC),
-               ("h0", 128), ("t1", 128), ("t2", 128), ("t3", 128), ("u1", 128), ("u2", 128), ("p1", 384), ("p2", 384),
-               ("v", 128), ("e", 512), ("w", 512), ("z", 512), ("y", C)):
+for _n, _w in (("x", C + 4 * PC), ("h", KA + 4 * PC), ("f", 128 + 5 * PC), ("a", 128 + 4 * PC), ("g", 128 + 4 * PC),
+               ("f2", 128), ("h0", 128), ("t1", 128), ("t2", 128), ("t3", 128), ("u1", 128), ("u2", 128), ("p1", 384),
+               ("p2", 384), ("v", 128), ("e", 512), ("w", 512), ("z", 512), ("y", C)):
     SCRATCH["q" + _n] = ("sbuf", [128, _w], X4)
     SCRATCH["s" + _n] = ("sbuf", [128, _w], U8)
 for _n, _w, _d in (
         ("win", 4 * (C + KA), BF), ("xp", 4 * C, BF), ("hp", 4 * KA, BF), ("tu1", 512, BF), ("tu2", 512, BF),
         ("tv", 512, BF), ("tf", 4 * KA, BF), ("th", 4 * KA, BF), ("tg", 4 * 224, BF), ("tt", 4 * 176, BF),
-        ("te", 516, BF), ("one", 516, BF), ("zero", C, BF), ("hs", 1024, BF), ("alt", 2 * KB, BF),
-        ("nw", 1024, BF), ("tx", 4 * C, BF), ("yb", C, F32),
-        ("oi", 24, I32), ("offc", 24, U16), ("pi", 4, I32), ("pf", 8, F32), ("m16", 12, F32), ("thr", 18, F32),
-        ("ramp", C, F32), ("jm", C, BF), ("gate", C, BF), ("m2", 8, F32), ("thr2", 8, F32),
-        ("l1", KA, F32), ("olr", 128, F32), ("old", 128, F32), ("offs", 32, U16), ("pa", 2 * C, BF),
-        ("yy", 6 * KB, F32), ("offx", KB, U16), ("srt", 48, F32), ("two", 16, F32), ("cd", 32, F32),
-        ("cj1", 6 * W1, BF), ("cc1", 12 * W1, BF), ("co1", 6 * W1, BF), ("ck1", 6, F32), ("off1", 12, U16),
-        ("cc2", 8 * W2, BF), ("co2", 4 * W2, F32), ("ck2", 8, F32), ("off2", 8, U16)):
+        ("te", 516, BF), ("one", 516, BF), ("zero", C, BF), ("hs", 1024, BF), ("alt", C, BF), ("nw", 1024, BF),
+        ("tx", 4 * C, BF), ("yb", C, F32), ("oi", 24, I32), ("offc", 24, U16), ("pi", 4, I32), ("ramp", C, F32),
+        ("jm", C, BF), ("gate", C, BF), ("l1", KA, F32), ("olr", 128, F32), ("old", 128, F32), ("offs", 32, U16),
+        ("pa", 2 * C, BF), ("yy", 6 * KB, F32), ("offx", KB, U16), ("ps", C, BF), ("cj1", 5 * 256, BF),
+        ("cc1", 12 * W1, BF), ("co1", 6 * W1, BF), ("off1", 12, U16), ("c2", 4 * 130, BF), ("s2", 4 * 65, BF),
+        ("cc2", 8 * W2, BF), ("off2", 8, U16)):
     SCRATCH[_n] = ("sbuf", [128, _w], _d)
-for _i, _c, _k, _m in ((1, C, KA, 16), (2, KA, KB, 12)):
-    for _n, _w, _d in (("tr", _c, F32), ("ks", 16, F32), ("junk", 12 * _c, BF), ("cmp", 7 * _c, BF),
-                       ("so", 7 * _k, BF), ("gd", _m, F32), ("gk", 4, F32), ("lb", _m + 32, F32),
-                       ("la", _m + 32, F32), ("ex", 192, F32), ("tex", 96, F32), ("red", 33, F32), ("gt", _c, BF),
+for _i, _c, _k in ((1, C, KA), (2, KA, KB)):
+    for _n, _w, _d in (("tr", _c, F32), ("junk", 12 * _c, BF), ("cmp", 8 * _c, BF), ("so", 8 * _k, BF), ("gt", _c, BF),
                        ("ge", _c, BF), ("sg", _c, BF), ("cap", _c, BF), ("pos", _c + 2, BF)):
         SCRATCH["%s%d" % (_n, _i)] = ("sbuf", [128, _w], _d)
+PART, _at = {}, 0
+for _n, _w in (("cl", 256), ("lb1", 48), ("b1l", 40), ("lb2", 40), ("ch", 256), ("la1", 40), ("b1h", 40), ("la2", 48),
+               ("pf", 12), ("thr", 60), ("m32", 60), ("m2", 8), ("thr2", 8), ("two", 32), ("cd", 16), ("ck1", 12),
+               ("u3", 256), ("r3", 256), ("e1", 320), ("t1", 256), ("jj", 2), ("g2", 4), ("co2", 4 * W2), ("ck2", 8),
+               ("ks1", 16), ("gk1", 4), ("red1", 65), ("ks2", 6), ("gd2", 6), ("gk2", 1), ("ex2", 320), ("tex2", 192),
+               ("red2", 65)):
+    PART[_n] = (_at, _w)
+    _at += -(-_w // 8) * 8
+SCRATCH["sel"] = ("sbuf", [128, _at], F32)
 for _i in range(8):
     SCRATCH["b%d" % _i] = ("psum", [128, 512], F32)
 
 SEMAPHORES = (["cV", "cS", "cP", "cG", "left1", "left2"] + ["arr%d" % _i for _i in range(6)]
               + ["d%02d" % _i for _i in range(40)])
 
-ORDER = [
-    0, 1, 2, 3, 13, 4, 15, 5, 6, 7, 8, 9, 10, 11, 19, 16, 20, 21, 12, 18, 17, 38, 23, 22, 14, 40, 24, 44, 25, 26, 27, 28,
-    43, 39, 45, 41, 29, 42, 30, 31, 56, 46, 57, 47, 49, 58, 48, 69, 52, 50, 59, 70, 51, 121, 76, 53, 71, 34, 72, 77, 75,
-    60, 79, 73, 80, 81, 78, 83, 61, 93, 92, 62, 74, 55, 82, 63, 89, 64, 65, 84, 85, 90, 88, 100, 86, 101, 66, 91, 87, 67,
-    94, 102, 96, 68, 99, 103, 120, 105, 95, 106, 108, 54, 104, 113, 97, 117, 112, 109, 116, 110, 98, 115, 111, 107, 119,
-    114, 118, 131, 126, 132, 133, 134, 127, 128, 129, 136, 135, 130, 140, 32, 137, 142, 141, 138, 139, 33, 143, 144,
-    145, 146, 123, 147, 148, 150, 35, 149, 152, 151, 187, 153, 168, 162, 155, 156, 157, 159, 154, 160, 170, 158, 165,
-    164, 166, 171, 163, 161, 167, 172, 125, 169, 173, 174, 175, 177, 176, 179, 178, 194, 181, 186, 208, 188, 182, 183,
-    185, 37, 124, 189, 190, 193, 200, 196, 184, 192, 180, 197, 201, 199, 198, 202, 232, 205, 206, 191, 210, 209, 211,
-    215, 220, 203, 213, 204, 212, 214, 223, 221, 225, 207, 218, 227, 224, 217, 222, 216, 219, 228, 226, 230, 233, 122,
-    234, 239, 243, 242, 238, 236, 240, 241, 237, 235, 248, 36, 244, 246, 247, 245, 250, 251, 249, 252, 253, 254, 255,
-    195, 256, 257, 258, 229, 259, 260, 275, 263, 274, 262, 278, 265, 261, 266, 277, 264, 279, 270, 273, 269, 268, 267,
-    280, 281, 276, 284, 282, 271, 283, 272, 285, 231, 286, 293, 289, 299, 298, 301, 337, 292, 287, 300, 291, 294, 296,
-    290, 311, 310, 344, 309, 302, 303, 288, 305, 304, 308, 314, 306, 312, 319, 315, 313, 307, 316, 320, 317, 324, 321,
-    323, 297, 322, 335, 325, 334, 333, 342, 326, 336, 295, 318, 341, 347, 350, 327, 340, 343, 345, 349, 346, 348, 354,
-    351, 328, 339, 357, 353, 352, 358, 329, 356, 362, 338, 330, 359, 355, 365, 366, 367, 363, 360, 368, 364, 361, 370,
-    371, 369, 331, 332, 372, 373, 374, 375, 376, 377, 379, 378, 381, 382, 383, 384, 380, 385, 386, 387, 388]
+ORDER = [0,12,1,2,11,32,75,10,9,3,4,5,6,7,25,26,27,15,28,24,51,16,14,47,41,40,43,17,42,48,49,53,29,35,34,30,37,33,36,39,31,38,77,80,78,74,81,76,8,52,58,56,59,62,61,54,65,46,45,23,22,55,57,44,13,50,63,82,83,87,84,60,64,67,66,68,93,94,86,120,89,88,98,90,85,95,110,96,97,113,99,92,91,102,100,103,107,106,104,111,112,108,116,128,126,130,129,131,105,101,109,115,114,71,72,136,117,118,139,119,135,132,144,146,145,134,133,143,151,138,149,147,153,152,148,150,154,140,137,155,156,19,20,121,159,161,160,157,158,164,162,163,165,141,142,167,122,127,166,219,222,168,171,172,376,169,170,173,174,73,69,79,70,124,125,21,177,176,175,183,185,191,187,193,195,189,186,184,188,196,192,194,190,197,178,179,180,181,182,18,201,199,220,198,200,202,206,204,208,212,213,211,210,205,203,218,223,209,233,221,231,226,228,214,216,217,215,269,229,224,225,230,235,234,232,227,236,239,240,238,237,244,267,248,245,207,246,340,255,241,253,252,247,256,258,254,265,242,249,259,262,261,250,264,260,263,266,270,257,271,251,282,243,279,274,273,272,275,284,283,277,280,276,278,286,281,285,287,123,288,289,290,291,328,292,268,301,293,305,303,294,302,299,306,304,297,295,296,300,308,309,311,310,307,298,312,321,317,315,314,316,324,369,326,318,329,322,323,325,313,319,320,332,333,330,331,336,344,337,341,334,343,335,370,342,348,354,345,353,347,338,352,346,351,327,358,357,349,368,356,355,365,371,366,339,367,375,372,373,350,374,359,377,378,360,380,379,382,381,384,388,383,391,386,389,385,390,392,387,396,397,362,394,361,395,398,363,364,400,393,399,402,401,404,403,405,406,407,408,411,409,413,412,410,414,415,419,417,416,418,420,423,422,421]
 
 
 def rank_program(g, core, T, topo):
@@ -73,6 +62,9 @@ def rank_program(g, core, T, topo):
         return T[n][:, a:b] if s == 1 else T[n][:, a:b:s]
 
     def v(n, a=0, b=None, s=1):
+        if n in PART:
+            at, w = PART[n]
+            return ("sel", at + a, at + (w if b is None else min(b, w)), s)
         return (n, a, SCRATCH[n][1][1] if b is None and s > 0 else b, s)
 
     def cols(w):
@@ -137,12 +129,12 @@ def rank_program(g, core, T, topo):
 
     V, S = g.vector, g.scalar
 
-    def fill(w, c):
-        op("V", lambda: V.memset(ap(w), c), [], [w])
-
     def act(o, i, f, bias=0.0, scale=1.0, acc=None):
         op("S", lambda: S.activation(ap(o), ap(i), f, bias=val(bias), scale=val(scale), accum_out=val(acc)),
            views(i, bias, scale), views(o, acc))
+
+    def fill(w, c):
+        act(w, v("zero", 0, len(cols(w))), F.Identity, c)
 
     def copy(o, i, e="V"):
         if e == "V":
@@ -176,6 +168,9 @@ def rank_program(g, core, T, topo):
 
     def sign(o, row, thr, acc=None):
         act(o, row, F.Sign, thr, -1.0, acc)
+
+    def gate(o, i):
+        act(o, i, F.Identity, BIG / 2, -BIG)
 
     def relu(e, o, i):
         if e == "V":
@@ -244,65 +239,20 @@ def rank_program(g, core, T, topo):
     steps = sorted(range(1, N), key=lambda j: all(topo.die(T.cores[r]) == topo.die(T.cores[r ^ j]) for r in range(N)))
     dest = [rank ^ j for j in steps] + [rank]
 
-    def consts(i, m):
-        fill(v("lb%d" % i, m), -64 * BIG)
-        fill(v("la%d" % i, m), 64 * BIG)
-
-    def vcmp(i, n, slot, bank, thr):
-        ts(v("cmp%d" % i, n * slot, n * slot + n), v("b%d" % bank, 0, n), thr, A.is_gt, BIG, A.mult)
-
-    def vcmp1(slot, c):
-        for h, bank in enumerate((1, 3)):
-            ts(v("cmp1", C * slot + KA * h, C * slot + KA * h + KA), v("b%d" % bank, 0, KA), cand(c), A.is_gt, BIG, A.mult)
-
     def vsum(i, n, slot):
         k = n // 2
         scan(v("so%d" % i, k * slot, k * slot + k), v("cmp%d" % i, n * slot, n * slot + k),
              v("cmp%d" % i, n * slot + k, n * slot + n), (0.5 - k) * BIG, A.add, A.add)
 
-    def gate(o, i):
-        ts(o, i, 0.5, A.subtract, -BIG, A.mult)
-
-    def threshold(i, n, m, cands, terms, weight):
-        s, w = str(i), m // 2 + 16
-
-        def spread(block, src, init, alu):
-            at = 64 * block + 16
-            for h, o in enumerate((v("ex" + s, at + 16 - w, at + 16), v("ex" + s, at + 15 + w, at + 15, -1))):
-                d = v(src + s, h, 2 * w, 2)
-                scan(o, d, d, init, alu, alu)
-
-        def across(block):
-            turn(v("tex" + s, 32 * block, 32 * block + 32), v("ex" + s, 64 * block + 16, 64 * block + 48))
-
-        for j, (w_, signed) in enumerate(terms):
-            if w_:
-                act(v("junk" + s, 11 * n + 8 * j, 11 * n + 8 * j + len(cols(w_))), w_, F.Sign, 0.0 if signed else -0.5,
-                    -1.0 if signed else 1.0, v("gk" + s, j, j + 1))
-        for a, b, step, c_, d_ in cands:
-            tt(v("lb" + s, a, b, step), c_, d_, A.min)
-            tt(v("la" + s, a, b, step), c_, d_, A.max)
-        for h in range(2):
-            act(v("ex" + s, 16 + 16 * h, 32 + 16 * h), weight, F.Identity, v("gk" + s, 2 + h, 3 + h),
-                v("gk" + s, h, h + 1) if terms[h][0] else 0.0)
-        spread(1, "lb", -64 * BIG, A.max)
-        spread(2, "la", 64 * BIG, A.min)
-        across(0)
-        act(v("junk" + s, 11 * n + 32, 11 * n + 64), v("tex" + s, 0, 32), F.Identity, BIG / 64, BIG, v("red" + s, 32, 33))
-        across(1)
-        across(2)
-        scan(v("red" + s, 0, 32), v("tex" + s, 32, 64), v("tex" + s, 64, 96), v("red" + s, 32, 33), A.max, A.min)
-
-    def running(i, n, k, bank, bank2, cut):
+    def running(i, n, k, t, bank, bank2, cut):
         s = str(i)
-        t = v("red" + s, 31, 32)
         ts(v("gt" + s), v("b%d" % bank, 0, n), t, A.is_gt)
         ts(v("ge" + s, 0, cut), v("b%d" % bank, 0, cut), t, A.is_ge)
         if cut < n:
             sign(v("sg" + s, cut, n), v("b%d" % bank2, cut, n), t)
             act(v("ge" + s, cut, n), v("sg" + s, cut, n), F.Sign, 1.0, -1.0)
-        scan(v("cap" + s, n - 2, None, -1), v("zero", 0, n - 1), v("gt" + s, n - 1, 0, -1), float(k), A.add, A.subtract)
-        scan(v("pos" + s, 1, n + 1), v("ge" + s), v("cap" + s), 0.0, A.add, A.min)
+        scan(v("cap" + s, n - 2, None, -1), v("zero", 0, n - 1), v("gt" + s, n - 1, 0, -1), float(KB), A.add, A.subtract)
+        scan(v("pos" + s, 1, n + 1), v("ge" + s), v("cap" + s), float(KB - k), A.add, A.min)
 
     def emake(b):
         quant("e", 128 * b, 128 * b + 128, v("te", 3 - b, 515 - b))
@@ -320,52 +270,64 @@ def rank_program(g, core, T, topo):
     iota(v("oi", 0, 16), [[16, 2], [32, 4], [0, 2]], 0)
     iota(v("oi", 16, 24), [[16, 8]], 0)
     iota(v("pi", 0, 1), [[0, 1]], 0, 1)
-    fill(v("zero"), 0.0)
-    consts(1, 16)
-    consts(2, 12)
+    op("V", lambda: V.memset(ap(v("zero")), 0.0), [], [v("zero")])
+    fill(("sel", 0, 384, 1), -64 * BIG)
+    fill(("sel", 384, 768, 1), 64 * BIG)
+    fill(v("e1", 64, 112), -64 * BIG)
+    fill(v("c2", 0, 520, 130), -128 * BIG)
+    fill(v("c2", 129, 520, 130), 0.0)
+    fill(v("ex2", 208, 224), 1.0)
+    fill(v("ex2", 240, 256), 0.0)
+    fill(v("ex2", 272, 288), -64 * BIG)
+    fill(v("ex2", 304, 320), 64 * BIG)
+    fill(v("ex2", 96, 144), -64 * BIG)
     fill(v("yy", 0, 2 * KB, 2), -2.0 ** 30)
     copy(v("offc"), v("oi"))
     ts(v("pi", 1, 2), v("pi", 0, 1), 15, A.bitwise_and)
     ts(v("pi", 3, 4), v("pi", 0, 1), 3, A.bitwise_and)
     ts(v("pi", 2, 3), v("pi", 1, 2), 2, A.logical_shift_right)
     copy(v("pf", 0, 4), v("pi"))
-    iota(v("m16"), [[16, 12]], 0)
     for i in range(N):
         iota(v("m2", 2 * i, 2 * i + 2), [[16, 2]], PC * dest[i])
     level(v("two"), 2)
-    NS1 = 5
-    iota(v("thr", 13, 12 + NS1), [[32, NS1 - 1]], W1 - 224)
-    level(v("cap1", C - 1), KA)
-    level(v("pos1", 0, 1), 0)
-    act(v("pf", 4, 5), v("pf", 1, 2), F.Identity, 0.5)
-    act(v("thr", 0, 12), v("m16", 0, 12), F.Identity, v("pf", 4, 5))
-    act(v("pf", 6, 7), v("pf", 1, 2), F.Identity, 4.0 * C - 4 - FAR, -1.0)
+    iota(v("m32", 0, 12), [[32, 12]], 1 - KA)
+    iota(v("m32", 12, 36), [[2, 2], [32, 12]], -KA)
+    iota(v("m32", 36, 48), [[-16 - 16 * W1, 12]], KA + W1 // 2 * (KA - 2))
+    iota(v("m32", 48, 60), [[16, 12]], 0)
+    level(v("cap1", C - 1), KB)
+    level(v("pos1", 0, 1), -KB)
+    act(v("pf", 4, 5), v("pf", 1, 2), F.Identity, 0.5 - KB)
+    act(v("pf", 8, 9), v("pf", 1, 2), F.Identity, 0.0, 2.0)
+    act(v("pf", 9, 10), v("pf", 1, 2), F.Identity, 0.0, -float(W1))
+    act(v("pf", 10, 11), v("pf", 1, 2), F.Identity, 0.5)
+    act(v("thr", 0, 36), v("m32", 0, 36), F.Identity, v("pf", 8, 9))
+    act(v("thr", 36, 48), v("m32", 36, 48), F.Identity, v("pf", 9, 10))
+    act(v("thr", 48, 60), v("m32", 48, 60), F.Identity, v("pf", 4, 5))
+    act(v("pf", 6, 7), v("pf", 1, 2), F.Identity, 4.0 * C - 4 - FAR + 4 * KB, -1.0)
     act(v("pf", 7, 8), v("pf", 2, 3), F.Identity, FAR, FAR)
     act(v("pf", 5, 6), v("pf", 3, 4), F.Identity, v("pf", 6, 7))
-    act(v("m2"), v("m2"), F.Identity, v("pf", 4, 5))
+    act(v("m2"), v("m2"), F.Identity, v("pf", 10, 11))
 
     def cand(c):
         return v("cd", 2 * c + 1, 2 * c + 2)
 
-    def sort3(h, step):
+    def sort3(h):
         ca, cb, cc = (v("tr1", 192 * h + 64 * j, 192 * h + 64 * j + 64, 16) for j in range(3))
         at = 192 * h + 128
         d0, d1 = (v("tr1", at + j, at + 64, 8) for j in range(2))
         mn, mx = (v("tr1", at + 8 + j, at + 64, 16) for j in range(2))
-        if step == 0:
-            tt(mx, ca, cb, A.max)
-            tt(mn, ca, cb, A.min)
-        elif step == 1:
-            scan(v("cd", 8 * h, 8 * h + 8), d0, d1, 0.0, A.max, A.min)
-        else:
-            tt(v("srt", 32 + 4 * h, 36 + 4 * h), mn, cc, A.min)
-            tt(v("srt", 40 + 4 * h, 44 + 4 * h), mx, cc, A.max)
+        tt(mx, ca, cb, A.max)
+        tt(mn, ca, cb, A.min)
+        scan(v("cd", 8 * h, 8 * h + 8), d0, d1, 0.0, A.max, A.min)
+        tt(v("cl", 4 * h, 4 * h + 4), mn, cc, A.min)
+        tt(v("ch", 4 * h, 4 * h + 4), mx, cc, A.max)
 
-    def scount(j, c):
-        sign(v("junk1", C * j, C * j + C), v("b%d" % (4 if c % 2 else 2), 0, C), cand(c), v("ks1", c, c + 1))
+    def g1(a, b, st=1):
+        return v("so1", KA * a + KA - 1, KA * b, KA * st)
 
-    def choose(c, d=None):
-        ts(cand(8 + c), d or v("gd1", c, c + 1), v("srt", 40 + c, 41 + c), A.min, v("srt", 32 + c, 33 + c), A.max)
+    def choose(c):
+        b = 128 * (c % 2) + 32 * (c // 2)
+        scan(v("u3", b, b + 32), v("cl", c, 256, 8), v("ch", c, 256, 8), g1(c, c + 1), A.max, A.min)
 
     quant("u1", 0, 128, v("tu1"))
     for a, b in ((256, 384), (128, 256), (0, 128)):
@@ -392,183 +354,199 @@ def rank_program(g, core, T, topo):
     level(v("tg", 128, 512), 0)
     iota(v("ramp"), [[1, C]], 0)
     level(v("tt", 4 * 104), 0)
-    iota(v("alt"), [[0, KB], [1, 2]], 0)
+    iota(v("alt"), [[0, KA], [1, 2]], 0)
 
-    sort3(0, 0)
-    sort3(0, 1)
-    scount(0, 0)
-    scount(1, 2)
-    scount(2, 1)
-    sort3(0, 2)
+    sort3(0)
     turn(v("tr1", KA, C), v("b5", 0, KA))
-    vcmp1(0, 3)
-    sort3(1, 0)
-    vsum(1, C, 0)
-    sort3(1, 1)
-    gate(v("gd1", 0, 4, 2), v("ks1", 0, 4, 2))
-    choose(3, v("so1", KA - 1, KA))
-    choose(0)
-    choose(2)
-    gate(v("gd1", 1, 2), v("ks1", 1, 2))
-    vcmp1(1, 5)
-    choose(1)
-    sort3(1, 2)
-    for j, c in enumerate((7, 4, 6, 8, 10)):
-        scount(3 + j, c)
-    vcmp1(3, 11)
-    vsum(1, C, 1)
-    gate(v("gd1", 7, 8), v("ks1", 7, 8))
-    vcmp1(2, 9)
-    choose(5, v("so1", 2 * KA - 1, 2 * KA))
-    choose(7)
-    vsum(1, C, 3)
-    gate(v("gd1", 4, 8, 2), v("ks1", 4, 8, 2))
-    vcmp1(4, 13)
-    vsum(1, C, 2)
-    choose(4)
-    choose(6)
-    scount(9, 12)
-    scount(10, 14)
-    vcmp1(5, 15)
-    vsum(1, C, 4)
-    vsum(1, C, 5)
-    copy(v("gd1", 3, 6, 2), v("so1", KA - 1, 2 * KA, KA))
+    sort3(1)
+    for j, c in enumerate((0, 2, 4, 6, 1)):
+        sign(v("junk1", C * j, C * j + C), v("b%d" % (4 if c % 2 else 2), 0, C), cand(c), v("ks1", c, c + 1))
+    for c in (3, 5, 7):
+        for h, bank in enumerate((1, 3)):
+            ts(v("cmp1", C * c + KA * h, C * c + KA * h + KA), v("b%d" % bank, 0, KA), cand(c), A.is_gt, BIG, A.mult)
+        vsum(1, C, c)
+        choose(c)
+    for cs in ((0, 2), (4, 6), (1,)):
+        gate(g1(cs[0], cs[-1] + 1, len(cs)), v("ks1", cs[0], cs[-1] + 1, len(cs)))
+        for c in cs:
+            choose(c)
+    for a in range(0, 256, 128):
+        turn(v("r3", a, a + 128), v("u3", a, a + 128))
     quant("u2", 0, 128, v("tu2"))
-    ts(v("thr2"), v("m2"), KB - 0.5, A.min)
+    act(v("thr2"), v("m2"), F.Relu, KB - 0.5, -1.0)
+    act(v("thr2"), v("thr2"), F.Identity, KB - 0.5, -1.0)
     emake(0)
-    picks("S", "2", 0, 256)
-    picks("S", "2", 256, 384)
-    gate(v("gd1", 8, 16, 2), v("ks1", 8, 16, 2))
-    late = v("so1", 3 * KA - 1, 6 * KA, KA)
-    threshold(1, C, 16, [(0, 8, 1, v("cd", 1, 16, 2), v("gd1", 0, 8)), (9, 16, 2, v("cd", 19, 32, 4), late),
-                         (8, 16, 2, v("cd", 17, 32, 4), v("gd1", 8, 16, 2))],
-              [(v("gd1", 0, 8, 2), True), (v("gd1", 1, 8, 2), True), (v("ks1", 8, 16, 2), False), (late, True)], v("two"))
-    running(1, C, KA, 6, 7, 160)
+    cuts = ((0, 128), (128, 256), (256, 320), (320, 384))
+    for a, b in cuts:
+        picks("S", "2", a, b)
+    JK = 11 * C
+    for h in range(2):
+        act(v("junk1", JK + 8 * h, JK + 8 * h + 4), g1(h, 8, 2), F.Sign, 0.0, 1.0, v("gk1", h, h + 1))
+        act(v("e1", 256 + 32 * h, 288 + 32 * h), v("two"), F.Identity, 0.0, v("gk1", h, h + 1))
+    turn(v("t1", 192, 256), v("e1", 256, 320))
+    for h in range(2):
+        act(v("junk1", JK + 32 + 32 * h, JK + 64 + 32 * h), v("t1", 192 + 32 * h, 224 + 32 * h), F.Identity, BIG / 64,
+            -BIG, v("jj", h, h + 1))
+    tt(v("b1l", 0, 8), v("cd", 1, 16, 2), g1(0, 8), A.min)
+    tt(v("b1h", 0, 8), v("cd", 1, 16, 2), g1(0, 8), A.max)
 
-    for m in list(range(1, NS1)) + [0]:
-        sign(v("cj1", W1 * m, W1 * m + W1), v("pos1", 1 + 16 * m, 1 + 16 * m + W1), v("thr", m, m + 1),
+    def spread(at, ins, init, alu):
+        for d, o in zip(ins, (v("e1", at - 3, at + 16), v("e1", at + 34, at + 15, -1))):
+            scan(o, d, d, init, alu, alu)
+
+    spread(160, [v("b1l", h, 38, 2) for h in range(2)], -64 * BIG, A.max)
+    spread(208, [v("b1h", h, 38, 2) for h in range(2)], 64 * BIG, A.min)
+    turn(v("t1", 32, 64), v("e1", 160, 192))
+    turn(v("t1", 160, 192), v("e1", 208, 240))
+
+    for b in range(4):
+        sign(v("junk1", C * 7 + 128 * b, C * 7 + 128 * b + 128), v("r3", 0, 128), v("u3", 32 * b, 32 * b + 1),
+             v("ks1", 8 + b, 9 + b))
+    for j in range(4):
+        ts(v("c2", 130 * j + 1, 130 * j + 129), v("r3", 128, 256), v("u3", 128 + 32 * j, 129 + 32 * j), A.is_gt,
+           2 * BIG, A.mult)
+        scan(v("s2", 65 * j, 65 * j + 65), v("c2", 130 * j, 130 * j + 65), v("c2", 130 * j + 65, 130 * j + 130),
+             v("jj", 1, 2), A.add, A.add)
+    act(v("g2"), v("ks1", 8, 12), F.Identity, v("jj", 0, 1), -BIG)
+    act(v("junk1", JK + 16, JK + 20), v("ks1", 8, 12), F.Sign, v("jj", 0, 1), -BIG, v("gk1", 2, 3))
+    tt(v("lb1", 16, 20), v("u3", 0, 128, 32), v("g2"), A.min)
+    tt(v("la1", 16, 20), v("u3", 0, 128, 32), v("g2"), A.max)
+    act(v("e1", 0, 16), v("two", 0, 16), F.Identity, v("gk1", 2, 3), v("gk1", 0, 1))
+    tt(v("la1", 20, 24), v("u3", 128, 256, 32), v("s2", 64, 260, 65), A.max)
+    act(v("e1", 16, 32), v("two", 0, 16), F.Identity, -257.0 / 64, v("gk1", 1, 2))
+    spread(48, [v("lb1", 19, 0, -1)], -64 * BIG, A.max)
+    spread(112, [v("la1", 19, 0, -1), v("la1", 20, 39)], 64 * BIG, A.min)
+    turn(v("t1", 0, 32), v("e1", 0, 32))
+    act(v("junk1", JK + 96, JK + 128), v("t1", 0, 32), F.Identity, BIG / 64, -BIG, v("red1", 64, 65))
+    turn(v("t1", 64, 160), v("e1", 48, 144))
+    scan(v("red1", 0, 64), v("t1", 95, 31, -1), v("t1", 128, 192), v("red1", 64, 65), A.max, A.min)
+    running(1, C, KA, v("red1", 63, 64), 6, 7, 160)
+
+    H1, Q1 = W1 // 2, W1 // 4
+    SR, SP, VR, VP = (0, 1), (2, 3, 4), (5, 6), (7, 8, 9, 10, 11)
+    scan(v("ps"), v("alt"), v("pos1", 1, C + 1), 0.0, A.mult, A.add)
+    WR = W1 + 16 * (len(SR) - 1)
+    for m in SR:
+        sign(v("cj1", 256 * m, 256 * m + WR), v("pos1", 1, 1 + WR), v("thr", 48 + m, 49 + m), v("ck1", m, m + 1))
+    ts(v("off1", SR[0], SR[-1] + 1), v("ck1", SR[0], SR[-1] + 1), 0.5, A.mult, WR / 2, A.add)
+    WU = H1 + 8 * (len(SP) - 1)
+    for m in SP:
+        sign(v("cj1", 256 * m, 256 * m + WU), v("ps", 16 * SP[0] + 1, 16 * SP[0] + 2 * WU, 2), v("thr", m, m + 1),
              v("ck1", m, m + 1))
-    H1 = W1 // 2
-
-    def cmp1(m):
-        ts(v("cc1", W1 * m, W1 * m + W1), v("pos1", 1 + 16 * m, 1 + 16 * m + W1), v("thr", m, m + 1), A.is_le,
-           2.0, A.mult)
-
-    def tot1(m):
+    ts(v("off1", SP[0], SP[-1] + 1), v("ck1", SP[0], SP[-1] + 1), float(WU + 16 * SP[0]), A.add)
+    for m in VR:
+        ts(v("cc1", W1 * m, W1 * m + W1), v("pos1", 1 + 16 * m, 1 + 16 * m + W1), v("thr", 48 + m, 49 + m), A.is_le,
+           -1.0, A.mult)
         scan(v("co1", H1 * m, H1 * m + H1), v("cc1", W1 * m, W1 * m + H1), v("cc1", W1 * m + H1, W1 * m + W1),
-             float(32 * m - 256), A.add, A.add)
-
-    cmp1(NS1)
-    for m in range(NS1 + 1, 12):
-        cmp1(m)
-        tot1(m - 1)
-    tot1(11)
-    tt(v("co1", 2 * H1 - 1, H1 * NS1, H1), v("ck1", 1, NS1), v("thr", 13, 12 + NS1), A.add)
-    ts(v("off1", 0, 1), v("ck1", 0, 1), 0.5, A.mult, W1 / 2, A.add)
-    ts(v("off1", 1, 12), v("co1", 2 * H1 - 1, 12 * H1, H1), 0.5, A.mult, 128.0, A.add)
+             float(KA - 16 * m), A.add, A.add)
+    for m in VP:
+        ts(v("cc1", W1 * m, W1 * m + H1), v("ps", 16 * m + 1, 16 * m + W1, 2), v("thr", 12 + m, 13 + m), A.max,
+           v("thr", 24 + m, 25 + m), A.min)
+        scan(v("co1", H1 * m + Q1, H1 * m + H1), v("cc1", W1 * m, W1 * m + Q1), v("cc1", W1 * m + Q1, W1 * m + H1),
+             v("thr", 36 + m, 37 + m), A.add, A.add)
+    for a, b in ((5, 8), (8, 12)):
+        ts(v("off1", a, b), v("co1", (1 + a) * H1 - 1, b * H1, H1), -1.0, A.mult, float(KA), A.add)
 
     for t, e in enumerate("SVSV"):
-        gather(e, v("tf", t, 4 * KA, 4), v("xp", C * t, C * t + C), v("off1"))
+        gather(e, v("tf", t, 512, 4), v("xp", C * t, C * t + C), v("off1", 0, 8))
+    for t, e in enumerate("SVSV"):
+        gather(e, v("tf", 512 + t, 4 * KA, 4), v("xp", C * t, C * t + C), v("off1", 8, 12))
     emake(1)
-    quant("f", 0, KA, v("tf"))
+    quant("f", 0, 128, v("tf", 0, 512))
+    quant("f2", 0, 128, v("tf", 256, 768))
     for b in range(4):
-        mm(b, "w", 128 * b, "f", 0, KA)
+        mm(b, "w", 128 * b, "f", 0, 128)
+    for b in range(4):
+        mm(4 + b, "w", 128 * b, "f2", 0, 128)
     fh = v("win", 4 * C)
     dma("Y", ap(fh), ap(v("tf")), [v("tf")], [fh])
     act(v("gate"), v("jm"), F.Relu, v("pf", 7, 8), -FAR)
-    picks("V", "2", 0, 256)
-    relu("S", v("th", 0, 4 * KA, 4), v("b0", 0, KA))
-    relu("S", v("th", 1, 4 * KA, 4), v("b1", 0, KA))
+    for a, b in cuts:
+        picks("V", "2", a, b)
+
+    def relus(b, e):
+        relu(e, v("th", b, 512, 4), v("b%d" % b, 0, 128))
+        relu(e, v("th", 512 + b, 4 * KA, 4), v("b%d" % (4 + b), 64, 128))
+
+    relus(0, "S")
+    relus(1, "V")
     scan(v("pa", 0, C), v("gate"), v("pos1", 1, C + 1), 0.0, A.add, A.min)
-    relu("V", v("th", 2, 4 * KA, 4), v("b2", 0, KA))
-    relu("S", v("th", 3, 4 * KA, 4), v("b3", 0, KA))
+    relus(2, "S")
+    relus(3, "V")
     scan(v("pa", C, 2 * C), v("gate"), v("pos1", 0, C), 0.0, A.add, A.min)
     act(v("yy", 1, 2 * KB, 2), v("pa", 3, C, 4), F.Identity, v("pf", 5, 6), FAR + 4)
     act(v("yy", 2 * KB, 4 * KB, 2), v("pa", C + 3, 2 * C, 4), F.Identity, 0.0, -FAR)
     quant("h0", 0, 128, v("th", 0, 512))
-    mm(4, "u2", 0, "h0", 0, 128)
+    mm(3, "p2", 256, "h0", 0, 128)
     quant("h", 0, KA, v("th"))
     planes("hp", "th", 0, KA)
     dma("G", ap(fh), ap(v("th")), [v("th"), fh], [fh], accum_op=A.add)
     mm(5, "p2", 0, "h", 0, KA)
     mm(6, "p2", 128, "h", 0, KA)
-    mm(7, "p2", 128, "h", 0, KA)
-    picks("V", "2", 256, 384)
 
-    turn(v("tr2", 0, 64), v("b4", 0, 64))
-    turn(v("tr2", 64, 128), v("b4", 64, 128))
     mm(0, "p2", 256, "h", 0, KA)
     turn(v("tr2", 128, KA), v("b0", 128, KA))
-    for j, c in enumerate((0, 2, 4, 6, 8, 10, 11)):
-        sign(v("junk2", KA * j, KA * j + KA), v("b%d" % (7 if c % 2 else 5), 0, KA), v("tr2", 16 * c, 16 * c + 1),
-             v("ks2", c, c + 1))
-    vcmp(2, KA, 0, 6, v("tr2", 16, 17))
-    for j in range(1, 5):
-        vcmp(2, KA, j, 6, v("tr2", 32 * j + 16, 32 * j + 17))
-        vsum(2, KA, j - 1)
+    turn(v("tr2", 0, 128), v("b3", 0, 128))
+    for j in range(6):
+        sign(v("junk2", KA * j, KA * j + KA), v("b5", 0, KA), v("tr2", 32 * j, 32 * j + 1), v("ks2", j, j + 1))
+        ts(v("cmp2", KA * j, KA * j + KA), v("b6", 0, KA), v("tr2", 32 * j + 16, 32 * j + 17), A.is_gt, BIG, A.mult)
+        vsum(2, KA, j)
     scan(v("yy", 4 * KB), v("yy", 0, 2 * KB), v("yy", 2 * KB, 4 * KB), 0.0, A.add, A.max)
-    vsum(2, KA, 4)
     ts(v("offx"), v("yy", 4 * KB + 1, 6 * KB, 2), v("pf", 1, 2), A.add)
     gather("S", v("l1"), v("ramp"), v("off1"))
-    gate(v("gd2", 0, 12, 2), v("ks2", 0, 12, 2))
-    gate(v("gd2", 11, 12), v("ks2", 11, 12))
-    late = v("so2", KB - 1, 5 * KB, KB)
-    threshold(2, KA, 12, [(1, 10, 2, v("tr2", 16, 160, 32), late), (11, 12, 1, v("tr2", 176, 177), v("gd2", 11, 12)),
-                          (0, 12, 2, v("tr2", 0, KA, 32), v("gd2", 0, 12, 2))],
-              [(None, True), (v("ks2", 11, 12), False), (v("ks2", 0, 12, 2), False), (late, True)], v("one", 0, 16))
-    running(2, KA, KB, 0, 1, KA)
+    gate(v("gd2", 0, 5), v("ks2", 0, 5))
+    act(v("junk2", 11 * KA, 11 * KA + 5), v("ks2", 0, 5), F.Sign, -0.5, 1.0, v("gk2"))
+    act(v("ex2", 192, 208), v("zero", 0, 16), F.Identity, v("gk2"))
+    tt(v("lb2", 0, 5), v("tr2", 0, 160, 32), v("gd2", 0, 5), A.min)
+    tt(v("la2", 0, 10, 2), v("tr2", 0, 160, 32), v("gd2", 0, 5), A.max)
+    tt(v("la2", 1, 12, 2), v("tr2", 16, KA, 32), v("so2", KB - 1, 6 * KB, KB), A.max)
+    scan(v("ex2", 75, 96), v("lb2", 0, 21), v("lb2", 0, 21), -64 * BIG, A.max, A.max)
+    scan(v("ex2", 139, 160), v("la2", 0, 42, 2), v("la2", 0, 42, 2), 64 * BIG, A.min, A.min)
+    scan(v("ex2", 180, 159, -1), v("la2", 1, 43, 2), v("la2", 1, 43, 2), 64 * BIG, A.min, A.min)
+    act(v("ex2", 224, 240), v("two", 0, 16), F.Sign, -1.0, v("ks2", 5, 6))
+    turn(v("tex2", 0, 64), v("ex2", 192, 256))
+    act(v("junk2", 11 * KA + 32, 11 * KA + 96), v("tex2", 0, 64), F.Identity, BIG / 128, BIG, v("red2", 64, 65))
+    gate(v("gd2", 5, 6), v("ks2", 5, 6))
+    ts(v("ex2", 256, 272), v("tr2", 160, 176), v("gd2", 5, 6), A.min)
+    ts(v("ex2", 288, 304), v("tr2", 160, 176), v("gd2", 5, 6), A.max)
+    turn(v("tex2", 64, 96), v("ex2", 80, 112))
+    turn(v("tex2", 96, 160), v("ex2", 256, 320))
+    turn(v("tex2", 160, 192), v("ex2", 144, 176))
+    scan(v("red2", 0, 64), v("tex2", 64, 128), v("tex2", 128, 192), v("red2", 64, 65), A.max, A.min)
+    running(2, KA, KB, v("red2", 63, 64), 0, 1, KA)
 
     H2 = W2 // 2
-
-    def span2(m):
+    S2 = (0, 1, 2, 3, 4)
+    for m in range(8):
         a = PC * dest[m // 2] + 16 * (m % 2)
-        return a, min(a + W2, KA)
-
-    def cmp2(m):
-        a, b = span2(m)
-        ts(v("cc2", W2 * m, W2 * m + b - a), v("pos2", 1 + a, 1 + b), v("thr2", m, m + 1), A.is_le)
-
-    def tot2(m):
-        a, b = span2(m)
+        b = min(a + W2, KA)
+        if m < 4:
+            a, b = PC * dest[m // 2], PC * dest[m // 2] + 120
         h = (b - a) // 2
-        scan(v("co2", H2 * m + H2 - h, H2 * m + H2), v("cc2", W2 * m, W2 * m + h), v("cc2", W2 * m + h, W2 * m + 2 * h),
-             float(a), A.add, A.add)
-
-    def scnt2(m):
-        a, b = span2(m)
-        sign(v("cj1", W2 * m, W2 * m + b - a), v("pos2", 1 + a, 1 + b), v("thr2", m, m + 1), v("ck2", m, m + 1))
-
-    def sout2(m):
-        a, b = span2(m)
-        ts(v("off2", m, m + 1), v("ck2", m, m + 1), 0.5, A.mult, (a + b) / 2, A.add)
+        if m in S2:
+            sign(v("cj1", 128 * m, 128 * m + b - a), v("pos2", 1 + a, 1 + b), v("thr2", m, m + 1), v("ck2", m, m + 1))
+            if m in (1, 3):
+                ts(v("off2", m - 1, m + 1), v("ck2", m - 1, m + 1), 0.5, A.mult, (a + b) / 2, A.add)
+            elif m == 4:
+                ts(v("off2", m, m + 1), v("ck2", m, m + 1), 0.5, A.mult, (a + b) / 2, A.add)
+        else:
+            ts(v("cc2", W2 * m, W2 * m + b - a), v("pos2", 1 + a, 1 + b), v("thr2", m, m + 1), A.is_le)
+            scan(v("co2", H2 * m + H2 - h, H2 * m + H2), v("cc2", W2 * m, W2 * m + h),
+                 v("cc2", W2 * m + h, W2 * m + 2 * h), float(a), A.add, A.add)
+    copy(v("off2", 5, 8), v("co2", 6 * H2 - 1, 8 * H2, H2))
 
     def tcol(i):
         return 96 + 32 * i if i else 0
 
-    for m in (0, 1, 2, 3):
-        scnt2(m)
-    cmp2(5)
-    tot2(5)
-    sout2(0)
-    sout2(1)
     for t, e in enumerate("SVSV"):
         gather(e, v("tg", t, 128, 4), v("hp", KA * t, KA * t + KA), v("off2", 0, 2))
     quant("a", 0, 128, v("tg", 0, 512))
     send(dest[0], "a", 0, "g", 128, True, "arr0", "left1")
-    scnt2(4)
-    cmp2(6)
-    cmp2(7)
-    sout2(2)
-    tot2(6)
-    tot2(7)
-    for m in (3, 4):
-        sout2(m)
-    copy(v("off2", 5, 8), v("co2", 6 * H2 - 1, 8 * H2, H2))
     for t, e in enumerate("SVSV"):
         gather(e, v("tg", 512 + t, 896, 4), v("hp", KA * t, KA * t + KA), v("off2", 2, 8))
     quant("g", 0, 128, v("tg", 384, 896))
     send(dest[1], "g", 32, "x", C, True, "arr1", "left1")
-    send(dest[2], "g", 64, "f", KA, False, "arr2", "left1")
+    send(dest[2], "g", 64, "f", 128, False, "arr2", "left1")
 
     A1, A2 = 128, 208
     at4 = (0, 10, 16, 24)
@@ -583,11 +561,11 @@ def rank_program(g, core, T, topo):
     place("V", A2 + 64, C)
     ts(v("offs"), v("old", 3, 128, 4), 4.0, A.mult, v("pf", 3, 4), A.add)
 
-    def through(banks, src, a, at, to, n):
+    def through(banks, src, a, at, to, n, es):
         for b in range(4):
             mm(banks[b], "z", 128 * b, src, a, 128)
         for b in range(4):
-            relu("S", v("tt", 4 * to + b, 4 * (to + 128 - at), 4), v("b%d" % banks[b], at, 128))
+            relu(es[b], v("tt", 4 * to + b, 4 * (to + 128 - at), 4), v("b%d" % banks[b], at, 128))
         quant(n, 0, 128, v("tt", 4 * to, 4 * to + 512))
 
     def unpack(banks, src, a):
@@ -605,7 +583,7 @@ def rank_program(g, core, T, topo):
 
     def up2(i):
         run = (32 * at4[i], 32 * at4[i] + 2 * KB)
-        scan(v("nw", *run), v("alt"), v("hs", *run), 0.0, A.mult, A.add)
+        scan(v("nw", *run), v("alt", 0, KA), v("hs", *run), 0.0, A.mult, A.add)
 
     def put(i):
         scatter(v("tx"), v("offs", at4[i], at4[i] + 6), v("nw", 32 * at4[i] + 1, 32 * at4[i] + 2 * KB, 2))
@@ -614,13 +592,13 @@ def rank_program(g, core, T, topo):
     parts(3, 1)
     emake(2)
     ts(v("offs", 10, 16), v("old", 35, 56, 4), 4.0, A.mult, v("pf", 3, 4), A.add)
-    through(hi4, "g", PC, 72, 2 * PC, "t1")
+    through(hi4, "g", PC, 72, 2 * PC, "t1", "SVSV")
     send(dest[0], "t1", 32, "h", KA, True, "arr3", "left2")
     emake(3)
-    through(lo4, "x", C + PC - 128, 104, PC, "t2")
+    through(lo4, "x", C + PC - 128, 104, PC, "t2", "SSSV")
     send(dest[1], "t2", 0, "a", 128, True, "arr4", "left2")
-    through(hi4, "f", KA + PC - 128, 104, 0, "t3")
-    send(dest[2], "t3", 0, "f", KA + PC, True, "arr5", "left2")
+    through(hi4, "f", PC, 104, 0, "t3", "SSSV")
+    send(dest[2], "t3", 0, "f", 128 + PC, True, "arr5", "left2")
     for i in range(N):
         dma("Y", T.ol[:, PC * dest[i]:PC * dest[i] + PC], T.olr[0:128:16, 32 * i:32 * i + PC], [v("olr")], [], "left2")
 
@@ -639,7 +617,7 @@ def rank_program(g, core, T, topo):
     up(lo4, 104, 1, (0,))
     put(0)
     up(lo4, 104, 1, (1, 2, 3))
-    unpack(hi4, "f", KA + 2 * PC - 128)
+    unpack(hi4, "f", 2 * PC)
     up(hi4, 104, 2, (0,))
     up2(1)
     up(hi4, 104, 2, (1, 2, 3))
@@ -647,10 +625,9 @@ def rank_program(g, core, T, topo):
     up2(2)
     put(2)
 
-    quant("y", 0, 256, v("tx", 0, 1024))
-    mm(0, "v", 0, "y", 0, 256)
-    quant("y", 256, C, v("tx", 1024))
-    mm(1, "v", 0, "y", 256, 128)
+    for j in range(3):
+        quant("y", 128 * j, 128 * j + 128, v("tx", 512 * j, 512 * j + 512))
+        mm(j, "v", 0, "y", 128 * j, 128)
     dma("Y", T.oc[:], codes("y", 0, C), [v("qy")], [])
 
     def scales(e, k):
@@ -658,8 +635,8 @@ def rank_program(g, core, T, topo):
 
     scales("Y", 0)
     scales("Y", 1)
-    copy(v("yb", 0, 256), v("b0", 0, 256), "S")
-    copy(v("yb", 256, C), v("b1", 0, 128), "V")
+    for j, e in enumerate("SSV"):
+        copy(v("yb", 128 * j, 128 * j + 128), v("b%d" % j, 0, 128), e)
     dma("Y", T.y[:], ap(v("yb")), [v("yb")], [])
     scales("S", 2)
     scales("S", 3)

from concourse.bass import DstId, RemoteDMATransfer
from concourse.mybir import dt, AluOpType as A, ActivationFunctionType as F

C, KA, KB, PC = 384, 192, 96, 24
BIG = 2.0 ** 90
W1, W2 = C - KA + 16, KA - KB + 16
FAR = 4096.0
X4, U8, BF, F32, I32, U16 = "float8_e4m3fn_x4", "uint8", "bfloat16", "float32", "int32", "uint16"

SCRATCH = {}
for _n, _w in (("x", C + 4 * PC), ("h", KA + 4 * PC), ("f", 128 + 5 * PC), ("a", 128 + 4 * PC), ("g", 128 + 4 * PC),
               ("f2", 128), ("h0", 128), ("t1", 128), ("t2", 128), ("t3", 128), ("u1", 128), ("u2", 128), ("p1", 384),
               ("p2", 384), ("v", 128), ("e", 512), ("w", 512), ("z", 512), ("y", C)):
    SCRATCH["q" + _n] = ("sbuf", [128, _w], X4)
    SCRATCH["s" + _n] = ("sbuf", [128, _w], U8)
for _n, _w, _d in (
        ("win", 4 * (C + KA), BF), ("xp", 4 * C, BF), ("hp", 4 * KA, BF), ("tu1", 512, BF), ("tu2", 512, BF),
        ("tv", 512, BF), ("tf", 4 * KA, BF), ("th", 4 * KA, BF), ("tg", 4 * 224, BF), ("tt", 4 * 176, BF),
        ("te", 516, BF), ("one", 516, BF), ("zero", C, BF), ("hs", 1024, BF), ("alt", C, BF), ("nw", 1024, BF),
        ("tx", 4 * C, BF), ("yb", C, F32), ("oi", 24, I32), ("offc", 24, U16), ("pi", 4, I32), ("ramp", C, F32),
        ("jm", C, BF), ("gate", C, BF), ("l1", KA, F32), ("olr", 128, F32), ("old", 128, F32), ("offs", 32, U16),
        ("pa", 2 * C, BF), ("yy", 6 * KB, F32), ("offx", KB, U16), ("ps", C, BF), ("cj1", 5 * 256, BF),
        ("cc1", 12 * W1, BF), ("co1", 6 * W1, BF), ("off1", 12, U16), ("c2", 4 * 130, BF), ("s2", 4 * 65, BF),
        ("cc2", 8 * W2, BF), ("off2", 8, U16)):
    SCRATCH[_n] = ("sbuf", [128, _w], _d)
for _i, _c, _k in ((1, C, KA), (2, KA, KB)):
    for _n, _w, _d in (("tr", _c, F32), ("junk", 12 * _c, BF), ("cmp", 8 * _c, BF), ("so", 8 * _k, BF), ("gt", _c, BF),
                       ("ge", _c, BF), ("sg", _c, BF), ("cap", _c, BF), ("pos", _c + 2, BF)):
        SCRATCH["%s%d" % (_n, _i)] = ("sbuf", [128, _w], _d)
PART, _at = {}, 0
for _n, _w in (("cl", 256), ("lb1", 48), ("b1l", 40), ("lb2", 40), ("ch", 256), ("la1", 40), ("b1h", 40), ("la2", 48),
               ("pf", 12), ("thr", 60), ("m32", 60), ("m2", 8), ("thr2", 8), ("two", 32), ("cd", 16), ("ck1", 12),
               ("u3", 256), ("r3", 256), ("e1", 320), ("t1", 256), ("jj", 2), ("g2", 4), ("co2", 4 * W2), ("ck2", 8),
               ("ks1", 16), ("gk1", 4), ("red1", 65), ("ks2", 6), ("gd2", 6), ("gk2", 1), ("ex2", 320), ("tex2", 192),
               ("red2", 65)):
    PART[_n] = (_at, _w)
    _at += -(-_w // 8) * 8
SCRATCH["sel"] = ("sbuf", [128, _at], F32)
for _i in range(8):
    SCRATCH["b%d" % _i] = ("psum", [128, 512], F32)

SEMAPHORES = (["cV", "cS", "cP", "cG", "left1", "left2"] + ["arr%d" % _i for _i in range(6)]
              + ["d%02d" % _i for _i in range(40)])

ORDER = [0,12,1,2,11,32,75,10,9,3,4,5,6,7,25,26,27,15,28,24,51,16,14,47,41,40,43,17,42,48,49,53,29,35,34,30,37,33,36,39,31,38,77,80,78,74,81,76,8,52,58,56,59,62,61,54,65,46,45,23,22,55,57,44,13,50,63,82,83,87,84,60,64,67,66,68,93,94,86,120,89,88,98,90,85,95,110,96,97,113,99,92,91,102,100,103,107,106,104,111,112,108,116,128,126,130,129,131,105,101,109,115,114,71,72,136,117,118,139,119,135,132,144,146,145,134,133,143,151,138,149,147,153,152,148,150,154,140,137,155,156,19,20,121,159,161,160,157,158,164,162,163,165,141,142,167,122,127,166,219,222,168,171,172,376,169,170,173,174,73,69,79,70,124,125,21,177,176,175,183,185,191,187,193,195,189,186,184,188,196,192,194,190,197,178,179,180,181,182,18,201,199,220,198,200,202,206,204,208,212,213,211,210,205,203,218,223,209,233,221,231,226,228,214,216,217,215,269,229,224,225,230,235,234,232,227,236,239,240,238,237,244,267,248,245,207,246,340,255,241,253,252,247,256,258,254,265,242,249,259,262,261,250,264,260,263,266,270,257,271,251,282,243,279,274,273,272,275,284,283,277,280,276,278,286,281,285,287,123,288,289,290,291,328,292,268,301,293,305,303,294,302,299,306,304,297,295,296,300,308,309,311,310,307,298,312,321,317,315,314,316,324,369,326,318,329,322,323,325,313,319,320,332,333,330,331,336,344,337,341,334,343,335,370,342,348,354,345,353,347,338,352,346,351,327,358,357,349,368,356,355,365,371,366,339,367,375,372,373,350,374,359,377,378,360,380,379,382,381,384,388,383,391,386,389,385,390,392,387,396,397,362,394,361,395,398,363,364,400,393,399,402,401,404,403,405,406,407,408,411,409,413,412,410,414,415,419,417,416,418,420,423,422,421]


def rank_program(g, core, T, topo):
    rank = T.rank_of(core)
    if rank is None:
        return
    N = len(T.cores)
    Q = {"V": g.vector, "S": g.scalar, "P": g.tensor, "G": g, "Y": g.sync}
    clock = {e: {} for e in Q}
    count = {}
    seen = {}
    log = {}
    ndma, last = [0], [None]

    def ap(w):
        n, a, b, s = w
        return T[n][:, a:b] if s == 1 else T[n][:, a:b:s]

    def v(n, a=0, b=None, s=1):
        if n in PART:
            at, w = PART[n]
            return ("sel", at + a, at + (w if b is None else min(b, w)), s)
        return (n, a, SCRATCH[n][1][1] if b is None and s > 0 else b, s)

    def cols(w):
        n, a, b, s = w
        return set(range(a, -1 if b is None else b, s))

    def wait(e, sem, c, ck):
        if clock[e].get(sem, 0) < c:
            Q[e].wait_ge(T.sem[sem], c)
            clock[e][sem] = c
            seen[sem] = max(seen.get(sem, 0), c)
            for k, x in ck.items():
                if clock[e].get(k, 0) < x:
                    clock[e][k] = x

    def order(e, reads, writes):
        need = {}
        for w, wr in [(w, False) for w in reads] + [(w, True) for w in writes]:
            cs, bank = cols(w), SCRATCH[w[0]][0] == "psum"
            for (e2, sem, c, ck, cs2, wr2) in log.get(w[0], []):
                if (bank and e2 != e) or ((wr or wr2) and cs & cs2):
                    if need.get(sem, (0, None))[0] < c:
                        need[sem] = (c, ck)
        for sem, (c, ck) in sorted(need.items(), key=lambda kv: -len(kv[1][1])):
            wait(e, sem, c, ck)

    def note(e, sem, c, reads, writes):
        ck = dict(clock[e]) if e in clock else {}
        for w, wr in [(w, False) for w in reads] + [(w, True) for w in writes]:
            log.setdefault(w[0], []).append((e, sem, c, ck, cols(w), wr))

    todo = []

    def op(e, call, reads, writes):
        def issue():
            order(e, reads, writes)
            sem = "c" + e
            count[sem] = count.get(sem, 0) + 1
            call().then_inc(T.sem[sem], 1)
            note(e, sem, count[sem], reads, writes)
        todo.append((e, issue, reads, writes))

    def dma(e, out, in_, reads, writes, after=None, **how):
        def issue():
            if after:
                wait(e, after, count[after], {})
            order(e, reads, writes)
            sem = "d%02d" % ndma[0]
            ndma[0] += 1
            count[sem] = 16
            if writes == [] and reads == [v("yb")]:
                last[0] = sem
            Q[e].dma_start(out, in_, **how).then_inc(T.sem[sem], 16)
            note(e, sem, 16, reads, writes)
        todo.append((e, issue, reads, writes))

    def views(*xs):
        return [x for x in xs if isinstance(x, tuple)]

    def val(x):
        return ap(x) if isinstance(x, tuple) else x

    V, S = g.vector, g.scalar

    def act(o, i, f, bias=0.0, scale=1.0, acc=None):
        op("S", lambda: S.activation(ap(o), ap(i), f, bias=val(bias), scale=val(scale), accum_out=val(acc)),
           views(i, bias, scale), views(o, acc))

    def fill(w, c):
        act(w, v("zero", 0, len(cols(w))), F.Identity, c)

    def copy(o, i, e="V"):
        if e == "V":
            op("V", lambda: V.tensor_copy(ap(o), ap(i)), [i], [o])
        else:
            op("S", lambda: S.activation(ap(o), ap(i), F.Copy), [i], [o])

    def tt(o, a, b, alu):
        op("V", lambda: V.tensor_tensor(ap(o), ap(a), ap(b), alu), [a, b], [o])

    def ts(o, a, s1, o1, s2=None, o2=None):
        if o2 is None:
            op("V", lambda: V.tensor_scalar(ap(o), ap(a), val(s1), None, o1), views(a, s1), [o])
        else:
            op("V", lambda: V.tensor_scalar(ap(o), ap(a), val(s1), val(s2), o1, o2), views(a, s1, s2), [o])

    def scan(o, d0, d1, init, o0, o1):
        op("V", lambda: V.tensor_tensor_scan(ap(o), ap(d0), ap(d1), val(init), o0, o1), views(d0, d1, init), [o])

    def turn(o, i):
        op("V", lambda: V.transpose(ap(o), ap(i)), [i], [o])

    def gather(e, o, w, off):
        if e == "V":
            op("V", lambda: V.tensor_copy(ap(o), ap(w).indirect(ap(off))), [w, off], [o])
        else:
            op("S", lambda: S.activation(ap(o), ap(w).indirect(ap(off)), F.Copy), [w, off], [o])

    def scatter(w, off, i):
        op("V", lambda: V.tensor_copy(ap(w).indirect(ap(off)), ap(i)), [i, off], [w])

    def sign(o, row, thr, acc=None):
        act(o, row, F.Sign, thr, -1.0, acc)

    def gate(o, i):
        act(o, i, F.Identity, BIG / 2, -BIG)

    def relu(e, o, i):
        if e == "V":
            ts(o, i, 0.0, A.max, 0.03125, A.mult)
        else:
            act(o, i, F.Relu, 0.0, 0.03125)

    def quant(n, a, b, tile):
        q, s = v("q" + n, a, b), v("s" + n, a, b)
        op("V", lambda: V.quantize_mx(ap(q), ap(s), ap(tile)), [tile], [q, s])

    def mm(bank, l, la, r, ra, n):
        o, lq, ls = v("b%d" % bank, 0, n), v("q" + l, la, la + 128), v("s" + l, la, la + 128)
        rq, rs = v("q" + r, ra, ra + n), v("s" + r, ra, ra + n)
        op("P", lambda: g.tensor.matmul_mx(ap(o), ap(lq), ap(ls), ap(rq), ap(rs), True, True), [lq, ls, rq, rs], [o])

    def iota(o, pattern, base, cm=0):
        if SCRATCH[o[0]][2] == I32:
            op("G", lambda: g.iota(ap(o), pattern, base, cm), [], [o])
        else:
            op("G", lambda: g.iota(ap(o), pattern, base, cm, allow_small_or_imprecise_dtypes=True), [], [o])

    def level(o, c):
        iota(o, [[0, len(cols(o))]], c)

    def planes(dst, src, a, n):
        for t in range(4):
            o, i = v(dst, n * t, n * t + n), v(src, a + t, a + 4 * n, 4)
            op("G", lambda o=o, i=i: g.affine_select(ap(o), ap(i), [[0, n]], A.is_ge, 0.0, 0, 0), [i], [o])

    def picks(e, n, a, b):
        off = v("offc", a // 16, b // 16)
        if e == "V":
            o, i = v("qp" + n, a, b), v("qu" + n)
            op("V", lambda: V.tensor_copy(ap(o).bitcast(dt.uint32), ap(i).bitcast(dt.uint32).indirect(ap(off))),
               [i, off], [o])
        else:
            o, i = v("sp" + n, a, b), v("su" + n)
            op("S", lambda: S.activation(ap(o), ap(i).indirect(ap(off)), F.Copy), [i, off], [o])

    def codes(n, a, b):
        return ap(v("q" + n, a, b)).bitcast(dt.uint8)

    def send(d, src, a, dst, b, both, sem, left):
        en = topo.engines(core, T.cores[d])
        rid, pid = topo.addr(T.cores[d])[:2]
        wide = 4 * PC if both else PC
        reads = [v("q" + src, a, a + PC), v("s" + src, a, a + wide)]
        lands = [v("q" + dst, b, b + PC), v("s" + dst, b, b + wide)]
        pair = [(codes(src, a, a + PC), codes(dst, b, b + PC)),
                (ap(v("s" + src, a, a + wide)), ap(v("s" + dst, b, b + wide)))]
        half = len(en) // 2
        use = (en[:half], en[half:]) if both else (en, en)
        trs = [RemoteDMATransfer(dst_ids=[DstId(rid=rid, pnc=pid)], dma_engine_mask=sum(1 << x for x in u),
                                 remote_sem=T.sem[sem], src=i, dst=o) for (i, o), u in zip(pair, use)]

        def issue():
            order("G", reads, [])
            for call in ([trs] if both else [trs[:1], trs[1:]]):
                g.remote_dma_fused(call, local_sem=T.sem[left])
            for k in (sem, left):
                count[k] = count.get(k, 0) + len(use[0]) + len(use[1])
            note("remote", sem, count[sem], [], lands)
        todo.append(("G", issue, reads, lands))

    steps = sorted(range(1, N), key=lambda j: all(topo.die(T.cores[r]) == topo.die(T.cores[r ^ j]) for r in range(N)))
    dest = [rank ^ j for j in steps] + [rank]

    def vsum(i, n, slot):
        k = n // 2
        scan(v("so%d" % i, k * slot, k * slot + k), v("cmp%d" % i, n * slot, n * slot + k),
             v("cmp%d" % i, n * slot + k, n * slot + n), (0.5 - k) * BIG, A.add, A.add)

    def running(i, n, k, t, bank, bank2, cut):
        s = str(i)
        ts(v("gt" + s), v("b%d" % bank, 0, n), t, A.is_gt)
        ts(v("ge" + s, 0, cut), v("b%d" % bank, 0, cut), t, A.is_ge)
        if cut < n:
            sign(v("sg" + s, cut, n), v("b%d" % bank2, cut, n), t)
            act(v("ge" + s, cut, n), v("sg" + s, cut, n), F.Sign, 1.0, -1.0)
        scan(v("cap" + s, n - 2, None, -1), v("zero", 0, n - 1), v("gt" + s, n - 1, 0, -1), float(KB), A.add, A.subtract)
        scan(v("pos" + s, 1, n + 1), v("ge" + s), v("cap" + s), float(KB - k), A.add, A.min)

    def emake(b):
        quant("e", 128 * b, 128 * b + 128, v("te", 3 - b, 515 - b))

    dma("Y", ap(v("tu1")), T.u1[:], [], [v("tu1")])
    dma("Y", ap(v("win", 0, 768)), T.x[:, 0:768], [], [v("win", 0, 768)])
    dma("Y", ap(v("win", 768, 1536)), T.x[:, 768:1536], [], [v("win", 768, 1536)])
    dma("Y", ap(v("tu2")), T.u2[:], [], [v("tu2")])
    dma("Y", codes("w", 0, 512), T.wc[:], [], [v("qw")])
    dma("Y", ap(v("sw")), T.ws[:], [], [v("sw")])
    dma("Y", codes("z", 0, 512), T.zc[:], [], [v("qz")])
    dma("Y", ap(v("sz")), T.zs[:], [], [v("sz")])
    dma("Y", ap(v("tv")), T.v[:], [], [v("tv")])

    iota(v("oi", 0, 16), [[16, 2], [32, 4], [0, 2]], 0)
    iota(v("oi", 16, 24), [[16, 8]], 0)
    iota(v("pi", 0, 1), [[0, 1]], 0, 1)
    op("V", lambda: V.memset(ap(v("zero")), 0.0), [], [v("zero")])
    fill(("sel", 0, 384, 1), -64 * BIG)
    fill(("sel", 384, 768, 1), 64 * BIG)
    fill(v("e1", 64, 112), -64 * BIG)
    fill(v("c2", 0, 520, 130), -128 * BIG)
    fill(v("c2", 129, 520, 130), 0.0)
    fill(v("ex2", 208, 224), 1.0)
    fill(v("ex2", 240, 256), 0.0)
    fill(v("ex2", 272, 288), -64 * BIG)
    fill(v("ex2", 304, 320), 64 * BIG)
    fill(v("ex2", 96, 144), -64 * BIG)
    fill(v("yy", 0, 2 * KB, 2), -2.0 ** 30)
    copy(v("offc"), v("oi"))
    ts(v("pi", 1, 2), v("pi", 0, 1), 15, A.bitwise_and)
    ts(v("pi", 3, 4), v("pi", 0, 1), 3, A.bitwise_and)
    ts(v("pi", 2, 3), v("pi", 1, 2), 2, A.logical_shift_right)
    copy(v("pf", 0, 4), v("pi"))
    for i in range(N):
        iota(v("m2", 2 * i, 2 * i + 2), [[16, 2]], PC * dest[i])
    level(v("two"), 2)
    iota(v("m32", 0, 12), [[32, 12]], 1 - KA)
    iota(v("m32", 12, 36), [[2, 2], [32, 12]], -KA)
    iota(v("m32", 36, 48), [[-16 - 16 * W1, 12]], KA + W1 // 2 * (KA - 2))
    iota(v("m32", 48, 60), [[16, 12]], 0)
    level(v("cap1", C - 1), KB)
    level(v("pos1", 0, 1), -KB)
    act(v("pf", 4, 5), v("pf", 1, 2), F.Identity, 0.5 - KB)
    act(v("pf", 8, 9), v("pf", 1, 2), F.Identity, 0.0, 2.0)
    act(v("pf", 9, 10), v("pf", 1, 2), F.Identity, 0.0, -float(W1))
    act(v("pf", 10, 11), v("pf", 1, 2), F.Identity, 0.5)
    act(v("thr", 0, 36), v("m32", 0, 36), F.Identity, v("pf", 8, 9))
    act(v("thr", 36, 48), v("m32", 36, 48), F.Identity, v("pf", 9, 10))
    act(v("thr", 48, 60), v("m32", 48, 60), F.Identity, v("pf", 4, 5))
    act(v("pf", 6, 7), v("pf", 1, 2), F.Identity, 4.0 * C - 4 - FAR + 4 * KB, -1.0)
    act(v("pf", 7, 8), v("pf", 2, 3), F.Identity, FAR, FAR)
    act(v("pf", 5, 6), v("pf", 3, 4), F.Identity, v("pf", 6, 7))
    act(v("m2"), v("m2"), F.Identity, v("pf", 10, 11))

    def cand(c):
        return v("cd", 2 * c + 1, 2 * c + 2)

    def sort3(h):
        ca, cb, cc = (v("tr1", 192 * h + 64 * j, 192 * h + 64 * j + 64, 16) for j in range(3))
        at = 192 * h + 128
        d0, d1 = (v("tr1", at + j, at + 64, 8) for j in range(2))
        mn, mx = (v("tr1", at + 8 + j, at + 64, 16) for j in range(2))
        tt(mx, ca, cb, A.max)
        tt(mn, ca, cb, A.min)
        scan(v("cd", 8 * h, 8 * h + 8), d0, d1, 0.0, A.max, A.min)
        tt(v("cl", 4 * h, 4 * h + 4), mn, cc, A.min)
        tt(v("ch", 4 * h, 4 * h + 4), mx, cc, A.max)

    def g1(a, b, st=1):
        return v("so1", KA * a + KA - 1, KA * b, KA * st)

    def choose(c):
        b = 128 * (c % 2) + 32 * (c // 2)
        scan(v("u3", b, b + 32), v("cl", c, 256, 8), v("ch", c, 256, 8), g1(c, c + 1), A.max, A.min)

    quant("u1", 0, 128, v("tu1"))
    for a, b in ((256, 384), (128, 256), (0, 128)):
        picks("V", "1", a, b)
        picks("S", "1", a, b)
    quant("x", 0, KA, v("win", 0, 768))
    mm(0, "p1", 256, "x", 0, KA)
    mm(1, "p1", 128, "x", 0, KA)
    turn(v("tr1", 0, KA), v("b0", 0, KA))
    quant("x", KA, C, v("win", 768, 1536))
    mm(2, "p1", 0, "x", 0, C)
    mm(3, "p1", 128, "x", KA, KA)
    mm(5, "p1", 256, "x", KA, KA)
    mm(4, "p1", 128, "x", 0, C)
    mm(6, "p1", 256, "x", 0, C)
    mm(7, "p1", 256, "x", 0, C)
    level(v("one"), 1)
    op("G", lambda: g.affine_select(ap(v("te")), ap(v("one")), [[1, 516]], A.is_equal, 0.0, -3, -4), [v("one")],
       [v("te")])
    planes("xp", "win", 0, C)
    level(v("cap2", KA - 1), KB)
    iota(v("jm"), [[0, KB], [1, 4]], 0)
    iota(v("yy", 2 * KB + 1, 4 * KB, 2), [[16, KB]], 0)
    level(v("tg", 128, 512), 0)
    iota(v("ramp"), [[1, C]], 0)
    level(v("tt", 4 * 104), 0)
    iota(v("alt"), [[0, KA], [1, 2]], 0)

    sort3(0)
    turn(v("tr1", KA, C), v("b5", 0, KA))
    sort3(1)
    for j, c in enumerate((0, 2, 4, 6, 1)):
        sign(v("junk1", C * j, C * j + C), v("b%d" % (4 if c % 2 else 2), 0, C), cand(c), v("ks1", c, c + 1))
    for c in (3, 5, 7):
        for h, bank in enumerate((1, 3)):
            ts(v("cmp1", C * c + KA * h, C * c + KA * h + KA), v("b%d" % bank, 0, KA), cand(c), A.is_gt, BIG, A.mult)
        vsum(1, C, c)
        choose(c)
    for cs in ((0, 2), (4, 6), (1,)):
        gate(g1(cs[0], cs[-1] + 1, len(cs)), v("ks1", cs[0], cs[-1] + 1, len(cs)))
        for c in cs:
            choose(c)
    for a in range(0, 256, 128):
        turn(v("r3", a, a + 128), v("u3", a, a + 128))
    quant("u2", 0, 128, v("tu2"))
    act(v("thr2"), v("m2"), F.Relu, KB - 0.5, -1.0)
    act(v("thr2"), v("thr2"), F.Identity, KB - 0.5, -1.0)
    emake(0)
    cuts = ((0, 128), (128, 256), (256, 320), (320, 384))
    for a, b in cuts:
        picks("S", "2", a, b)
    JK = 11 * C
    for h in range(2):
        act(v("junk1", JK + 8 * h, JK + 8 * h + 4), g1(h, 8, 2), F.Sign, 0.0, 1.0, v("gk1", h, h + 1))
        act(v("e1", 256 + 32 * h, 288 + 32 * h), v("two"), F.Identity, 0.0, v("gk1", h, h + 1))
    turn(v("t1", 192, 256), v("e1", 256, 320))
    for h in range(2):
        act(v("junk1", JK + 32 + 32 * h, JK + 64 + 32 * h), v("t1", 192 + 32 * h, 224 + 32 * h), F.Identity, BIG / 64,
            -BIG, v("jj", h, h + 1))
    tt(v("b1l", 0, 8), v("cd", 1, 16, 2), g1(0, 8), A.min)
    tt(v("b1h", 0, 8), v("cd", 1, 16, 2), g1(0, 8), A.max)

    def spread(at, ins, init, alu):
        for d, o in zip(ins, (v("e1", at - 3, at + 16), v("e1", at + 34, at + 15, -1))):
            scan(o, d, d, init, alu, alu)

    spread(160, [v("b1l", h, 38, 2) for h in range(2)], -64 * BIG, A.max)
    spread(208, [v("b1h", h, 38, 2) for h in range(2)], 64 * BIG, A.min)
    turn(v("t1", 32, 64), v("e1", 160, 192))
    turn(v("t1", 160, 192), v("e1", 208, 240))

    for b in range(4):
        sign(v("junk1", C * 7 + 128 * b, C * 7 + 128 * b + 128), v("r3", 0, 128), v("u3", 32 * b, 32 * b + 1),
             v("ks1", 8 + b, 9 + b))
    for j in range(4):
        ts(v("c2", 130 * j + 1, 130 * j + 129), v("r3", 128, 256), v("u3", 128 + 32 * j, 129 + 32 * j), A.is_gt,
           2 * BIG, A.mult)
        scan(v("s2", 65 * j, 65 * j + 65), v("c2", 130 * j, 130 * j + 65), v("c2", 130 * j + 65, 130 * j + 130),
             v("jj", 1, 2), A.add, A.add)
    act(v("g2"), v("ks1", 8, 12), F.Identity, v("jj", 0, 1), -BIG)
    act(v("junk1", JK + 16, JK + 20), v("ks1", 8, 12), F.Sign, v("jj", 0, 1), -BIG, v("gk1", 2, 3))
    tt(v("lb1", 16, 20), v("u3", 0, 128, 32), v("g2"), A.min)
    tt(v("la1", 16, 20), v("u3", 0, 128, 32), v("g2"), A.max)
    act(v("e1", 0, 16), v("two", 0, 16), F.Identity, v("gk1", 2, 3), v("gk1", 0, 1))
    tt(v("la1", 20, 24), v("u3", 128, 256, 32), v("s2", 64, 260, 65), A.max)
    act(v("e1", 16, 32), v("two", 0, 16), F.Identity, -257.0 / 64, v("gk1", 1, 2))
    spread(48, [v("lb1", 19, 0, -1)], -64 * BIG, A.max)
    spread(112, [v("la1", 19, 0, -1), v("la1", 20, 39)], 64 * BIG, A.min)
    turn(v("t1", 0, 32), v("e1", 0, 32))
    act(v("junk1", JK + 96, JK + 128), v("t1", 0, 32), F.Identity, BIG / 64, -BIG, v("red1", 64, 65))
    turn(v("t1", 64, 160), v("e1", 48, 144))
    scan(v("red1", 0, 64), v("t1", 95, 31, -1), v("t1", 128, 192), v("red1", 64, 65), A.max, A.min)
    running(1, C, KA, v("red1", 63, 64), 6, 7, 160)

    H1, Q1 = W1 // 2, W1 // 4
    SR, SP, VR, VP = (0, 1), (2, 3, 4), (5, 6), (7, 8, 9, 10, 11)
    scan(v("ps"), v("alt"), v("pos1", 1, C + 1), 0.0, A.mult, A.add)
    WR = W1 + 16 * (len(SR) - 1)
    for m in SR:
        sign(v("cj1", 256 * m, 256 * m + WR), v("pos1", 1, 1 + WR), v("thr", 48 + m, 49 + m), v("ck1", m, m + 1))
    ts(v("off1", SR[0], SR[-1] + 1), v("ck1", SR[0], SR[-1] + 1), 0.5, A.mult, WR / 2, A.add)
    WU = H1 + 8 * (len(SP) - 1)
    for m in SP:
        sign(v("cj1", 256 * m, 256 * m + WU), v("ps", 16 * SP[0] + 1, 16 * SP[0] + 2 * WU, 2), v("thr", m, m + 1),
             v("ck1", m, m + 1))
    ts(v("off1", SP[0], SP[-1] + 1), v("ck1", SP[0], SP[-1] + 1), float(WU + 16 * SP[0]), A.add)
    for m in VR:
        ts(v("cc1", W1 * m, W1 * m + W1), v("pos1", 1 + 16 * m, 1 + 16 * m + W1), v("thr", 48 + m, 49 + m), A.is_le,
           -1.0, A.mult)
        scan(v("co1", H1 * m, H1 * m + H1), v("cc1", W1 * m, W1 * m + H1), v("cc1", W1 * m + H1, W1 * m + W1),
             float(KA - 16 * m), A.add, A.add)
    for m in VP:
        ts(v("cc1", W1 * m, W1 * m + H1), v("ps", 16 * m + 1, 16 * m + W1, 2), v("thr", 12 + m, 13 + m), A.max,
           v("thr", 24 + m, 25 + m), A.min)
        scan(v("co1", H1 * m + Q1, H1 * m + H1), v("cc1", W1 * m, W1 * m + Q1), v("cc1", W1 * m + Q1, W1 * m + H1),
             v("thr", 36 + m, 37 + m), A.add, A.add)
    for a, b in ((5, 8), (8, 12)):
        ts(v("off1", a, b), v("co1", (1 + a) * H1 - 1, b * H1, H1), -1.0, A.mult, float(KA), A.add)

    for t, e in enumerate("SVSV"):
        gather(e, v("tf", t, 512, 4), v("xp", C * t, C * t + C), v("off1", 0, 8))
    for t, e in enumerate("SVSV"):
        gather(e, v("tf", 512 + t, 4 * KA, 4), v("xp", C * t, C * t + C), v("off1", 8, 12))
    emake(1)
    quant("f", 0, 128, v("tf", 0, 512))
    quant("f2", 0, 128, v("tf", 256, 768))
    for b in range(4):
        mm(b, "w", 128 * b, "f", 0, 128)
    for b in range(4):
        mm(4 + b, "w", 128 * b, "f2", 0, 128)
    fh = v("win", 4 * C)
    dma("Y", ap(fh), ap(v("tf")), [v("tf")], [fh])
    act(v("gate"), v("jm"), F.Relu, v("pf", 7, 8), -FAR)
    for a, b in cuts:
        picks("V", "2", a, b)

    def relus(b, e):
        relu(e, v("th", b, 512, 4), v("b%d" % b, 0, 128))
        relu(e, v("th", 512 + b, 4 * KA, 4), v("b%d" % (4 + b), 64, 128))

    relus(0, "S")
    relus(1, "V")
    scan(v("pa", 0, C), v("gate"), v("pos1", 1, C + 1), 0.0, A.add, A.min)
    relus(2, "S")
    relus(3, "V")
    scan(v("pa", C, 2 * C), v("gate"), v("pos1", 0, C), 0.0, A.add, A.min)
    act(v("yy", 1, 2 * KB, 2), v("pa", 3, C, 4), F.Identity, v("pf", 5, 6), FAR + 4)
    act(v("yy", 2 * KB, 4 * KB, 2), v("pa", C + 3, 2 * C, 4), F.Identity, 0.0, -FAR)
    quant("h0", 0, 128, v("th", 0, 512))
    mm(3, "p2", 256, "h0", 0, 128)
    quant("h", 0, KA, v("th"))
    planes("hp", "th", 0, KA)
    dma("G", ap(fh), ap(v("th")), [v("th"), fh], [fh], accum_op=A.add)
    mm(5, "p2", 0, "h", 0, KA)
    mm(6, "p2", 128, "h", 0, KA)

    mm(0, "p2", 256, "h", 0, KA)
    turn(v("tr2", 128, KA), v("b0", 128, KA))
    turn(v("tr2", 0, 128), v("b3", 0, 128))
    for j in range(6):
        sign(v("junk2", KA * j, KA * j + KA), v("b5", 0, KA), v("tr2", 32 * j, 32 * j + 1), v("ks2", j, j + 1))
        ts(v("cmp2", KA * j, KA * j + KA), v("b6", 0, KA), v("tr2", 32 * j + 16, 32 * j + 17), A.is_gt, BIG, A.mult)
        vsum(2, KA, j)
    scan(v("yy", 4 * KB), v("yy", 0, 2 * KB), v("yy", 2 * KB, 4 * KB), 0.0, A.add, A.max)
    ts(v("offx"), v("yy", 4 * KB + 1, 6 * KB, 2), v("pf", 1, 2), A.add)
    gather("S", v("l1"), v("ramp"), v("off1"))
    gate(v("gd2", 0, 5), v("ks2", 0, 5))
    act(v("junk2", 11 * KA, 11 * KA + 5), v("ks2", 0, 5), F.Sign, -0.5, 1.0, v("gk2"))
    act(v("ex2", 192, 208), v("zero", 0, 16), F.Identity, v("gk2"))
    tt(v("lb2", 0, 5), v("tr2", 0, 160, 32), v("gd2", 0, 5), A.min)
    tt(v("la2", 0, 10, 2), v("tr2", 0, 160, 32), v("gd2", 0, 5), A.max)
    tt(v("la2", 1, 12, 2), v("tr2", 16, KA, 32), v("so2", KB - 1, 6 * KB, KB), A.max)
    scan(v("ex2", 75, 96), v("lb2", 0, 21), v("lb2", 0, 21), -64 * BIG, A.max, A.max)
    scan(v("ex2", 139, 160), v("la2", 0, 42, 2), v("la2", 0, 42, 2), 64 * BIG, A.min, A.min)
    scan(v("ex2", 180, 159, -1), v("la2", 1, 43, 2), v("la2", 1, 43, 2), 64 * BIG, A.min, A.min)
    act(v("ex2", 224, 240), v("two", 0, 16), F.Sign, -1.0, v("ks2", 5, 6))
    turn(v("tex2", 0, 64), v("ex2", 192, 256))
    act(v("junk2", 11 * KA + 32, 11 * KA + 96), v("tex2", 0, 64), F.Identity, BIG / 128, BIG, v("red2", 64, 65))
    gate(v("gd2", 5, 6), v("ks2", 5, 6))
    ts(v("ex2", 256, 272), v("tr2", 160, 176), v("gd2", 5, 6), A.min)
    ts(v("ex2", 288, 304), v("tr2", 160, 176), v("gd2", 5, 6), A.max)
    turn(v("tex2", 64, 96), v("ex2", 80, 112))
    turn(v("tex2", 96, 160), v("ex2", 256, 320))
    turn(v("tex2", 160, 192), v("ex2", 144, 176))
    scan(v("red2", 0, 64), v("tex2", 64, 128), v("tex2", 128, 192), v("red2", 64, 65), A.max, A.min)
    running(2, KA, KB, v("red2", 63, 64), 0, 1, KA)

    H2 = W2 // 2
    S2 = (0, 1, 2, 3, 4)
    for m in range(8):
        a = PC * dest[m // 2] + 16 * (m % 2)
        b = min(a + W2, KA)
        if m < 4:
            a, b = PC * dest[m // 2], PC * dest[m // 2] + 120
        h = (b - a) // 2
        if m in S2:
            sign(v("cj1", 128 * m, 128 * m + b - a), v("pos2", 1 + a, 1 + b), v("thr2", m, m + 1), v("ck2", m, m + 1))
            if m in (1, 3):
                ts(v("off2", m - 1, m + 1), v("ck2", m - 1, m + 1), 0.5, A.mult, (a + b) / 2, A.add)
            elif m == 4:
                ts(v("off2", m, m + 1), v("ck2", m, m + 1), 0.5, A.mult, (a + b) / 2, A.add)
        else:
            ts(v("cc2", W2 * m, W2 * m + b - a), v("pos2", 1 + a, 1 + b), v("thr2", m, m + 1), A.is_le)
            scan(v("co2", H2 * m + H2 - h, H2 * m + H2), v("cc2", W2 * m, W2 * m + h),
                 v("cc2", W2 * m + h, W2 * m + 2 * h), float(a), A.add, A.add)
    copy(v("off2", 5, 8), v("co2", 6 * H2 - 1, 8 * H2, H2))

    def tcol(i):
        return 96 + 32 * i if i else 0

    for t, e in enumerate("SVSV"):
        gather(e, v("tg", t, 128, 4), v("hp", KA * t, KA * t + KA), v("off2", 0, 2))
    quant("a", 0, 128, v("tg", 0, 512))
    send(dest[0], "a", 0, "g", 128, True, "arr0", "left1")
    for t, e in enumerate("SVSV"):
        gather(e, v("tg", 512 + t, 896, 4), v("hp", KA * t, KA * t + KA), v("off2", 2, 8))
    quant("g", 0, 128, v("tg", 384, 896))
    send(dest[1], "g", 32, "x", C, True, "arr1", "left1")
    send(dest[2], "g", 64, "f", 128, False, "arr2", "left1")

    A1, A2 = 128, 208
    at4 = (0, 10, 16, 24)

    def place(e, a, b):
        gather(e, v("tx", 4 * a, 4 * b), v("win"), v("offx", a // 4, b // 4))

    gather("S", v("olr"), v("l1"), v("off2"))
    place("S", 0, A1)
    place("V", A2, A2 + 64)
    scan(v("old"), v("gate", 0, 128), v("olr"), 0.0, A.add, A.min)
    place("V", A2 + 64, C)
    ts(v("offs"), v("old", 3, 128, 4), 4.0, A.mult, v("pf", 3, 4), A.add)

    def through(banks, src, a, at, to, n, es):
        for b in range(4):
            mm(banks[b], "z", 128 * b, src, a, 128)
        for b in range(4):
            relu(es[b], v("tt", 4 * to + b, 4 * (to + 128 - at), 4), v("b%d" % banks[b], at, 128))
        quant(n, 0, 128, v("tt", 4 * to, 4 * to + 512))

    def unpack(banks, src, a):
        for b in range(4):
            mm(banks[b], "e", 128 * b, src, a, 128)

    def parts(i, n):
        gather("S", v("hs", 32 * at4[i] + 1, 32 * at4[i] + 2 * KB * n, 2), v("win", 0, 4 * C),
               v("offs", at4[i], at4[i] + 6 * n))

    def up(banks, at, i, bs=range(4)):
        for b in bs:
            tt(v("hs", 32 * at4[i] + 2 * b, 32 * at4[i] + 2 * KB, 8), v("b%d" % banks[b], at, at + PC),
               v("tg", 4 * tcol(i) + b, 4 * (tcol(i) + PC), 4), A.add)

    def up2(i):
        run = (32 * at4[i], 32 * at4[i] + 2 * KB)
        scan(v("nw", *run), v("alt", 0, KA), v("hs", *run), 0.0, A.mult, A.add)

    def put(i):
        scatter(v("tx"), v("offs", at4[i], at4[i] + 6), v("nw", 32 * at4[i] + 1, 32 * at4[i] + 2 * KB, 2))

    lo4, hi4 = (0, 1, 2, 3), (4, 5, 6, 7)
    parts(3, 1)
    emake(2)
    ts(v("offs", 10, 16), v("old", 35, 56, 4), 4.0, A.mult, v("pf", 3, 4), A.add)
    through(hi4, "g", PC, 72, 2 * PC, "t1", "SVSV")
    send(dest[0], "t1", 32, "h", KA, True, "arr3", "left2")
    emake(3)
    through(lo4, "x", C + PC - 128, 104, PC, "t2", "SSSV")
    send(dest[1], "t2", 0, "a", 128, True, "arr4", "left2")
    through(hi4, "f", PC, 104, 0, "t3", "SSSV")
    send(dest[2], "t3", 0, "f", 128 + PC, True, "arr5", "left2")
    for i in range(N):
        dma("Y", T.ol[:, PC * dest[i]:PC * dest[i] + PC], T.olr[0:128:16, 32 * i:32 * i + PC], [v("olr")], [], "left2")

    unpack(lo4, "t1", 0)
    place("S", A1, A2)
    parts(0, 1)
    parts(1, 2)
    up(lo4, 0, 3)
    quant("v", 0, 128, v("tv"))
    up2(3)
    put(3)
    unpack(hi4, "h", KA + PC - 128)
    up(hi4, 104, 0)
    up2(0)
    unpack(lo4, "a", PC)
    up(lo4, 104, 1, (0,))
    put(0)
    up(lo4, 104, 1, (1, 2, 3))
    unpack(hi4, "f", 2 * PC)
    up(hi4, 104, 2, (0,))
    up2(1)
    up(hi4, 104, 2, (1, 2, 3))
    put(1)
    up2(2)
    put(2)

    for j in range(3):
        quant("y", 128 * j, 128 * j + 128, v("tx", 512 * j, 512 * j + 512))
        mm(j, "v", 0, "y", 128 * j, 128)
    dma("Y", T.oc[:], codes("y", 0, C), [v("qy")], [])

    def scales(e, k):
        dma(e, T.osc[4 * k:4 * k + 4, :], T.sy[32 * k:32 * k + 4, :], [v("sy")], [])

    scales("Y", 0)
    scales("Y", 1)
    for j, e in enumerate("SSV"):
        copy(v("yb", 128 * j, 128 * j + 128), v("b%d" % j, 0, 128), e)
    dma("Y", T.y[:], ap(v("yb")), [v("yb")], [])
    scales("S", 2)
    scales("S", 3)

    for i in ORDER or range(len(todo)):
        todo[i][1]()
    for sem in sorted(SEMAPHORES, key=lambda x: x == last[0]):
        if seen.get(sem, 0) < count.get(sem, 0):
            g.wait_ge(T.sem[sem], count[sem])
